import numpy as np
import ml_dtypes


def mxq(x, axis, fmt="e4m3"):
    dtype, down = {"e4m3": (ml_dtypes.float8_e4m3fn, 7), "e5m2": (ml_dtypes.float8_e5m2, 14)}[fmt]
    v = np.moveaxis(np.asarray(x, np.float32).astype(ml_dtypes.bfloat16).astype(np.float64), axis, -1)
    blocks = v.reshape(v.shape[:-1] + (-1, 32))
    amax = np.abs(blocks).max(-1, keepdims=True)
    byte = np.maximum(np.where(amax > 0, np.frexp(amax)[1] - 1 + 127, 0) - down, 1)
    scale = np.exp2(byte - 127.0)
    codes = (blocks / scale).astype(np.float32).astype(dtype).astype(np.float64)
    return np.moveaxis((codes * scale).reshape(v.shape), -1, axis)


WIDE = False


def mx_kscale(k):
    if not WIDE:
        return np.ones(k)
    levels = np.array([10, -10, 5, -5, 0])
    if k % 512:
        return np.exp2(np.random.permutation(np.resize(levels, k // 32))).repeat(32)
    a = np.empty((k // 512, 16))
    for p in range(k // 512):
        a[p, :8] = np.random.permutation(np.resize(levels, 8))
        for g in range(8):
            far = levels[np.abs(levels - a[p, g]) >= 10]
            a[p, g + 8] = far[np.random.randint(len(far))]
    return np.exp2(a.ravel()).repeat(32)


def f64(x):
    return np.asarray(x).astype(np.float64)


def striped(idx):
    return np.tile(idx.reshape(-1, 16).T, (8, 1)).astype(np.uint16)


def unstriped(offs):
    return offs[:16].T.reshape(-1).astype(np.int64)


def pack_weight(w):
    k, n = w.shape
    w = f64(np.asarray(w, np.float32).astype(ml_dtypes.bfloat16)).reshape(k // 32, 32, n)
    amax = np.abs(w).max(1)
    byte = np.clip(np.where(amax > 0, np.frexp(amax)[1] - 1 + 127 - 7, 1), 1, 254)
    scaled = (w * np.exp2(127.0 - byte)[:, None, :]).reshape(k, n).astype(np.float32)
    words = np.ascontiguousarray(scaled.reshape(k // 512, 128, 4, n).transpose(0, 1, 3, 2)).astype(ml_dtypes.float8_e4m3fn).view(np.uint8)
    return words, np.ascontiguousarray(byte.astype(np.uint8).reshape(k // 512, 16, n))


def unpack_weight(words, scales):
    g, p, n, _ = words.shape
    vals = np.ascontiguousarray(words).view(ml_dtypes.float8_e4m3fn).astype(np.float64) * np.repeat(np.exp2(scales.astype(np.float64) - 127.0), 8, axis=1)[..., None]
    return vals.transpose(0, 1, 3, 2).reshape(g * 512, n)


K, T, S, V, H, N = 512, 2048, 512, 256, 512, 256


def setup_inputs():
    n = np.random.standard_normal
    s = mx_kscale(K)[:, None]
    u = mx_kscale(H)
    near = np.random.permutation(S)
    packed_xT = pack_weight(n((K, T)) * s)
    return {
        "x_words": packed_xT[0],
        "x_scales": packed_xT[1],
        "w1": (n((K, H)) / np.sqrt(K) / s).astype(np.float32),
        "w2": (n((K, H)) / np.sqrt(K) / s).astype(np.float32),
        "w3": (n((K, H)) / np.sqrt(K) / s * u).astype(np.float32),
        "w4": (n((H, N)) / np.sqrt(H) / u[:, None]).astype(np.float32),
        "offs": striped(np.random.permutation(T)[:S]),
        "cen": striped(np.random.permutation(S)[:V]),
        "pos1": striped(near[:V]),
        "pos2": striped(near[V:]),
    }


def reference(x_words, x_scales, w1, w2, w3, w4, offs, cen, pos1, pos2):
    xq = unpack_weight(x_words, x_scales)[:, unstriped(offs)]
    h = mxq(f64(w3), 0, "e4m3").T @ xq
    e = mxq(f64(w2), 0, "e4m3").T @ xq
    y = mxq(f64(w1), 0, "e4m3").T @ xq
    yc = y[:, unstriped(cen)]
    a0 = np.exp(np.tanh(e[:, unstriped(pos1)] * yc))
    a1 = np.exp(np.tanh(e[:, unstriped(pos2)] * yc))
    num = h[:, unstriped(pos1)] * a0 + h[:, unstriped(pos2)] * a1
    den = a0 + a1
    z = num / den
    return mxq(f64(w4), 0, "e4m3").T @ mxq(z, 0, "e4m3")

@@ -1,0 +1,215 @@
+from contextlib import ExitStack
+
+import concourse.mybir as mybir
+
+K, T, S, V, H, N = 512, 2048, 512, 256, 512, 256
+P = 128
+FLOPS = 2 * K * S * H * 3 + 2 * H * N * V
+
+F32 = mybir.dt.float32
+BF16 = mybir.dt.bfloat16
+I32 = mybir.dt.int32
+U32 = mybir.dt.uint32
+U16 = mybir.dt.uint16
+U8 = mybir.dt.uint8
+FP8X4 = mybir.dt.float8_e4m3fn_x4
+ALU = mybir.AluOpType
+ACT = mybir.ActivationFunctionType
+
+
+def tile_picked_zpt_mul_p_kernel(tc, x_words, x_scales, w1, w2, w3, w4, offs, cen, pos1, pos2, out):
+    nc = tc.nc
+    with ExitStack() as ctx:
+        sb = ctx.enter_context(tc.tile_pool(name="sb", bufs=1))
+        ps = ctx.enter_context(tc.psum_pool(name="ps", bufs=1))
+
+        def tile(shape, dtype, name):
+            return sb.tile(shape, dtype, name=name, align_bytes=64)
+
+        def load_list(src, name):
+            lst = sb.tile(list(src.shape), U16, name=name)
+            nc.sync.dma_start(lst[:], src)
+            return lst
+
+        def load_w(w, name, c0, c1):
+            raw = tile([P, 4, c1 - c0], F32, name)
+            nc.sync.dma_start(out=raw[:], in_=w.rearrange("(p j) c -> p j c", j=4)[:, :, c0:c1])
+            return raw
+
+        xs_all = tile([P, T], U8, "xs_all")
+        nc.vector.memset(xs_all[:].bitcast(I32), 0)
+        xs_rows = x_scales[0].rearrange("(q r) c -> r q c", r=4)
+        for r in range(4):
+            nc.scalar.dma_start(out=xs_all[r:P:32, :].bitcast(I32), in_=xs_rows[r].bitcast(I32))
+        warm = tile([P, 2], F32, "warm")
+        nc.vector.memset(warm[:, 0:1], 0.0)
+        nc.scalar.activation(warm[:, 1:2], warm[:, 0:1], ACT.Sigmoid)
+
+        offs_t = load_list(offs, "offs_t")
+        xw_all = tile([P, T], I32, "xw_all")
+        raw = {}
+
+        def load_x():
+            nc.sync.dma_start(out=xw_all[:], in_=x_words[0].rearrange("p n t -> p (n t)").bitcast(I32))
+
+        def load_halves(w, name):
+            for hf in range(2):
+                raw[name, hf] = load_w(w, name + "raw%d" % hf, 256 * hf, 256 * hf + 256)
+
+        load_x()
+        load_halves(w1, "w1")
+        load_halves(w2, "w2")
+        cen_t = load_list(cen, "cen_t")
+        pos1_t = load_list(pos1, "pos1_t")
+        pos2_t = load_list(pos2, "pos2_t")
+        load_halves(w3, "w3")
+        w4raw = load_w(w4, "w4raw", 0, N)
+
+        xw = tile([P, S], U32, "xw")
+        xs = tile([P, S], U8, "xs")
+        grouped = {n: tile([P, 4, P, 4], BF16, n + "g") for n in ("w1", "w2", "w3")}
+        codes = {n: tile([P, H], U32, n + "c") for n in ("w1", "w2", "w3")}
+        scales = {n: tile([P, H], U8, n + "s") for n in ("w1", "w2", "w3")}
+        res = {(n, t): tile([P, S], F32, n + "r%d" % t) for n in ("w1", "w2", "w3") for t in range(4)}
+        w4g = tile([P, N, 4], BF16, "w4g")
+        w4c = tile([P, N], U32, "w4c")
+        w4s = tile([P, N], U8, "w4s")
+        yc = [tile([P, V], F32, "yc%d" % t) for t in range(4)]
+        u = [tile([P, 2, V], F32, "u%d" % t) for t in range(4)]
+        th = [tile([P, 2, V], F32, "th%d" % t) for t in range(4)]
+        d = [tile([P, V], F32, "d%d" % t) for t in range(4)]
+        sg = [tile([P, 2, V], F32, "sg%d" % t) for t in range(4)]
+        pr = [tile([P, 4, V], F32, "pr%d" % k) for k in range(2)]
+        zg = tile([P, V, 4], BF16, "zg")
+        zc = tile([P, V], U32, "zc")
+        zs = tile([P, V], U8, "zs")
+        pos = [pos1_t, pos2_t]
+
+        def copy(eng, dst, src):
+            if eng == "v":
+                nc.vector.tensor_copy(out=dst, in_=src)
+            elif eng == "g":
+                nc.gpsimd.tensor_copy(out=dst, in_=src)
+            else:
+                nc.scalar.copy(out=dst, in_=src)
+
+        def weave(n, hf, eng, m0=0, m1=64):
+            dst = grouped[n][:, :, 64 * hf + m0 : 64 * hf + m1, :].rearrange("p t m j -> p m j t")
+            src = raw[n, hf][:, :, 4 * m0 : 4 * m1].rearrange("p j (m t) -> p m j t", t=4)
+            copy(eng, dst, src)
+
+        def weave4(eng, c0=0, c1=N):
+            dst = w4g[:, c0:c1, :].rearrange("p (c i) j -> p c j i", i=4)
+            src = w4raw[:, :, c0:c1].rearrange("p j (c i) -> p c j i", i=4)
+            copy(eng, dst, src)
+
+        def quant(n, t0, t1):
+            nc.vector.quantize_mx(out=codes[n][:, P * t0 : P * t1].bitcast(FP8X4), scales=scales[n][:, P * t0 : P * t1],
+                                  in_=grouped[n][:, t0:t1, :, :].rearrange("p t m j -> p (t m j)"))
+
+        def quant4():
+            nc.vector.quantize_mx(out=w4c[:].bitcast(FP8X4), scales=w4s[:], in_=w4g[:].rearrange("p c j -> p (c j)"))
+
+        def prod(n, t, eng="s"):
+            acc = ps.tile([P, S], F32, name="acc", tag="acc", bufs=6)
+            nc.tensor.matmul_mx(out=acc[:], lhsT=codes[n][:, P * t : P * t + P].bitcast(FP8X4), lhsT_scale=scales[n][:, P * t : P * t + P],
+                                rhs=xw[:].bitcast(FP8X4), rhs_scale=xs[:], start=True, stop=True)
+            copy(eng, res[n, t][:], acc[:])
+
+        def gx():
+            nc.vector.tensor_copy(out=xw[:], in_=xw_all[:].bitcast(U32).indirect(offs_t[:]))
+
+        def gs():
+            nc.vector.tensor_copy(out=xs[:], in_=xs_all[:].indirect(offs_t[:]))
+
+        def gy(t):
+            nc.vector.tensor_copy(out=yc[t][:], in_=res["w1", t][:].indirect(cen_t[:]))
+
+        def ge(t):
+            for k in range(2):
+                nc.vector.tensor_tensor(u[t][:, k, :], res["w2", t][:].indirect(pos[k][:]), yc[t][:], ALU.mult)
+
+        def tanh(t):
+            nc.scalar.activation(th[t][:], u[t][:], ACT.Tanh)
+
+        def diff(t):
+            nc.vector.tensor_tensor(d[t][:], th[t][:, 0, :], th[t][:, 1, :], ALU.subtract)
+
+        def sig(t):
+            nc.scalar.activation(sg[t][:, 0, :], d[t][:], ACT.Sigmoid)
+            nc.scalar.activation(sg[t][:, 1, :], d[t][:], ACT.Sigmoid, scale=-1.0)
+
+        def gh(t):
+            for k in range(2):
+                nc.vector.tensor_tensor(pr[k][:, t, :], res["w3", t][:].indirect(pos[k][:]), sg[t][:, k, :], ALU.mult)
+
+        def zsum(hf):
+            cols = slice(P * hf, P * hf + P)
+            nc.vector.tensor_tensor(zg[:, cols, :].rearrange("p (c i) t -> p c t i", i=4),
+                                    pr[0][:, :, cols].rearrange("p t (c i) -> p c t i", i=4),
+                                    pr[1][:, :, cols].rearrange("p t (c i) -> p c t i", i=4), ALU.add)
+
+        def zquant(hf):
+            cols = slice(P * hf, P * hf + P)
+            nc.vector.quantize_mx(out=zc[:, cols].bitcast(FP8X4), scales=zs[:, cols], in_=zg[:, cols, :].rearrange("p v t -> p (v t)"))
+
+        gs()
+        gx()
+        weave("w1", 0, "s")
+        weave("w1", 1, "v")
+        quant("w1", 0, 2)
+        quant("w1", 2, 4)
+        weave("w2", 0, "v")
+        for t in range(4):
+            prod("w1", t)
+        weave("w2", 1, "v")
+        quant("w2", 0, 2)
+        quant("w2", 2, 4)
+        for t in range(4):
+            prod("w2", t)
+            gy(t)
+        weave("w3", 0, "s")
+        weave("w3", 1, "s")
+        ge(0)
+        tanh(0)
+        ge(1)
+        tanh(1)
+        quant("w3", 0, 4)
+        diff(0)
+        sig(0)
+        prod("w3", 0)
+        ge(2)
+        tanh(2)
+        diff(1)
+        sig(1)
+        prod("w3", 1)
+        ge(3)
+        tanh(3)
+        diff(2)
+        sig(2)
+        prod("w3", 2)
+        gh(0)
+        diff(3)
+        sig(3)
+        prod("w3", 3)
+        weave4("s")
+        gh(1)
+        gh(2)
+        quant4()
+        gh(3)
+
+        for hf in range(2):
+            zsum(hf)
+        for hf in range(2):
+            zquant(hf)
+        banks = [ps.tile([P, V], F32, name="o%d" % mt) for mt in range(2)]
+        for hf in range(2):
+            cols = slice(P * hf, P * hf + P)
+            for mt in range(2):
+                rows = slice(P * mt, P * mt + P)
+                nc.tensor.matmul_mx(out=banks[mt][:, cols], lhsT=w4c[:, rows].bitcast(FP8X4), lhsT_scale=w4s[:, rows],
+                                    rhs=zc[:, cols].bitcast(FP8X4), rhs_scale=zs[:, cols], start=True, stop=True)
+        for mt in range(2):
+            o = tile([P, V], F32, "osb%d" % mt)
+            copy("sv"[mt], o[:], banks[mt][:])
+            (nc.scalar if mt == 0 else nc.sync).dma_start(out=out[P * mt : P * mt + P, :], in_=o[:])

@@ -1,6 +1,7 @@
 from contextlib import ExitStack
 
 import concourse.mybir as mybir
+from concourse.masks import make_identity
 
 K, T, S, V, H, N = 512, 2048, 512, 256, 512, 256
 P = 128
@@ -37,10 +38,6 @@ def tile_picked_zpt_mul_p_kernel(tc, x_words, x_scales, w1, w2, w3, w4, offs, ce
             return raw
 
         xs_all = tile([P, T], U8, "xs_all")
-        nc.vector.memset(xs_all[:].bitcast(I32), 0)
-        xs_rows = x_scales[0].rearrange("(q r) c -> r q c", r=4)
-        for r in range(4):
-            nc.scalar.dma_start(out=xs_all[r:P:32, :].bitcast(I32), in_=xs_rows[r].bitcast(I32))
         warm = tile([P, 2], F32, "warm")
         nc.vector.memset(warm[:, 0:1], 0.0)
         nc.scalar.activation(warm[:, 1:2], warm[:, 0:1], ACT.Sigmoid)
@@ -52,32 +49,42 @@ def tile_picked_zpt_mul_p_kernel(tc, x_words, x_scales, w1, w2, w3, w4, offs, ce
         def load_x():
             nc.sync.dma_start(out=xw_all[:], in_=x_words[0].rearrange("p n t -> p (n t)").bitcast(I32))
 
-        def load_halves(w, name):
-            for hf in range(2):
-                raw[name, hf] = load_w(w, name + "raw%d" % hf, 256 * hf, 256 * hf + 256)
+        def load_scales():
+            for q in range(4):
+                rows = x_scales[0, 4 * q : 4 * q + 4, :].bitcast(I32)
+                nc.sync.dma_start(out=xs_all[32 * q : 32 * q + 32, :].bitcast(I32), in_=rows.unsqueeze(0).broadcast_to([8, 4, T // 4]))
+
+        def load_pieces(w, name, cuts):
+            for c0, c1 in zip(cuts, cuts[1:]):
+                raw[name, c0] = load_w(w, name + "raw%d" % c0, c0, c1)
 
         load_x()
-        load_halves(w1, "w1")
-        load_halves(w2, "w2")
+        load_scales()
+        load_pieces(w1, "w1", [0, 256, 384, 512])
+        load_pieces(w2, "w2", [0, 256, 384, 512])
         cen_t = load_list(cen, "cen_t")
         pos1_t = load_list(pos1, "pos1_t")
         pos2_t = load_list(pos2, "pos2_t")
-        load_halves(w3, "w3")
+        load_pieces(w3, "w3", [0, 256, 512])
         w4raw = load_w(w4, "w4raw", 0, N)
 
+        ident = tile([P, P], F32, "ident")
+        make_identity(nc, ident[:])
         xw = tile([P, S], U32, "xw")
         xs = tile([P, S], U8, "xs")
-        grouped = {n: tile([P, 4, P, 4], BF16, n + "g") for n in ("w1", "w2", "w3")}
+        def staged(shape, dtype, name):
+            return sb.tile(shape, dtype, name=name, tag="stage", align_bytes=64)
+
+        grouped = {n: staged([P, 4, P, 4], BF16, n + "g") for n in ("w1", "w2", "w3")}
         codes = {n: tile([P, H], U32, n + "c") for n in ("w1", "w2", "w3")}
         scales = {n: tile([P, H], U8, n + "s") for n in ("w1", "w2", "w3")}
         res = {(n, t): tile([P, S], F32, n + "r%d" % t) for n in ("w1", "w2", "w3") for t in range(4)}
-        w4g = tile([P, N, 4], BF16, "w4g")
         w4c = tile([P, N], U32, "w4c")
         w4s = tile([P, N], U8, "w4s")
         yc = [tile([P, V], F32, "yc%d" % t) for t in range(4)]
-        u = [tile([P, 2, V], F32, "u%d" % t) for t in range(4)]
+        u = [tile([P, 2, V], F32, "u%d" % t) for t in range(3)] + [staged([P, 2, V], F32, "u3")]
+        w4g = staged([P, N, 4], BF16, "w4g")
         th = [tile([P, 2, V], F32, "th%d" % t) for t in range(4)]
-        d = [tile([P, V], F32, "d%d" % t) for t in range(4)]
         sg = [tile([P, 2, V], F32, "sg%d" % t) for t in range(4)]
         pr = [tile([P, 4, V], F32, "pr%d" % k) for k in range(2)]
         zg = tile([P, V, 4], BF16, "zg")
@@ -93,9 +100,10 @@ def tile_picked_zpt_mul_p_kernel(tc, x_words, x_scales, w1, w2, w3, w4, offs, ce
             else:
                 nc.scalar.copy(out=dst, in_=src)
 
-        def weave(n, hf, eng, m0=0, m1=64):
-            dst = grouped[n][:, :, 64 * hf + m0 : 64 * hf + m1, :].rearrange("p t m j -> p m j t")
-            src = raw[n, hf][:, :, 4 * m0 : 4 * m1].rearrange("p j (m t) -> p m j t", t=4)
+        def weave(n, c0, eng):
+            width = raw[n, c0].shape[2]
+            dst = grouped[n][:, :, c0 // 4 : (c0 + width) // 4, :].rearrange("p t m j -> p m j t")
+            src = raw[n, c0][:].rearrange("p j (m t) -> p m j t", t=4)
             copy(eng, dst, src)
 
         def weave4(eng, c0=0, c1=N):
@@ -111,7 +119,7 @@ def tile_picked_zpt_mul_p_kernel(tc, x_words, x_scales, w1, w2, w3, w4, offs, ce
             nc.vector.quantize_mx(out=w4c[:].bitcast(FP8X4), scales=w4s[:], in_=w4g[:].rearrange("p c j -> p (c j)"))
 
         def prod(n, t, eng="s"):
-            acc = ps.tile([P, S], F32, name="acc", tag="acc", bufs=6)
+            acc = ps.tile([P, S], F32, name="acc", tag="acc", bufs=4)
             nc.tensor.matmul_mx(out=acc[:], lhsT=codes[n][:, P * t : P * t + P].bitcast(FP8X4), lhsT_scale=scales[n][:, P * t : P * t + P],
                                 rhs=xw[:].bitcast(FP8X4), rhs_scale=xs[:], start=True, stop=True)
             copy(eng, res[n, t][:], acc[:])
@@ -129,15 +137,30 @@ def tile_picked_zpt_mul_p_kernel(tc, x_words, x_scales, w1, w2, w3, w4, offs, ce
             for k in range(2):
                 nc.vector.tensor_tensor(u[t][:, k, :], res["w2", t][:].indirect(pos[k][:]), yc[t][:], ALU.mult)
 
+        flipped = {}
+        dsum = {}
+
+        def flip(t):
+            flipped[t] = ps.tile([P, 2, V], F32, name="ut", tag="ut", bufs=2)
+            for k in range(2):
+                for hf in range(2):
+                    cols = slice(P * hf, P * hf + P)
+                    nc.tensor.transpose(flipped[t][:, k, cols], u[t][:, k, cols], ident[:])
+
         def tanh(t):
-            nc.scalar.activation(th[t][:], u[t][:], ACT.Tanh)
+            for k in range(2):
+                nc.scalar.activation(th[t][:, k, :], flipped[t][:, k, :], ACT.Tanh, scale=1.0 - 2.0 * k)
 
         def diff(t):
-            nc.vector.tensor_tensor(d[t][:], th[t][:, 0, :], th[t][:, 1, :], ALU.subtract)
+            dsum[t] = ps.tile([P, V], F32, name="ds", tag="ds", bufs=2)
+            for hf in range(2):
+                cols = slice(P * hf, P * hf + P)
+                for k in range(2):
+                    nc.tensor.matmul(dsum[t][:, cols], th[t][:, k, cols], ident[:], start=(k == 0), stop=(k == 1), is_transpose=True)
 
         def sig(t):
-            nc.scalar.activation(sg[t][:, 0, :], d[t][:], ACT.Sigmoid)
-            nc.scalar.activation(sg[t][:, 1, :], d[t][:], ACT.Sigmoid, scale=-1.0)
+            for k in range(2):
+                nc.scalar.activation(sg[t][:, k, :], dsum[t][:], ACT.Sigmoid, scale=1.0 - 2.0 * k)
 
         def gh(t):
             for k in range(2):
@@ -153,63 +176,73 @@ def tile_picked_zpt_mul_p_kernel(tc, x_words, x_scales, w1, w2, w3, w4, offs, ce
             cols = slice(P * hf, P * hf + P)
             nc.vector.quantize_mx(out=zc[:, cols].bitcast(FP8X4), scales=zs[:, cols], in_=zg[:, cols, :].rearrange("p v t -> p (v t)"))
 
-        gs()
         gx()
+        gs()
         weave("w1", 0, "s")
-        weave("w1", 1, "v")
-        quant("w1", 0, 2)
+        weave("w1", 256, "v")
+        weave("w1", 384, "v")
+        quant("w1", 0, 1)
+        quant("w1", 1, 2)
         quant("w1", 2, 4)
-        weave("w2", 0, "v")
         for t in range(4):
             prod("w1", t)
-        weave("w2", 1, "v")
+        weave("w2", 0, "v")
+        weave("w2", 256, "v")
+        weave("w2", 384, "v")
+        gy(0)
         quant("w2", 0, 2)
         quant("w2", 2, 4)
         for t in range(4):
             prod("w2", t)
+        for t in range(1, 4):
             gy(t)
         weave("w3", 0, "s")
-        weave("w3", 1, "s")
+        weave("w3", 256, "s")
         ge(0)
+        flip(0)
         tanh(0)
-        ge(1)
-        tanh(1)
-        quant("w3", 0, 4)
         diff(0)
+        ge(1)
+        flip(1)
+        ge(2)
+        quant("w3", 0, 2)
+        quant("w3", 2, 4)
+        tanh(1)
         sig(0)
         prod("w3", 0)
-        ge(2)
-        tanh(2)
         diff(1)
+        flip(2)
+        ge(3)
+        gh(0)
         sig(1)
         prod("w3", 1)
-        ge(3)
-        tanh(3)
+        tanh(2)
+        flip(3)
         diff(2)
-        sig(2)
-        prod("w3", 2)
-        gh(0)
-        diff(3)
-        sig(3)
-        prod("w3", 3)
-        weave4("s")
         gh(1)
+        prod("w3", 2)
+        sig(2)
+        tanh(3)
+        diff(3)
         gh(2)
-        quant4()
+        prod("w3", 3)
+        sig(3)
+        weave4("s")
         gh(3)
+        quant4()
 
         for hf in range(2):
             zsum(hf)
         for hf in range(2):
             zquant(hf)
-        banks = [ps.tile([P, V], F32, name="o%d" % mt) for mt in range(2)]
         for hf in range(2):
             cols = slice(P * hf, P * hf + P)
             for mt in range(2):
                 rows = slice(P * mt, P * mt + P)
-                nc.tensor.matmul_mx(out=banks[mt][:, cols], lhsT=w4c[:, rows].bitcast(FP8X4), lhsT_scale=w4s[:, rows],
+                bank = ps.tile([P, P], F32, name="o", tag="acc", bufs=4)
+                nc.tensor.matmul_mx(out=bank[:], lhsT=w4c[:, rows].bitcast(FP8X4), lhsT_scale=w4s[:, rows],
                                     rhs=zc[:, cols].bitcast(FP8X4), rhs_scale=zs[:, cols], start=True, stop=True)
-        for mt in range(2):
-            o = tile([P, V], F32, "osb%d" % mt)
-            copy("sv"[mt], o[:], banks[mt][:])
-            (nc.scalar if mt == 0 else nc.sync).dma_start(out=out[P * mt : P * mt + P, :], in_=o[:])
+                o = tile([P, P], F32, "osb%d%d" % (hf, mt))
+                last = hf == 1 and mt == 1
+                copy("v" if last else "s", o[:], bank[:])
+                (nc.scalar if hf == 1 and mt == 0 else nc.sync).dma_start(out=out[rows, cols], in_=o[:])

@@ -5,7 +5,11 @@ from concourse.masks import make_identity
 
 K, T, S, V, H, N = 512, 2048, 512, 256, 512, 256
 P = 128
+PACK = 4
+OCT = 8
 FLOPS = 2 * K * S * H * 3 + 2 * H * N * V
+
+PIECES = (0, 256, 384, 512)
 
 F32 = mybir.dt.float32
 BF16 = mybir.dt.bfloat16
@@ -24,225 +28,206 @@ def tile_picked_zpt_mul_p_kernel(tc, x_words, x_scales, w1, w2, w3, w4, offs, ce
         sb = ctx.enter_context(tc.tile_pool(name="sb", bufs=1))
         ps = ctx.enter_context(tc.psum_pool(name="ps", bufs=1))
 
-        def tile(shape, dtype, name):
-            return sb.tile(shape, dtype, name=name, align_bytes=64)
+        def tile(shape, dtype, name, tag=None):
+            return sb.tile(shape, dtype, name=name, tag=tag or name, align_bytes=64)
+
+        def bank(shape, name, number):
+            return ps.tile(shape, F32, name=name, tag="bank%d" % number)
 
         def load_list(src, name):
             lst = sb.tile(list(src.shape), U16, name=name)
             nc.sync.dma_start(lst[:], src)
             return lst
 
-        def load_w(w, name, c0, c1):
-            raw = tile([P, 4, c1 - c0], F32, name)
-            nc.sync.dma_start(out=raw[:], in_=w.rearrange("(p j) c -> p j c", j=4)[:, :, c0:c1])
-            return raw
+        scale_table = tile([P, T], U8, "scale_table")
+        nc.vector.memset(scale_table[:].bitcast(I32), 0)
 
-        xs_all = tile([P, T], U8, "xs_all")
-        warm = tile([P, 2], F32, "warm")
+        warm = tile([P, 2], F32, "warm", tag="weights")
         nc.vector.memset(warm[:, 0:1], 0.0)
         nc.scalar.activation(warm[:, 1:2], warm[:, 0:1], ACT.Sigmoid)
+        weights = tile([P, PACK * (3 * H + N)], F32, "weights")
 
-        offs_t = load_list(offs, "offs_t")
-        xw_all = tile([P, T], I32, "xw_all")
+        offs_list = load_list(offs, "offs_list")
+        word_table = tile([P, T], I32, "word_table")
+        cen_list = load_list(cen, "cen_list")
+        pos_lists = [load_list(pos1, "pos1_list"), load_list(pos2, "pos2_list")]
+        nc.sync.dma_start(out=word_table[:], in_=x_words[0].rearrange("p n j -> p (n j)").bitcast(I32))
+        scale_rows = x_scales[0].rearrange("(q r) c -> r q c", r=4)
+        for r in range(4):
+            nc.scalar.dma_start(out=scale_table[r:P:32, :].bitcast(I32), in_=scale_rows[r].bitcast(I32))
+
         raw = {}
-
-        def load_x():
-            nc.sync.dma_start(out=xw_all[:], in_=x_words[0].rearrange("p n t -> p (n t)").bitcast(I32))
-
-        def load_scales():
-            for q in range(4):
-                rows = x_scales[0, 4 * q : 4 * q + 4, :].bitcast(I32)
-                nc.sync.dma_start(out=xs_all[32 * q : 32 * q + 32, :].bitcast(I32), in_=rows.unsqueeze(0).broadcast_to([8, 4, T // 4]))
-
-        def load_pieces(w, name, cuts):
+        for place, (name, w, cuts) in enumerate((("y", w1, PIECES), ("e", w2, PIECES), ("h", w3, (0, H)))):
             for c0, c1 in zip(cuts, cuts[1:]):
-                raw[name, c0] = load_w(w, name + "raw%d" % c0, c0, c1)
-
-        load_x()
-        load_scales()
-        load_pieces(w1, "w1", [0, 256, 384, 512])
-        load_pieces(w2, "w2", [0, 256, 384, 512])
-        cen_t = load_list(cen, "cen_t")
-        pos1_t = load_list(pos1, "pos1_t")
-        pos2_t = load_list(pos2, "pos2_t")
-        load_pieces(w3, "w3", [0, 256, 512])
-        w4raw = load_w(w4, "w4raw", 0, N)
+                start = PACK * H * place
+                raw[name, c0] = weights[:, start + PACK * c0 : start + PACK * c1].rearrange("p (j c) -> p j c", j=PACK)
+                nc.sync.dma_start(out=raw[name, c0], in_=w.rearrange("(p j) c -> p j c", j=PACK)[:, :, c0:c1])
+        w4_raw = weights[:, 3 * PACK * H :].rearrange("p (t m) -> p t m", t=PACK)
+        w4_rows = w4.rearrange("(b t r) m -> t b r m", t=PACK, r=OCT)
+        for t in range(PACK):
+            nc.sync.dma_start(out=w4_raw[:, t, :], in_=w4_rows[t])
 
         ident = tile([P, P], F32, "ident")
         make_identity(nc, ident[:])
-        xw = tile([P, S], U32, "xw")
-        xs = tile([P, S], U8, "xs")
-        def staged(shape, dtype, name):
-            return sb.tile(shape, dtype, name=name, tag="stage", align_bytes=64)
 
-        grouped = {n: staged([P, 4, P, 4], BF16, n + "g") for n in ("w1", "w2", "w3")}
-        codes = {n: tile([P, H], U32, n + "c") for n in ("w1", "w2", "w3")}
-        scales = {n: tile([P, H], U8, n + "s") for n in ("w1", "w2", "w3")}
-        res = {(n, t): tile([P, S], F32, n + "r%d" % t) for n in ("w1", "w2", "w3") for t in range(4)}
-        w4c = tile([P, N], U32, "w4c")
-        w4s = tile([P, N], U8, "w4s")
-        yc = [tile([P, V], F32, "yc%d" % t) for t in range(4)]
-        u = [tile([P, 2, V], F32, "u%d" % t) for t in range(3)] + [staged([P, 2, V], F32, "u3")]
-        w4g = staged([P, N, 4], BF16, "w4g")
-        th = [tile([P, 2, V], F32, "th%d" % t) for t in range(4)]
-        sg = [tile([P, 2, V], F32, "sg%d" % t) for t in range(4)]
-        pr = [tile([P, 4, V], F32, "pr%d" % k) for k in range(2)]
-        zg = tile([P, V, 4], BF16, "zg")
-        zc = tile([P, V], U32, "zc")
-        zs = tile([P, V], U8, "zs")
-        pos = [pos1_t, pos2_t]
+        x_codes = tile([P, S], U32, "x_codes")
+        x_bytes = tile([P, S], U8, "x_bytes")
+        woven = {name: tile([P, PACK, P, PACK], BF16, name + "_woven", tag="early") for name in "ye"}
+        w_scales = {name: tile([P, H], U8, name + "_scales") for name in "yeh"}
+        rows = {(name, t): tile([P, S], F32, name + "_rows%d" % t) for name in "yeh" for t in range(PACK) if (name, t) != ("y", PACK - 1)}
+        rows["y", PACK - 1] = tile([P, S], F32, "y_rows_last", tag="late")
+        woven["h"] = tile([P, PACK, P, PACK], BF16, "h_woven", tag="late")
+        w4_codes = tile([P, N], U32, "w4_codes")
+        w4_scales = tile([P, N], U8, "w4_scales")
+        query_first = tile([P, V], F32, "query_first")
+        query_rest = tile([P, PACK - 1, V], F32, "query_rest", tag="early")
+        query = [query_first[:]] + [query_rest[:, t, :] for t in range(PACK - 1)]
+        w_codes = {(name, pair): tile([P, 2 * P], U32, name + "_codes%d" % pair) for name in "yeh" for pair in range(2)}
+        prod = [tile([P, 2, V], F32, "prod%d" % t) for t in range(PACK - 1)] + [tile([P, 2, V], F32, "prod_last", tag="late")]
+        w4_woven = tile([P, N, PACK], BF16, "w4_woven", tag="late")
+        tanhs = [tile([P, 2, V], F32, "tanhs%d" % t) for t in range(PACK)]
+        gates = [tile([P, 2, V], F32, "gates%d" % t) for t in range(PACK)]
+        parts = [tile([P, PACK, V], F32, "parts%d" % side) for side in range(2)]
+        z_woven = tile([P, V, PACK], BF16, "z_woven")
+        z_codes = tile([P, V], U32, "z_codes")
+        z_scales = tile([P, V], U8, "z_scales")
+        halves = [slice(0, P), slice(P, 2 * P)]
+        signs = [1.0, -1.0]
+        sums, turned, diffs = {}, {}, {}
 
-        def copy(eng, dst, src):
-            if eng == "v":
-                nc.vector.tensor_copy(out=dst, in_=src)
-            elif eng == "g":
-                nc.gpsimd.tensor_copy(out=dst, in_=src)
-            else:
-                nc.scalar.copy(out=dst, in_=src)
+        def weave_piece(name, c0, copy):
+            piece = raw[name, c0]
+            places = slice(c0 // PACK, (c0 + piece.shape[2]) // PACK)
+            copy(out=woven[name][:, :, places, :].rearrange("p t (b r) j -> p t b r j", r=OCT),
+                 in_=piece.rearrange("p j (b t r) -> p t b r j", t=PACK, r=OCT))
 
-        def weave(n, c0, eng):
-            width = raw[n, c0].shape[2]
-            dst = grouped[n][:, :, c0 // 4 : (c0 + width) // 4, :].rearrange("p t m j -> p m j t")
-            src = raw[n, c0][:].rearrange("p j (m t) -> p m j t", t=4)
-            copy(eng, dst, src)
+        def weave_h(t):
+            nc.scalar.copy(out=woven["h"][:, t, :, :].rearrange("p (b a r) j -> p b a j r", a=2, r=4),
+                           in_=raw["h", 0].rearrange("p j (b t a r) -> p t b a j r", t=PACK, a=2, r=4)[:, t])
 
-        def weave4(eng, c0=0, c1=N):
-            dst = w4g[:, c0:c1, :].rearrange("p (c i) j -> p c j i", i=4)
-            src = w4raw[:, :, c0:c1].rearrange("p j (c i) -> p c j i", i=4)
-            copy(eng, dst, src)
+        def quantise(name, t0, t1):
+            first = P * (t0 % 2)
+            nc.vector.quantize_mx(out=w_codes[name, t0 // 2][:, first : first + P * (t1 - t0)].bitcast(FP8X4),
+                                  scales=w_scales[name][:, P * t0 : P * t1],
+                                  in_=woven[name][:, t0:t1, :, :].rearrange("p t m j -> p (t m j)"))
 
-        def quant(n, t0, t1):
-            nc.vector.quantize_mx(out=codes[n][:, P * t0 : P * t1].bitcast(FP8X4), scales=scales[n][:, P * t0 : P * t1],
-                                  in_=grouped[n][:, t0:t1, :, :].rearrange("p t m j -> p (t m j)"))
+        def multiply(name, t):
+            sums[name, t] = bank([P, S], "sums", t + 4 if name == "h" else t)
+            nc.tensor.matmul_mx(out=sums[name, t][:], lhsT=w_codes[name, t // 2][:, halves[t % 2]].bitcast(FP8X4),
+                                lhsT_scale=w_scales[name][:, P * t : P * t + P],
+                                rhs=x_codes[:].bitcast(FP8X4), rhs_scale=x_bytes[:], start=True, stop=True)
 
-        def quant4():
-            nc.vector.quantize_mx(out=w4c[:].bitcast(FP8X4), scales=w4s[:], in_=w4g[:].rearrange("p c j -> p (c j)"))
+        def empty(name, t):
+            nc.scalar.copy(out=rows[name, t][:], in_=sums[name, t][:])
 
-        def prod(n, t, eng="s"):
-            acc = ps.tile([P, S], F32, name="acc", tag="acc", bufs=4)
-            nc.tensor.matmul_mx(out=acc[:], lhsT=codes[n][:, P * t : P * t + P].bitcast(FP8X4), lhsT_scale=scales[n][:, P * t : P * t + P],
-                                rhs=xw[:].bitcast(FP8X4), rhs_scale=xs[:], start=True, stop=True)
-            copy(eng, res[n, t][:], acc[:])
+        def gather_query(t):
+            nc.vector.tensor_copy(out=query[t], in_=rows["y", t][:].indirect(cen_list[:]))
 
-        def gx():
-            nc.vector.tensor_copy(out=xw[:], in_=xw_all[:].bitcast(U32).indirect(offs_t[:]))
+        def gather_keys(t):
+            for side in range(2):
+                nc.vector.tensor_tensor(prod[t][:, side, :], rows["e", t][:].indirect(pos_lists[side][:]), query[t], ALU.mult)
 
-        def gs():
-            nc.vector.tensor_copy(out=xs[:], in_=xs_all[:].indirect(offs_t[:]))
-
-        def gy(t):
-            nc.vector.tensor_copy(out=yc[t][:], in_=res["w1", t][:].indirect(cen_t[:]))
-
-        def ge(t):
-            for k in range(2):
-                nc.vector.tensor_tensor(u[t][:, k, :], res["w2", t][:].indirect(pos[k][:]), yc[t][:], ALU.mult)
-
-        flipped = {}
-        dsum = {}
-
-        def flip(t):
-            flipped[t] = ps.tile([P, 2, V], F32, name="ut", tag="ut", bufs=2)
-            for k in range(2):
-                for hf in range(2):
-                    cols = slice(P * hf, P * hf + P)
-                    nc.tensor.transpose(flipped[t][:, k, cols], u[t][:, k, cols], ident[:])
+        def turn(t):
+            turned[t] = bank([P, 2, V], "turned", 4 + t % 2)
+            for side in range(2):
+                for cols in halves:
+                    nc.tensor.transpose(turned[t][:, side, cols], prod[t][:, side, cols], ident[:])
 
         def tanh(t):
-            for k in range(2):
-                nc.scalar.activation(th[t][:, k, :], flipped[t][:, k, :], ACT.Tanh, scale=1.0 - 2.0 * k)
+            for side in range(2):
+                nc.scalar.activation(tanhs[t][:, side, :], turned[t][:, side, :], ACT.Tanh, scale=signs[side])
 
-        def diff(t):
-            dsum[t] = ps.tile([P, V], F32, name="ds", tag="ds", bufs=2)
-            for hf in range(2):
-                cols = slice(P * hf, P * hf + P)
-                for k in range(2):
-                    nc.tensor.matmul(dsum[t][:, cols], th[t][:, k, cols], ident[:], start=(k == 0), stop=(k == 1), is_transpose=True)
+        def difference(t):
+            diffs[t] = bank([P, V], "diffs", t + 6 if t < 2 else t)
+            for cols in halves:
+                for side in range(2):
+                    nc.tensor.matmul(diffs[t][:, cols], tanhs[t][:, side, cols], ident[:], start=(side == 0), stop=(side == 1), is_transpose=True)
 
-        def sig(t):
-            for k in range(2):
-                nc.scalar.activation(sg[t][:, k, :], dsum[t][:], ACT.Sigmoid, scale=1.0 - 2.0 * k)
+        def sigmoid(t):
+            for side in range(2):
+                nc.scalar.activation(gates[t][:, side, :], diffs[t][:], ACT.Sigmoid, scale=signs[side])
 
-        def gh(t):
-            for k in range(2):
-                nc.vector.tensor_tensor(pr[k][:, t, :], res["w3", t][:].indirect(pos[k][:]), sg[t][:, k, :], ALU.mult)
+        def gather_values(t):
+            for side in range(2):
+                nc.vector.tensor_tensor(parts[side][:, t, :], rows["h", t][:].indirect(pos_lists[side][:]), gates[t][:, side, :], ALU.mult)
 
-        def zsum(hf):
-            cols = slice(P * hf, P * hf + P)
-            nc.vector.tensor_tensor(zg[:, cols, :].rearrange("p (c i) t -> p c t i", i=4),
-                                    pr[0][:, :, cols].rearrange("p t (c i) -> p c t i", i=4),
-                                    pr[1][:, :, cols].rearrange("p t (c i) -> p c t i", i=4), ALU.add)
+        nc.vector.tensor_copy(out=x_bytes[:], in_=scale_table[:].indirect(offs_list[:]))
+        nc.vector.tensor_copy(out=x_codes[:], in_=word_table[:].bitcast(U32).indirect(offs_list[:]))
+        weave_piece("y", PIECES[0], nc.scalar.copy)
+        for c0 in PIECES[1:-1]:
+            weave_piece("y", c0, nc.vector.tensor_copy)
+        for t0, t1 in ((0, 1), (1, 2), (2, 4)):
+            quantise("y", t0, t1)
+        for t in range(PACK):
+            multiply("y", t)
+            empty("y", t)
 
-        def zquant(hf):
-            cols = slice(P * hf, P * hf + P)
-            nc.vector.quantize_mx(out=zc[:, cols].bitcast(FP8X4), scales=zs[:, cols], in_=zg[:, cols, :].rearrange("p v t -> p (v t)"))
+        for c0 in PIECES[:-1]:
+            weave_piece("e", c0, nc.vector.tensor_copy)
+        gather_query(0)
+        quantise("e", 0, 2)
+        quantise("e", 2, 4)
+        for t in range(PACK):
+            multiply("e", t)
+            empty("e", t)
+        for t in range(1, PACK):
+            gather_query(t)
 
-        gx()
-        gs()
-        weave("w1", 0, "s")
-        weave("w1", 256, "v")
-        weave("w1", 384, "v")
-        quant("w1", 0, 1)
-        quant("w1", 1, 2)
-        quant("w1", 2, 4)
-        for t in range(4):
-            prod("w1", t)
-        weave("w2", 0, "v")
-        weave("w2", 256, "v")
-        weave("w2", 384, "v")
-        gy(0)
-        quant("w2", 0, 2)
-        quant("w2", 2, 4)
-        for t in range(4):
-            prod("w2", t)
-        for t in range(1, 4):
-            gy(t)
-        weave("w3", 0, "s")
-        weave("w3", 256, "s")
-        ge(0)
-        flip(0)
+        for t in range(PACK):
+            weave_h(t)
+        gather_keys(0)
+        turn(0)
         tanh(0)
-        diff(0)
-        ge(1)
-        flip(1)
-        ge(2)
-        quant("w3", 0, 2)
-        quant("w3", 2, 4)
+        difference(0)
+        gather_keys(1)
+        turn(1)
+        gather_keys(2)
+        quantise("h", 0, 2)
+        quantise("h", 2, 4)
+        multiply("h", 0)
         tanh(1)
-        sig(0)
-        prod("w3", 0)
-        diff(1)
-        flip(2)
-        ge(3)
-        gh(0)
-        sig(1)
-        prod("w3", 1)
+        sigmoid(0)
+        empty("h", 0)
+        difference(1)
+        multiply("h", 1)
+        gather_keys(3)
+        turn(2)
+        gather_values(0)
+        sigmoid(1)
+        empty("h", 1)
+        multiply("h", 2)
+        turn(3)
         tanh(2)
-        flip(3)
-        diff(2)
-        gh(1)
-        prod("w3", 2)
-        sig(2)
+        difference(2)
+        gather_values(1)
+        multiply("h", 3)
         tanh(3)
-        diff(3)
-        gh(2)
-        prod("w3", 3)
-        sig(3)
-        weave4("s")
-        gh(3)
-        quant4()
+        difference(3)
+        empty("h", 2)
+        sigmoid(2)
+        gather_values(2)
+        empty("h", 3)
+        sigmoid(3)
+        nc.scalar.copy(out=w4_woven[:].rearrange("p (c i) t -> p c t i", i=4), in_=w4_raw.rearrange("p t (c i) -> p c t i", i=4))
+        gather_values(3)
+        nc.vector.quantize_mx(out=w4_codes[:].bitcast(FP8X4), scales=w4_scales[:], in_=w4_woven[:].rearrange("p m t -> p (m t)"))
 
-        for hf in range(2):
-            zsum(hf)
-        for hf in range(2):
-            zquant(hf)
-        for hf in range(2):
-            cols = slice(P * hf, P * hf + P)
-            for mt in range(2):
-                rows = slice(P * mt, P * mt + P)
-                bank = ps.tile([P, P], F32, name="o", tag="acc", bufs=4)
-                nc.tensor.matmul_mx(out=bank[:], lhsT=w4c[:, rows].bitcast(FP8X4), lhsT_scale=w4s[:, rows],
-                                    rhs=zc[:, cols].bitcast(FP8X4), rhs_scale=zs[:, cols], start=True, stop=True)
-                o = tile([P, P], F32, "osb%d%d" % (hf, mt))
-                last = hf == 1 and mt == 1
-                copy("v" if last else "s", o[:], bank[:])
-                (nc.scalar if hf == 1 and mt == 0 else nc.sync).dma_start(out=out[rows, cols], in_=o[:])
+        for cols in halves:
+            nc.vector.tensor_tensor(z_woven[:, cols, :].rearrange("p (c i) t -> p c t i", i=4),
+                                    parts[0][:, :, cols].rearrange("p t (c i) -> p c t i", i=4),
+                                    parts[1][:, :, cols].rearrange("p t (c i) -> p c t i", i=4), ALU.add)
+        for cols in halves:
+            nc.vector.quantize_mx(out=z_codes[:, cols].bitcast(FP8X4), scales=z_scales[:, cols],
+                                  in_=z_woven[:, cols, :].rearrange("p v t -> p (v t)"))
+        for half, cols in enumerate(halves):
+            for block, out_rows in enumerate(halves):
+                result = bank([P, P], "result", 2 * half + block)
+                nc.tensor.matmul_mx(out=result[:], lhsT=w4_codes[:, out_rows].bitcast(FP8X4), lhsT_scale=w4_scales[:, out_rows],
+                                    rhs=z_codes[:, cols].bitcast(FP8X4), rhs_scale=z_scales[:, cols], start=True, stop=True)
+                staged = tile([P, P], F32, "staged%d%d" % (half, block))
+                if (half, block) == (1, 1):
+                    nc.vector.tensor_copy(out=staged[:], in_=result[:])
+                else:
+                    nc.scalar.copy(out=staged[:], in_=result[:])
+                queue = nc.scalar if (half, block) == (1, 0) else nc.sync
+                queue.dma_start(out=out[out_rows, cols], in_=staged[:])

@@ -1,7 +1,6 @@
 from contextlib import ExitStack
 
 import concourse.mybir as mybir
-from concourse.masks import make_identity
 
 K, T, S, V, H, N = 512, 2048, 512, 256, 512, 256
 P = 128
@@ -67,9 +66,6 @@ def tile_picked_zpt_mul_p_kernel(tc, x_words, x_scales, w1, w2, w3, w4, offs, ce
         for t in range(PACK):
             nc.sync.dma_start(out=w4_raw[:, t, :], in_=w4_rows[t])
 
-        ident = tile([P, P], F32, "ident")
-        make_identity(nc, ident[:])
-
         x_codes = tile([P, S], U32, "x_codes")
         x_bytes = tile([P, S], U8, "x_bytes")
         woven = {name: tile([P, PACK, P, PACK], BF16, name + "_woven", tag="early") for name in "ye"}
@@ -86,6 +82,7 @@ def tile_picked_zpt_mul_p_kernel(tc, x_words, x_scales, w1, w2, w3, w4, offs, ce
         prod = [tile([P, 2, V], F32, "prod%d" % t) for t in range(PACK - 1)] + [tile([P, 2, V], F32, "prod_last", tag="late")]
         w4_woven = tile([P, N, PACK], BF16, "w4_woven", tag="late")
         tanhs = [tile([P, 2, V], F32, "tanhs%d" % t) for t in range(PACK)]
+        diffs = [tile([P, V], F32, "diffs%d" % t) for t in range(PACK)]
         gates = [tile([P, 2, V], F32, "gates%d" % t) for t in range(PACK)]
         parts = [tile([P, PACK, V], F32, "parts%d" % side) for side in range(2)]
         z_woven = tile([P, V, PACK], BF16, "z_woven")
@@ -93,7 +90,7 @@ def tile_picked_zpt_mul_p_kernel(tc, x_words, x_scales, w1, w2, w3, w4, offs, ce
         z_scales = tile([P, V], U8, "z_scales")
         halves = [slice(0, P), slice(P, 2 * P)]
         signs = [1.0, -1.0]
-        sums, turned, diffs = {}, {}, {}
+        sums = {}
 
         def weave_piece(name, c0, copy):
             piece = raw[name, c0]
@@ -112,7 +109,7 @@ def tile_picked_zpt_mul_p_kernel(tc, x_words, x_scales, w1, w2, w3, w4, offs, ce
                                   in_=woven[name][:, t0:t1, :, :].rearrange("p t m j -> p (t m j)"))
 
         def multiply(name, t):
-            sums[name, t] = bank([P, S], "sums", t + 4 if name == "h" else t)
+            sums[name, t] = bank([P, S], "sums", t + PACK if name == "e" else t)
             nc.tensor.matmul_mx(out=sums[name, t][:], lhsT=w_codes[name, t // 2][:, halves[t % 2]].bitcast(FP8X4),
                                 lhsT_scale=w_scales[name][:, P * t : P * t + P],
                                 rhs=x_codes[:].bitcast(FP8X4), rhs_scale=x_bytes[:], start=True, stop=True)
@@ -127,21 +124,11 @@ def tile_picked_zpt_mul_p_kernel(tc, x_words, x_scales, w1, w2, w3, w4, offs, ce
             for side in range(2):
                 nc.vector.tensor_tensor(prod[t][:, side, :], rows["e", t][:].indirect(pos_lists[side][:]), query[t], ALU.mult)
 
-        def turn(t):
-            turned[t] = bank([P, 2, V], "turned", 4 + t % 2)
-            for side in range(2):
-                for cols in halves:
-                    nc.tensor.transpose(turned[t][:, side, cols], prod[t][:, side, cols], ident[:])
-
         def tanh(t):
-            for side in range(2):
-                nc.scalar.activation(tanhs[t][:, side, :], turned[t][:, side, :], ACT.Tanh, scale=signs[side])
+            nc.scalar.activation(tanhs[t][:], prod[t][:], ACT.Tanh)
 
         def difference(t):
-            diffs[t] = bank([P, V], "diffs", t + 6 if t < 2 else t)
-            for cols in halves:
-                for side in range(2):
-                    nc.tensor.matmul(diffs[t][:, cols], tanhs[t][:, side, cols], ident[:], start=(side == 0), stop=(side == 1), is_transpose=True)
+            nc.vector.tensor_tensor(diffs[t][:], tanhs[t][:, 0, :], tanhs[t][:, 1, :], ALU.subtract)
 
         def sigmoid(t):
             for side in range(2):
@@ -173,43 +160,30 @@ def tile_picked_zpt_mul_p_kernel(tc, x_words, x_scales, w1, w2, w3, w4, offs, ce
         for t in range(1, PACK):
             gather_query(t)
 
+        gather_keys(0)
+        tanh(0)
         for t in range(PACK):
             weave_h(t)
-        gather_keys(0)
-        turn(0)
-        tanh(0)
-        difference(0)
         gather_keys(1)
-        turn(1)
         gather_keys(2)
+        difference(0)
         quantise("h", 0, 2)
         quantise("h", 2, 4)
-        multiply("h", 0)
+        for t in range(PACK):
+            multiply("h", t)
         tanh(1)
         sigmoid(0)
         empty("h", 0)
-        difference(1)
-        multiply("h", 1)
         gather_keys(3)
-        turn(2)
-        gather_values(0)
-        sigmoid(1)
-        empty("h", 1)
-        multiply("h", 2)
-        turn(3)
-        tanh(2)
-        difference(2)
-        gather_values(1)
-        multiply("h", 3)
-        tanh(3)
-        difference(3)
-        empty("h", 2)
-        sigmoid(2)
-        gather_values(2)
-        empty("h", 3)
-        sigmoid(3)
+        for t in range(1, PACK):
+            difference(t)
+            gather_values(t - 1)
+            if t + 1 < PACK:
+                tanh(t + 1)
+            empty("h", t)
+            sigmoid(t)
         nc.scalar.copy(out=w4_woven[:].rearrange("p (c i) t -> p c t i", i=4), in_=w4_raw.rearrange("p t (c i) -> p c t i", i=4))
-        gather_values(3)
+        gather_values(PACK - 1)
         nc.vector.quantize_mx(out=w4_codes[:].bitcast(FP8X4), scales=w4_scales[:], in_=w4_woven[:].rearrange("p m t -> p (m t)"))
 
         for cols in halves:

@@ -5,10 +5,10 @@ import concourse.mybir as mybir
 K, T, S, V, H, N = 512, 2048, 512, 256, 512, 256
 P = 128
 PACK = 4
-OCT = 8
 FLOPS = 2 * K * S * H * 3 + 2 * H * N * V
 
-PIECES = (0, 256, 384, 512)
+W1_CUTS = (0, 256, 512)
+W2_CUTS = (0, 256, 384, 512)
 
 F32 = mybir.dt.float32
 BF16 = mybir.dt.bfloat16
@@ -38,73 +38,53 @@ def tile_picked_zpt_mul_p_kernel(tc, x_words, x_scales, w1, w2, w3, w4, offs, ce
             nc.sync.dma_start(lst[:], src)
             return lst
 
+        def k_rows(w, c0, c1):
+            return w.rearrange("(p j) c -> p j c", j=PACK)[:, :, c0:c1]
+
+        warm = tile([P, 2], F32, "warm", tag="words")
+        nc.vector.memset(warm[:, 0:1], 0.0)
+        nc.scalar.activation(warm[:, 1:2], warm[:, 0:1], ACT.Sigmoid)
         scale_table = tile([P, T], U8, "scale_table")
         nc.vector.memset(scale_table[:].bitcast(I32), 0)
 
-        warm = tile([P, 2], F32, "warm", tag="weights")
-        nc.vector.memset(warm[:, 0:1], 0.0)
-        nc.scalar.activation(warm[:, 1:2], warm[:, 0:1], ACT.Sigmoid)
-        weights = tile([P, PACK * (3 * H + N)], F32, "weights")
-
+        raw = {}
         offs_list = load_list(offs, "offs_list")
-        word_table = tile([P, T], I32, "word_table")
         cen_list = load_list(cen, "cen_list")
-        pos_lists = [load_list(pos1, "pos1_list"), load_list(pos2, "pos2_list")]
-        nc.sync.dma_start(out=word_table[:], in_=x_words[0].rearrange("p n j -> p (n j)").bitcast(I32))
+        pos_lists = [load_list(pos1, "pos1_list")]
+        first = tile([P, PACK, W1_CUTS[1]], F32, "w1_first", tag="stage")
+        raw["y", 0] = first[:]
+        nc.sync.dma_start(out=first[:], in_=k_rows(w1, 0, W1_CUTS[1]))
+        second = tile([P, PACK, H - W1_CUTS[1]], F32, "w1_second")
+        raw["y", W1_CUTS[1]] = second[:]
+        nc.sync.dma_start(out=second[:], in_=k_rows(w1, W1_CUTS[1], H))
+        pos_lists.append(load_list(pos2, "pos2_list"))
         scale_rows = x_scales[0].rearrange("(q r) c -> r q c", r=4)
         for r in range(4):
-            nc.scalar.dma_start(out=scale_table[r:P:32, :].bitcast(I32), in_=scale_rows[r].bitcast(I32))
-
-        raw = {}
-        for place, (name, w, cuts) in enumerate((("y", w1, PIECES), ("e", w2, PIECES), ("h", w3, (0, H)))):
-            for c0, c1 in zip(cuts, cuts[1:]):
-                start = PACK * H * place
-                raw[name, c0] = weights[:, start + PACK * c0 : start + PACK * c1].rearrange("p (j c) -> p j c", j=PACK)
-                nc.sync.dma_start(out=raw[name, c0], in_=w.rearrange("(p j) c -> p j c", j=PACK)[:, :, c0:c1])
-        w4_raw = weights[:, 3 * PACK * H :].rearrange("p (t m) -> p t m", t=PACK)
-        w4_rows = w4.rearrange("(b t r) m -> t b r m", t=PACK, r=OCT)
-        for t in range(PACK):
-            nc.sync.dma_start(out=w4_raw[:, t, :], in_=w4_rows[t])
+            nc.sync.dma_start(out=scale_table[r:P:32, :].bitcast(I32), in_=scale_rows[r].bitcast(I32))
+        word_table = tile([P, T], I32, "word_table", tag="words")
+        nc.sync.dma_start(out=word_table[:], in_=x_words[0].rearrange("p n j -> p (n j)").bitcast(I32))
 
         x_codes = tile([P, S], U32, "x_codes")
         x_bytes = tile([P, S], U8, "x_bytes")
-        woven = {name: tile([P, PACK, P, PACK], BF16, name + "_woven", tag="early") for name in "ye"}
+        woven = {"y": tile([P, PACK, P, PACK], BF16, "y_woven")}
         w_scales = {name: tile([P, H], U8, name + "_scales") for name in "yeh"}
-        rows = {(name, t): tile([P, S], F32, name + "_rows%d" % t) for name in "yeh" for t in range(PACK) if (name, t) != ("y", PACK - 1)}
-        rows["y", PACK - 1] = tile([P, S], F32, "y_rows_last", tag="late")
-        woven["h"] = tile([P, PACK, P, PACK], BF16, "h_woven", tag="late")
-        w4_codes = tile([P, N], U32, "w4_codes")
-        w4_scales = tile([P, N], U8, "w4_scales")
-        query_first = tile([P, V], F32, "query_first")
-        query_rest = tile([P, PACK - 1, V], F32, "query_rest", tag="early")
-        query = [query_first[:]] + [query_rest[:, t, :] for t in range(PACK - 1)]
         w_codes = {(name, pair): tile([P, 2 * P], U32, name + "_codes%d" % pair) for name in "yeh" for pair in range(2)}
-        prod = [tile([P, 2, V], F32, "prod%d" % t) for t in range(PACK - 1)] + [tile([P, 2, V], F32, "prod_last", tag="late")]
-        w4_woven = tile([P, N, PACK], BF16, "w4_woven", tag="late")
-        tanhs = [tile([P, 2, V], F32, "tanhs%d" % t) for t in range(PACK)]
-        diffs = [tile([P, V], F32, "diffs%d" % t) for t in range(PACK)]
-        gates = [tile([P, 2, V], F32, "gates%d" % t) for t in range(PACK)]
-        parts = [tile([P, PACK, V], F32, "parts%d" % side) for side in range(2)]
-        z_woven = tile([P, V, PACK], BF16, "z_woven")
-        z_codes = tile([P, V], U32, "z_codes")
-        z_scales = tile([P, V], U8, "z_scales")
+        rows = {(name, t): tile([P, S], F32, name + "_rows%d" % t) for name in "yeh" for t in range(PACK)}
         halves = [slice(0, P), slice(P, 2 * P)]
         signs = [1.0, -1.0]
         sums = {}
 
-        def weave_piece(name, c0, copy):
-            piece = raw[name, c0]
-            places = slice(c0 // PACK, (c0 + piece.shape[2]) // PACK)
-            copy(out=woven[name][:, :, places, :].rearrange("p t (b r) j -> p t b r j", r=OCT),
-                 in_=piece.rearrange("p j (b t r) -> p t b r j", t=PACK, r=OCT))
+        def weave(name, c0, m0, m1, copy):
+            base = c0 // 16
+            copy(out=woven[name][:].rearrange("p t (m r) j -> p m t j r", r=4)[:, base + m0 : base + m1],
+                 in_=raw[name, c0].rearrange("p j (m t r) -> p m t j r", t=PACK, r=4)[:, m0:m1])
 
-        def weave_h(t):
-            nc.scalar.copy(out=woven["h"][:, t, :, :].rearrange("p (b a r) j -> p b a j r", a=2, r=4),
-                           in_=raw["h", 0].rearrange("p j (b t a r) -> p t b a j r", t=PACK, a=2, r=4)[:, t])
+        def weave_piece(name, c0, copy):
+            weave(name, c0, 0, raw[name, c0].shape[2] // 16, copy)
 
         def quantise(name, t0, t1):
-            first = P * (t0 % 2)
-            nc.vector.quantize_mx(out=w_codes[name, t0 // 2][:, first : first + P * (t1 - t0)].bitcast(FP8X4),
+            lo = P * (t0 % 2)
+            nc.vector.quantize_mx(out=w_codes[name, t0 // 2][:, lo : lo + P * (t1 - t0)].bitcast(FP8X4),
                                   scales=w_scales[name][:, P * t0 : P * t1],
                                   in_=woven[name][:, t0:t1, :, :].rearrange("p t m j -> p (t m j)"))
 
@@ -117,12 +97,52 @@ def tile_picked_zpt_mul_p_kernel(tc, x_words, x_scales, w1, w2, w3, w4, offs, ce
         def empty(name, t):
             nc.scalar.copy(out=rows[name, t][:], in_=sums[name, t][:])
 
-        def gather_query(t):
-            nc.vector.tensor_copy(out=query[t], in_=rows["y", t][:].indirect(cen_list[:]))
+        weave_piece("y", 0, nc.vector.tensor_copy)
+
+        weights = tile([P, PACK * (2 * H + N)], F32, "weights", tag="stage")
+        for place, (name, w, cuts) in enumerate((("e", w2, W2_CUTS), ("h", w3, (0, H)))):
+            for c0, c1 in zip(cuts, cuts[1:]):
+                start = PACK * H * place
+                raw[name, c0] = weights[:, start + PACK * c0 : start + PACK * c1].rearrange("p (j c) -> p j c", j=PACK)
+                nc.sync.dma_start(out=raw[name, c0], in_=k_rows(w, c0, c1))
+        w4_raw = weights[:, 2 * PACK * H :].rearrange("p (t n) -> p t n", t=PACK)
+        w4_rows = w4.rearrange("(m t r) n -> t m r n", t=PACK, r=4)
+        for t in range(PACK):
+            nc.sync.dma_start(out=w4_raw[:, t, :], in_=w4_rows[t])
+
+        weave_piece("y", W1_CUTS[1], nc.vector.tensor_copy)
+        nc.vector.tensor_copy(out=x_bytes[:], in_=scale_table[:].indirect(offs_list[:]))
+        quantise("y", 0, 2)
+        quantise("y", 2, 4)
+        nc.vector.tensor_copy(out=x_codes[:], in_=word_table[:].bitcast(U32).indirect(offs_list[:]))
+        for t in range(PACK):
+            multiply("y", t)
+            empty("y", t)
+
+        woven["e"] = tile([P, PACK, P, PACK], BF16, "e_woven", tag="early")
+        for c0 in W2_CUTS[:-1]:
+            weave_piece("e", c0, nc.vector.tensor_copy)
+        quantise("e", 0, 2)
+        quantise("e", 2, 4)
+        for t in range(PACK):
+            multiply("e", t)
+            empty("e", t)
+        query = tile([P, PACK, V], F32, "query", tag="early")
+        for t in range(PACK):
+            nc.vector.tensor_copy(out=query[:, t, :], in_=rows["y", t][:].indirect(cen_list[:]))
+
+        woven["h"] = tile([P, PACK, P, PACK], BF16, "h_woven", tag="late")
+        for m0 in (0, 16):
+            weave("h", 0, m0, m0 + 16, nc.scalar.copy)
+        prod = [tile([P, 2, V], F32, "prod%d" % t) for t in range(PACK - 1)]
+        tanhs = [tile([P, 2, V], F32, "tanhs%d" % t) for t in range(PACK)]
+        diffs = [tile([P, V], F32, "diffs%d" % t) for t in range(PACK)]
+        gates = [tile([P, 2, V], F32, "gates%d" % t) for t in range(PACK)]
+        parts = [tile([P, PACK, V], F32, "parts%d" % side) for side in range(2)]
 
         def gather_keys(t):
             for side in range(2):
-                nc.vector.tensor_tensor(prod[t][:, side, :], rows["e", t][:].indirect(pos_lists[side][:]), query[t], ALU.mult)
+                nc.vector.tensor_tensor(prod[t][:, side, :], rows["e", t][:].indirect(pos_lists[side][:]), query[:, t, :], ALU.mult)
 
         def tanh(t):
             nc.scalar.activation(tanhs[t][:], prod[t][:], ACT.Tanh)
@@ -134,68 +154,49 @@ def tile_picked_zpt_mul_p_kernel(tc, x_words, x_scales, w1, w2, w3, w4, offs, ce
             for side in range(2):
                 nc.scalar.activation(gates[t][:, side, :], diffs[t][:], ACT.Sigmoid, scale=signs[side])
 
-        def gather_values(t):
+        def gather_values(t, v0, v1):
             for side in range(2):
-                nc.vector.tensor_tensor(parts[side][:, t, :], rows["h", t][:].indirect(pos_lists[side][:]), gates[t][:, side, :], ALU.mult)
+                nc.vector.tensor_tensor(parts[side][:, t, v0:v1], rows["h", t][:].indirect(pos_lists[side][:, v0 // 16 : v1 // 16]),
+                                        gates[t][:, side, v0:v1], ALU.mult)
 
-        nc.vector.tensor_copy(out=x_bytes[:], in_=scale_table[:].indirect(offs_list[:]))
-        nc.vector.tensor_copy(out=x_codes[:], in_=word_table[:].bitcast(U32).indirect(offs_list[:]))
-        weave_piece("y", PIECES[0], nc.scalar.copy)
-        for c0 in PIECES[1:-1]:
-            weave_piece("y", c0, nc.vector.tensor_copy)
-        for t0, t1 in ((0, 1), (1, 2), (2, 4)):
-            quantise("y", t0, t1)
-        for t in range(PACK):
-            multiply("y", t)
-            empty("y", t)
-
-        for c0 in PIECES[:-1]:
-            weave_piece("e", c0, nc.vector.tensor_copy)
-        gather_query(0)
-        quantise("e", 0, 2)
-        quantise("e", 2, 4)
-        for t in range(PACK):
-            multiply("e", t)
-            empty("e", t)
-        for t in range(1, PACK):
-            gather_query(t)
-
-        gather_keys(0)
-        tanh(0)
-        for t in range(PACK):
-            weave_h(t)
-        gather_keys(1)
-        gather_keys(2)
-        difference(0)
+        for t in range(PACK - 1):
+            gather_keys(t)
         quantise("h", 0, 2)
         quantise("h", 2, 4)
         for t in range(PACK):
             multiply("h", t)
-        tanh(1)
-        sigmoid(0)
-        empty("h", 0)
-        gather_keys(3)
-        for t in range(1, PACK):
+        prod.append(tile([P, 2, V], F32, "prod_last", tag="late"))
+        gather_keys(PACK - 1)
+        for t in range(PACK - 1):
+            tanh(t)
             difference(t)
-            gather_values(t - 1)
-            if t + 1 < PACK:
-                tanh(t + 1)
-            empty("h", t)
+        empty("h", 0)
+        tanh(PACK - 1)
+        difference(PACK - 1)
+        for t in range(PACK):
+            if t > 0:
+                empty("h", t)
             sigmoid(t)
-        nc.scalar.copy(out=w4_woven[:].rearrange("p (c i) t -> p c t i", i=4), in_=w4_raw.rearrange("p t (c i) -> p c t i", i=4))
-        gather_values(PACK - 1)
-        nc.vector.quantize_mx(out=w4_codes[:].bitcast(FP8X4), scales=w4_scales[:], in_=w4_woven[:].rearrange("p m t -> p (m t)"))
+            if t < PACK - 1:
+                gather_values(t, 0, V)
 
-        for cols in halves:
+        w4_woven = tile([P, N, PACK], BF16, "w4_woven", tag="late")
+        w4_codes = tile([P, N], U32, "w4_codes")
+        w4_scales = tile([P, N], U8, "w4_scales")
+        z_woven = tile([P, V, PACK], BF16, "z_woven")
+        z_codes = tile([P, V], U32, "z_codes")
+        z_scales = tile([P, V], U8, "z_scales")
+        nc.scalar.copy(out=w4_woven[:].rearrange("p (c i) t -> p c t i", i=4), in_=w4_raw.rearrange("p t (c i) -> p c t i", i=4))
+        nc.vector.quantize_mx(out=w4_codes[:].bitcast(FP8X4), scales=w4_scales[:], in_=w4_woven[:].rearrange("p m t -> p (m t)"))
+        for half, cols in enumerate(halves):
+            gather_values(PACK - 1, cols.start, cols.stop)
             nc.vector.tensor_tensor(z_woven[:, cols, :].rearrange("p (c i) t -> p c t i", i=4),
                                     parts[0][:, :, cols].rearrange("p t (c i) -> p c t i", i=4),
                                     parts[1][:, :, cols].rearrange("p t (c i) -> p c t i", i=4), ALU.add)
-        for cols in halves:
             nc.vector.quantize_mx(out=z_codes[:, cols].bitcast(FP8X4), scales=z_scales[:, cols],
                                   in_=z_woven[:, cols, :].rearrange("p v t -> p (v t)"))
-        for half, cols in enumerate(halves):
             for block, out_rows in enumerate(halves):
-                result = bank([P, P], "result", 2 * half + block)
+                result = bank([P, P], "result", PACK + 2 * half + block)
                 nc.tensor.matmul_mx(out=result[:], lhsT=w4_codes[:, out_rows].bitcast(FP8X4), lhsT_scale=w4_scales[:, out_rows],
                                     rhs=z_codes[:, cols].bitcast(FP8X4), rhs_scale=z_scales[:, cols], start=True, stop=True)
                 staged = tile([P, P], F32, "staged%d%d" % (half, block))

@@ -7,9 +7,6 @@ P = 128
 PACK = 4
 FLOPS = 2 * K * S * H * 3 + 2 * H * N * V
 
-W1_CUTS = (0, 256, 512)
-W2_CUTS = (0, 256, 384, 512)
-
 F32 = mybir.dt.float32
 BF16 = mybir.dt.bfloat16
 I32 = mybir.dt.int32
@@ -38,55 +35,57 @@ def tile_picked_zpt_mul_p_kernel(tc, x_words, x_scales, w1, w2, w3, w4, offs, ce
             nc.sync.dma_start(lst[:], src)
             return lst
 
-        def k_rows(w, c0, c1):
-            return w.rearrange("(p j) c -> p j c", j=PACK)[:, :, c0:c1]
+        def k_rows(w):
+            return w.rearrange("(p j) c -> p j c", j=PACK)
 
-        warm = tile([P, 2], F32, "warm", tag="words")
-        nc.vector.memset(warm[:, 0:1], 0.0)
-        nc.scalar.activation(warm[:, 1:2], warm[:, 0:1], ACT.Sigmoid)
+        pairs = [slice(0, 2), slice(2, 4)]
+
+        warm_in = tile([P, 1], F32, "warm_in", tag="words")
+        warm_out = tile([P, 1], F32, "warm_out", tag="weights")
+        nc.vector.memset(warm_in[:], 0.0)
+        nc.scalar.activation(warm_out[:], warm_in[:], ACT.Sigmoid)
         scale_table = tile([P, T], U8, "scale_table")
         nc.vector.memset(scale_table[:].bitcast(I32), 0)
 
-        raw = {}
         offs_list = load_list(offs, "offs_list")
         cen_list = load_list(cen, "cen_list")
         pos_lists = [load_list(pos1, "pos1_list")]
-        first = tile([P, PACK, W1_CUTS[1]], F32, "w1_first", tag="stage")
-        raw["y", 0] = first[:]
-        nc.sync.dma_start(out=first[:], in_=k_rows(w1, 0, W1_CUTS[1]))
-        second = tile([P, PACK, H - W1_CUTS[1]], F32, "w1_second")
-        raw["y", W1_CUTS[1]] = second[:]
-        nc.sync.dma_start(out=second[:], in_=k_rows(w1, W1_CUTS[1], H))
+        w1_raw = tile([P, PACK, H], F32, "w1_raw")
+        nc.sync.dma_start(out=w1_raw[:], in_=k_rows(w1))
         pos_lists.append(load_list(pos2, "pos2_list"))
         scale_rows = x_scales[0].rearrange("(q r) c -> r q c", r=4)
         for r in range(4):
             nc.sync.dma_start(out=scale_table[r:P:32, :].bitcast(I32), in_=scale_rows[r].bitcast(I32))
         word_table = tile([P, T], I32, "word_table", tag="words")
         nc.sync.dma_start(out=word_table[:], in_=x_words[0].rearrange("p n j -> p (n j)").bitcast(I32))
+        weights = tile([P, PACK * (2 * H + N)], F32, "weights", tag="weights")
+        raw = {"y": w1_raw[:]}
+        for place, name in enumerate("eh"):
+            raw[name] = weights[:, PACK * H * place : PACK * H * (place + 1)].rearrange("p (j c) -> p j c", j=PACK)
+        nc.sync.dma_start(out=raw["e"], in_=k_rows(w2))
+        nc.sync.dma_start(out=raw["h"], in_=k_rows(w3))
+        w4_raw = weights[:, 2 * PACK * H :].rearrange("p (t n) -> p t n", t=PACK)
+        w4_rows = w4.rearrange("(m t r) n -> t m r n", t=PACK, r=4)
+        for t in range(PACK):
+            nc.sync.dma_start(out=w4_raw[:, t, :], in_=w4_rows[t])
 
         x_codes = tile([P, S], U32, "x_codes")
         x_bytes = tile([P, S], U8, "x_bytes")
-        woven = {"y": tile([P, PACK, P, PACK], BF16, "y_woven")}
+        woven = {("y", pair): tile([P, 2, P, PACK], BF16, "y_woven%d" % pair)[:] for pair in range(2)}
         w_scales = {name: tile([P, H], U8, name + "_scales") for name in "yeh"}
-        w_codes = {(name, pair): tile([P, 2 * P], U32, name + "_codes%d" % pair) for name in "yeh" for pair in range(2)}
+        w_codes = {(name, pair): tile([P, 2 * P], U32, name + "_codes%d" % pair, tag="late" if (name, pair) == ("e", 1) else None) for name in "yeh" for pair in range(2)}
         rows = {(name, t): tile([P, S], F32, name + "_rows%d" % t) for name in "yeh" for t in range(PACK)}
         halves = [slice(0, P), slice(P, 2 * P)]
         signs = [1.0, -1.0]
         sums = {}
 
-        def weave(name, c0, m0, m1, copy):
-            base = c0 // 16
-            copy(out=woven[name][:].rearrange("p t (m r) j -> p m t j r", r=4)[:, base + m0 : base + m1],
-                 in_=raw[name, c0].rearrange("p j (m t r) -> p m t j r", t=PACK, r=4)[:, m0:m1])
+        def weave(dst, name, ts, js, copy):
+            copy(out=dst.rearrange("p t (m r) j -> p m t j r", r=4)[:, :, :, js, :],
+                 in_=raw[name].rearrange("p j (m t r) -> p m t j r", t=PACK, r=4)[:, :, ts, js, :])
 
-        def weave_piece(name, c0, copy):
-            weave(name, c0, 0, raw[name, c0].shape[2] // 16, copy)
-
-        def quantise(name, t0, t1):
-            lo = P * (t0 % 2)
-            nc.vector.quantize_mx(out=w_codes[name, t0 // 2][:, lo : lo + P * (t1 - t0)].bitcast(FP8X4),
-                                  scales=w_scales[name][:, P * t0 : P * t1],
-                                  in_=woven[name][:, t0:t1, :, :].rearrange("p t m j -> p (t m j)"))
+        def quantise(name, pair):
+            nc.vector.quantize_mx(out=w_codes[name, pair][:].bitcast(FP8X4), scales=w_scales[name][:, 2 * P * pair : 2 * P * (pair + 1)],
+                                  in_=woven[name, pair].rearrange("p t m j -> p (t m j)"))
 
         def multiply(name, t):
             sums[name, t] = bank([P, S], "sums", t + PACK if name == "e" else t)
@@ -97,43 +96,34 @@ def tile_picked_zpt_mul_p_kernel(tc, x_words, x_scales, w1, w2, w3, w4, offs, ce
         def empty(name, t):
             nc.scalar.copy(out=rows[name, t][:], in_=sums[name, t][:])
 
-        weave_piece("y", 0, nc.vector.tensor_copy)
-
-        weights = tile([P, PACK * (2 * H + N)], F32, "weights", tag="stage")
-        for place, (name, w, cuts) in enumerate((("e", w2, W2_CUTS), ("h", w3, (0, H)))):
-            for c0, c1 in zip(cuts, cuts[1:]):
-                start = PACK * H * place
-                raw[name, c0] = weights[:, start + PACK * c0 : start + PACK * c1].rearrange("p (j c) -> p j c", j=PACK)
-                nc.sync.dma_start(out=raw[name, c0], in_=k_rows(w, c0, c1))
-        w4_raw = weights[:, 2 * PACK * H :].rearrange("p (t n) -> p t n", t=PACK)
-        w4_rows = w4.rearrange("(m t r) n -> t m r n", t=PACK, r=4)
-        for t in range(PACK):
-            nc.sync.dma_start(out=w4_raw[:, t, :], in_=w4_rows[t])
-
-        weave_piece("y", W1_CUTS[1], nc.vector.tensor_copy)
+        weave(woven["y", 0], "y", pairs[0], slice(0, PACK), nc.vector.tensor_copy)
+        weave(woven["y", 1], "y", pairs[1], slice(0, PACK), nc.scalar.copy)
         nc.vector.tensor_copy(out=x_bytes[:], in_=scale_table[:].indirect(offs_list[:]))
-        quantise("y", 0, 2)
-        quantise("y", 2, 4)
+        quantise("y", 0)
+        quantise("y", 1)
         nc.vector.tensor_copy(out=x_codes[:], in_=word_table[:].bitcast(U32).indirect(offs_list[:]))
         for t in range(PACK):
             multiply("y", t)
             empty("y", t)
 
-        woven["e"] = tile([P, PACK, P, PACK], BF16, "e_woven", tag="early")
-        for c0 in W2_CUTS[:-1]:
-            weave_piece("e", c0, nc.vector.tensor_copy)
-        quantise("e", 0, 2)
-        quantise("e", 2, 4)
+        for pair, ts in enumerate(pairs):
+            woven["e", pair] = tile([P, 2, P, PACK], BF16, "e_woven%d" % pair, tag="early%d" % pair)[:]
+            weave(woven["e", pair], "e", ts, slice(0, PACK), nc.vector.tensor_copy)
+        quantise("e", 0)
+        quantise("e", 1)
         for t in range(PACK):
             multiply("e", t)
             empty("e", t)
-        query = tile([P, PACK, V], F32, "query", tag="early")
+        query_first = tile([P, V], F32, "query_first", tag="early0")
+        query_rest = tile([P, PACK - 1, V], F32, "query_rest", tag="early1")
+        query = [query_first[:]] + [query_rest[:, t, :] for t in range(PACK - 1)]
         for t in range(PACK):
-            nc.vector.tensor_copy(out=query[:, t, :], in_=rows["y", t][:].indirect(cen_list[:]))
+            nc.vector.tensor_copy(out=query[t], in_=rows["y", t][:].indirect(cen_list[:]))
 
-        woven["h"] = tile([P, PACK, P, PACK], BF16, "h_woven", tag="late")
-        for m0 in (0, 16):
-            weave("h", 0, m0, m0 + 16, nc.scalar.copy)
+        h_woven = tile([P, PACK, P, PACK], BF16, "h_woven", tag="late")
+        for pair, ts in enumerate(pairs):
+            woven["h", pair] = h_woven[:, ts, :, :]
+            weave(woven["h", pair], "h", ts, slice(0, PACK), nc.scalar.copy)
         prod = [tile([P, 2, V], F32, "prod%d" % t) for t in range(PACK - 1)]
         tanhs = [tile([P, 2, V], F32, "tanhs%d" % t) for t in range(PACK)]
         diffs = [tile([P, V], F32, "diffs%d" % t) for t in range(PACK)]
@@ -142,7 +132,7 @@ def tile_picked_zpt_mul_p_kernel(tc, x_words, x_scales, w1, w2, w3, w4, offs, ce
 
         def gather_keys(t):
             for side in range(2):
-                nc.vector.tensor_tensor(prod[t][:, side, :], rows["e", t][:].indirect(pos_lists[side][:]), query[:, t, :], ALU.mult)
+                nc.vector.tensor_tensor(prod[t][:, side, :], rows["e", t][:].indirect(pos_lists[side][:]), query[t], ALU.mult)
 
         def tanh(t):
             nc.scalar.activation(tanhs[t][:], prod[t][:], ACT.Tanh)
@@ -161,8 +151,8 @@ def tile_picked_zpt_mul_p_kernel(tc, x_words, x_scales, w1, w2, w3, w4, offs, ce
 
         for t in range(PACK - 1):
             gather_keys(t)
-        quantise("h", 0, 2)
-        quantise("h", 2, 4)
+        quantise("h", 0)
+        quantise("h", 1)
         for t in range(PACK):
             multiply("h", t)
         prod.append(tile([P, 2, V], F32, "prod_last", tag="late"))

@@ -40,31 +40,29 @@ def tile_picked_zpt_mul_p_kernel(tc, x_words, x_scales, w1, w2, w3, w4, offs, ce
 
         pairs = [slice(0, 2), slice(2, 4)]
 
-        warm_in = tile([P, 1], F32, "warm_in", tag="words")
-        warm_out = tile([P, 1], F32, "warm_out", tag="weights")
-        nc.vector.memset(warm_in[:], 0.0)
-        nc.scalar.activation(warm_out[:], warm_in[:], ACT.Sigmoid)
         scale_table = tile([P, T], U8, "scale_table")
         nc.vector.memset(scale_table[:].bitcast(I32), 0)
+        warm = tile([P, 2], F32, "warm")
+        nc.vector.memset(warm[:, 0:1], 0.0)
+        nc.scalar.activation(warm[:, 1:2], warm[:, 0:1], ACT.Sigmoid)
 
         offs_list = load_list(offs, "offs_list")
+        word_table = tile([P, T], I32, "word_table")
+        nc.sync.dma_start(out=word_table[:], in_=x_words[0].rearrange("p n j -> p (n j)").bitcast(I32))
         cen_list = load_list(cen, "cen_list")
         pos_lists = [load_list(pos1, "pos1_list")]
-        w1_raw = tile([P, PACK, H], F32, "w1_raw")
-        nc.sync.dma_start(out=w1_raw[:], in_=k_rows(w1))
-        pos_lists.append(load_list(pos2, "pos2_list"))
         scale_rows = x_scales[0].rearrange("(q r) c -> r q c", r=4)
         for r in range(4):
             nc.sync.dma_start(out=scale_table[r:P:32, :].bitcast(I32), in_=scale_rows[r].bitcast(I32))
-        word_table = tile([P, T], I32, "word_table", tag="words")
-        nc.sync.dma_start(out=word_table[:], in_=x_words[0].rearrange("p n j -> p (n j)").bitcast(I32))
-        weights = tile([P, PACK * (2 * H + N)], F32, "weights", tag="weights")
-        raw = {"y": w1_raw[:]}
-        for place, name in enumerate("eh"):
-            raw[name] = weights[:, PACK * H * place : PACK * H * (place + 1)].rearrange("p (j c) -> p j c", j=PACK)
-        nc.sync.dma_start(out=raw["e"], in_=k_rows(w2))
-        nc.sync.dma_start(out=raw["h"], in_=k_rows(w3))
-        w4_raw = weights[:, 2 * PACK * H :].rearrange("p (t n) -> p t n", t=PACK)
+        w1_raw = tile([P, PACK, H], F32, "w1_raw")
+        nc.sync.dma_start(out=w1_raw[:], in_=k_rows(w1))
+        pos_lists.append(load_list(pos2, "pos2_list"))
+        w2_raw = tile([P, PACK, H], F32, "w2_raw")
+        nc.sync.dma_start(out=w2_raw[:], in_=k_rows(w2))
+        w3_raw = tile([P, PACK, H], F32, "w3_raw")
+        nc.sync.dma_start(out=w3_raw[:], in_=k_rows(w3))
+        raw = {"y": w1_raw[:], "e": w2_raw[:], "h": w3_raw[:]}
+        w4_raw = tile([P, PACK, N], F32, "w4_raw")[:]
         w4_rows = w4.rearrange("(m t r) n -> t m r n", t=PACK, r=4)
         for t in range(PACK):
             nc.sync.dma_start(out=w4_raw[:, t, :], in_=w4_rows[t])
@@ -73,8 +71,8 @@ def tile_picked_zpt_mul_p_kernel(tc, x_words, x_scales, w1, w2, w3, w4, offs, ce
         x_bytes = tile([P, S], U8, "x_bytes")
         woven = {("y", pair): tile([P, 2, P, PACK], BF16, "y_woven%d" % pair)[:] for pair in range(2)}
         w_scales = {name: tile([P, H], U8, name + "_scales") for name in "yeh"}
-        w_codes = {(name, pair): tile([P, 2 * P], U32, name + "_codes%d" % pair, tag="late" if (name, pair) == ("e", 1) else None) for name in "yeh" for pair in range(2)}
-        rows = {(name, t): tile([P, S], F32, name + "_rows%d" % t) for name in "yeh" for t in range(PACK)}
+        w_codes = {(name, pair): tile([P, 2 * P], U32, name + "_codes%d" % pair) for name in "yeh" for pair in range(2)}
+        rows = {(name, t): tile([P, S], F32, name + "_rows%d" % t)[:] for name in "yeh" for t in range(PACK)}
         halves = [slice(0, P), slice(P, 2 * P)]
         signs = [1.0, -1.0]
         sums = {}
@@ -94,14 +92,24 @@ def tile_picked_zpt_mul_p_kernel(tc, x_words, x_scales, w1, w2, w3, w4, offs, ce
                                 rhs=x_codes[:].bitcast(FP8X4), rhs_scale=x_bytes[:], start=True, stop=True)
 
         def empty(name, t):
-            nc.scalar.copy(out=rows[name, t][:], in_=sums[name, t][:])
+            nc.scalar.copy(out=rows[name, t], in_=sums[name, t][:])
 
-        weave(woven["y", 0], "y", pairs[0], slice(0, PACK), nc.vector.tensor_copy)
-        weave(woven["y", 1], "y", pairs[1], slice(0, PACK), nc.scalar.copy)
-        nc.vector.tensor_copy(out=x_bytes[:], in_=scale_table[:].indirect(offs_list[:]))
-        quantise("y", 0)
-        quantise("y", 1)
         nc.vector.tensor_copy(out=x_codes[:], in_=word_table[:].bitcast(U32).indirect(offs_list[:]))
+        nc.vector.tensor_copy(out=x_bytes[:], in_=scale_table[:].indirect(offs_list[:]))
+        def weave_y(t, copy):
+            weave(woven["y", t // 2][:, t % 2 : t % 2 + 1], "y", slice(t, t + 1), slice(0, PACK), copy)
+
+        def quantise_y(t):
+            nc.vector.quantize_mx(out=w_codes["y", 0][:, halves[t]].bitcast(FP8X4), scales=w_scales["y"][:, halves[t]],
+                                  in_=woven["y", 0][:, t].rearrange("p m j -> p (m j)"))
+
+        weave_y(0, nc.vector.tensor_copy)
+        weave_y(1, nc.vector.tensor_copy)
+        weave_y(3, nc.scalar.copy)
+        quantise_y(0)
+        weave_y(2, nc.vector.tensor_copy)
+        quantise_y(1)
+        quantise("y", 1)
         for t in range(PACK):
             multiply("y", t)
             empty("y", t)
@@ -118,12 +126,10 @@ def tile_picked_zpt_mul_p_kernel(tc, x_words, x_scales, w1, w2, w3, w4, offs, ce
         query_rest = tile([P, PACK - 1, V], F32, "query_rest", tag="early1")
         query = [query_first[:]] + [query_rest[:, t, :] for t in range(PACK - 1)]
         for t in range(PACK):
-            nc.vector.tensor_copy(out=query[t], in_=rows["y", t][:].indirect(cen_list[:]))
+            nc.vector.tensor_copy(out=query[t], in_=rows["y", t].indirect(cen_list[:]))
 
-        h_woven = tile([P, PACK, P, PACK], BF16, "h_woven", tag="late")
-        for pair, ts in enumerate(pairs):
-            woven["h", pair] = h_woven[:, ts, :, :]
-            weave(woven["h", pair], "h", ts, slice(0, PACK), nc.scalar.copy)
+        for pair in range(2):
+            woven["h", pair] = tile([P, 2, P, PACK], BF16, "h_woven%d" % pair)[:]
         prod = [tile([P, 2, V], F32, "prod%d" % t) for t in range(PACK - 1)]
         tanhs = [tile([P, 2, V], F32, "tanhs%d" % t) for t in range(PACK)]
         diffs = [tile([P, V], F32, "diffs%d" % t) for t in range(PACK)]
@@ -132,7 +138,7 @@ def tile_picked_zpt_mul_p_kernel(tc, x_words, x_scales, w1, w2, w3, w4, offs, ce
 
         def gather_keys(t):
             for side in range(2):
-                nc.vector.tensor_tensor(prod[t][:, side, :], rows["e", t][:].indirect(pos_lists[side][:]), query[t], ALU.mult)
+                nc.vector.tensor_tensor(prod[t][:, side, :], rows["e", t].indirect(pos_lists[side][:]), query[t], ALU.mult)
 
         def tanh(t):
             nc.scalar.activation(tanhs[t][:], prod[t][:], ACT.Tanh)
@@ -146,31 +152,36 @@ def tile_picked_zpt_mul_p_kernel(tc, x_words, x_scales, w1, w2, w3, w4, offs, ce
 
         def gather_values(t, v0, v1):
             for side in range(2):
-                nc.vector.tensor_tensor(parts[side][:, t, v0:v1], rows["h", t][:].indirect(pos_lists[side][:, v0 // 16 : v1 // 16]),
+                nc.vector.tensor_tensor(parts[side][:, t, v0:v1], rows["h", t].indirect(pos_lists[side][:, v0 // 16 : v1 // 16]),
                                         gates[t][:, side, v0:v1], ALU.mult)
+
+        def values(pair):
+            weave(woven["h", pair], "h", pairs[pair], slice(0, PACK), nc.scalar.copy)
+            quantise("h", pair)
+            multiply("h", 2 * pair)
+            multiply("h", 2 * pair + 1)
 
         for t in range(PACK - 1):
             gather_keys(t)
-        quantise("h", 0)
-        quantise("h", 1)
-        for t in range(PACK):
-            multiply("h", t)
-        prod.append(tile([P, 2, V], F32, "prod_last", tag="late"))
+        values(0)
+        tanh(0)
+        difference(0)
+        prod.append(tile([P, 2, V], F32, "prod_last", tag="prod0"))
         gather_keys(PACK - 1)
-        for t in range(PACK - 1):
+        values(1)
+        for t in range(1, PACK - 1):
             tanh(t)
             difference(t)
-        empty("h", 0)
-        tanh(PACK - 1)
-        difference(PACK - 1)
         for t in range(PACK):
-            if t > 0:
-                empty("h", t)
             sigmoid(t)
+            empty("h", t)
+            if t == 0:
+                tanh(PACK - 1)
+                difference(PACK - 1)
             if t < PACK - 1:
                 gather_values(t, 0, V)
 
-        w4_woven = tile([P, N, PACK], BF16, "w4_woven", tag="late")
+        w4_woven = tile([P, N, PACK], BF16, "w4_woven", tag="prod0")
         w4_codes = tile([P, N], U32, "w4_codes")
         w4_scales = tile([P, N], U8, "w4_scales")
         z_woven = tile([P, V, PACK], BF16, "z_woven")

@@ -59,9 +59,10 @@ def tile_picked_zpt_mul_p_kernel(tc, x_words, x_scales, w1, w2, w3, w4, offs, ce
         pos_lists.append(load_list(pos2, "pos2_list"))
         w2_raw = tile([P, PACK, H], F32, "w2_raw")
         nc.sync.dma_start(out=w2_raw[:], in_=k_rows(w2))
-        w3_raw = tile([P, PACK, H], F32, "w3_raw")
-        nc.sync.dma_start(out=w3_raw[:], in_=k_rows(w3))
-        raw = {"y": w1_raw[:], "e": w2_raw[:], "h": w3_raw[:]}
+        w3_raw = [tile([P, PACK, H // 2], F32, "w3_raw%d" % half) for half in range(2)]
+        for half in range(2):
+            nc.sync.dma_start(out=w3_raw[half][:], in_=k_rows(w3)[:, :, half * H // 2 : (half + 1) * H // 2])
+        raw = {"y": w1_raw[:], "e": w2_raw[:]}
         w4_raw = tile([P, PACK, N], F32, "w4_raw")[:]
         w4_rows = w4.rearrange("(m t r) n -> t m r n", t=PACK, r=4)
         for t in range(PACK):
@@ -128,8 +129,11 @@ def tile_picked_zpt_mul_p_kernel(tc, x_words, x_scales, w1, w2, w3, w4, offs, ce
         for t in range(PACK):
             nc.vector.tensor_copy(out=query[t], in_=rows["y", t].indirect(cen_list[:]))
 
-        for pair in range(2):
-            woven["h", pair] = tile([P, 2, P, PACK], BF16, "h_woven%d" % pair)[:]
+        h_woven = tile([P, PACK, P, PACK], BF16, "h_woven")
+        for half in range(2):
+            woven["h", half] = h_woven[:, pairs[half]]
+            nc.scalar.copy(out=h_woven[:].rearrange("p t (m r) j -> p m t j r", r=4)[:, 16 * half : 16 * (half + 1)],
+                           in_=w3_raw[half][:].rearrange("p j (m t r) -> p m t j r", t=PACK, r=4))
         prod = [tile([P, 2, V], F32, "prod%d" % t) for t in range(PACK - 1)]
         tanhs = [tile([P, 2, V], F32, "tanhs%d" % t) for t in range(PACK)]
         diffs = [tile([P, V], F32, "diffs%d" % t) for t in range(PACK)]
@@ -156,7 +160,6 @@ def tile_picked_zpt_mul_p_kernel(tc, x_words, x_scales, w1, w2, w3, w4, offs, ce
                                         gates[t][:, side, v0:v1], ALU.mult)
 
         def values(pair):
-            weave(woven["h", pair], "h", pairs[pair], slice(0, PACK), nc.scalar.copy)
             quantise("h", pair)
             multiply("h", 2 * pair)
             multiply("h", 2 * pair + 1)

@@ -5,6 +5,7 @@ import concourse.mybir as mybir
 K, T, S, V, H, N = 512, 2048, 512, 256, 512, 256
 P = 128
 PACK = 4
+EARLY = 192
 FLOPS = 2 * K * S * H * 3 + 2 * H * N * V
 
 F32 = mybir.dt.float32
@@ -41,27 +42,28 @@ def tile_picked_zpt_mul_p_kernel(tc, x_words, x_scales, w1, w2, w3, w4, offs, ce
         pairs = [slice(0, 2), slice(2, 4)]
 
         scale_table = tile([P, T], U8, "scale_table")
-        nc.vector.memset(scale_table[:].bitcast(I32), 0)
+        nc.vector.memset(scale_table[:, : T // 2].bitcast(I32), 0)
+        nc.gpsimd.memset(scale_table[:, T // 2 :].bitcast(I32), 0)
         warm = tile([P, 2], F32, "warm")
         nc.vector.memset(warm[:, 0:1], 0.0)
         nc.scalar.activation(warm[:, 1:2], warm[:, 0:1], ACT.Sigmoid)
 
-        offs_list = load_list(offs, "offs_list")
         word_table = tile([P, T], I32, "word_table")
         nc.sync.dma_start(out=word_table[:], in_=x_words[0].rearrange("p n j -> p (n j)").bitcast(I32))
+        offs_list = load_list(offs, "offs_list")
         cen_list = load_list(cen, "cen_list")
-        pos_lists = [load_list(pos1, "pos1_list")]
         scale_rows = x_scales[0].rearrange("(q r) c -> r q c", r=4)
         for r in range(4):
             nc.sync.dma_start(out=scale_table[r:P:32, :].bitcast(I32), in_=scale_rows[r].bitcast(I32))
         w1_raw = tile([P, PACK, H], F32, "w1_raw")
         nc.sync.dma_start(out=w1_raw[:], in_=k_rows(w1))
-        pos_lists.append(load_list(pos2, "pos2_list"))
+        w3_cols = [slice(0, EARLY), slice(EARLY, H)]
+        w3_raw = [tile([P, PACK, cols.stop - cols.start], F32, "w3_raw%d" % half) for half, cols in enumerate(w3_cols)]
+        nc.sync.dma_start(out=w3_raw[0][:], in_=k_rows(w3)[:, :, w3_cols[0]])
         w2_raw = tile([P, PACK, H], F32, "w2_raw")
         nc.sync.dma_start(out=w2_raw[:], in_=k_rows(w2))
-        w3_raw = [tile([P, PACK, H // 2], F32, "w3_raw%d" % half) for half in range(2)]
-        for half in range(2):
-            nc.sync.dma_start(out=w3_raw[half][:], in_=k_rows(w3)[:, :, half * H // 2 : (half + 1) * H // 2])
+        nc.sync.dma_start(out=w3_raw[1][:], in_=k_rows(w3)[:, :, w3_cols[1]])
+        pos_lists = [load_list(pos1, "pos1_list"), load_list(pos2, "pos2_list")]
         raw = {"y": w1_raw[:], "e": w2_raw[:]}
         w4_raw = tile([P, PACK, N], F32, "w4_raw")[:]
         w4_rows = w4.rearrange("(m t r) n -> t m r n", t=PACK, r=4)
@@ -105,36 +107,52 @@ def tile_picked_zpt_mul_p_kernel(tc, x_words, x_scales, w1, w2, w3, w4, offs, ce
                                   in_=woven["y", 0][:, t].rearrange("p m j -> p (m j)"))
 
         weave_y(0, nc.vector.tensor_copy)
-        weave_y(1, nc.vector.tensor_copy)
+        weave_y(1, nc.scalar.copy)
         weave_y(3, nc.scalar.copy)
         quantise_y(0)
         weave_y(2, nc.vector.tensor_copy)
         quantise_y(1)
         quantise("y", 1)
-        for t in range(PACK):
+        for part in range(2):
+            cols = slice(part * S // 2, (part + 1) * S // 2)
+            half_sums = bank([P, S // 2], "half_sums", PACK * (1 - part))
+            nc.tensor.matmul_mx(out=half_sums[:], lhsT=w_codes["y", 0][:, halves[0]].bitcast(FP8X4), lhsT_scale=w_scales["y"][:, halves[0]],
+                                rhs=x_codes[:, cols].bitcast(FP8X4), rhs_scale=x_bytes[:, cols], start=True, stop=True)
+            nc.scalar.copy(out=rows["y", 0][:, cols], in_=half_sums[:])
+        for t in range(1, PACK):
             multiply("y", t)
             empty("y", t)
-
-        for pair, ts in enumerate(pairs):
-            woven["e", pair] = tile([P, 2, P, PACK], BF16, "e_woven%d" % pair, tag="early%d" % pair)[:]
-            weave(woven["e", pair], "e", ts, slice(0, PACK), nc.vector.tensor_copy)
-        quantise("e", 0)
-        quantise("e", 1)
-        for t in range(PACK):
-            multiply("e", t)
-            empty("e", t)
-        query_first = tile([P, V], F32, "query_first", tag="early0")
-        query_rest = tile([P, PACK - 1, V], F32, "query_rest", tag="early1")
-        query = [query_first[:]] + [query_rest[:, t, :] for t in range(PACK - 1)]
-        for t in range(PACK):
-            nc.vector.tensor_copy(out=query[t], in_=rows["y", t].indirect(cen_list[:]))
 
         h_woven = tile([P, PACK, P, PACK], BF16, "h_woven")
         for half in range(2):
             woven["h", half] = h_woven[:, pairs[half]]
-            nc.scalar.copy(out=h_woven[:].rearrange("p t (m r) j -> p m t j r", r=4)[:, 16 * half : 16 * (half + 1)],
-                           in_=w3_raw[half][:].rearrange("p j (m t r) -> p m t j r", t=PACK, r=4))
-        prod = [tile([P, 2, V], F32, "prod%d" % t) for t in range(PACK - 1)]
+
+        def weave_values(half, copy):
+            copy(out=h_woven[:].rearrange("p t (m r) j -> p m t j r", r=4)[:, w3_cols[half].start // 16 : w3_cols[half].stop // 16],
+                 in_=w3_raw[half][:].rearrange("p j (m t r) -> p m t j r", t=PACK, r=4))
+
+        def gather_query(t):
+            nc.vector.tensor_copy(out=query[t], in_=rows["y", t].indirect(cen_list[:]))
+
+        weave_values(0, nc.vector.tensor_copy)
+        query_early = tile([P, 2, V], F32, "query_early", tag="w3_raw0")
+        query = [query_early[:, t, :] for t in range(2)]
+        gather_query(0)
+        gather_query(1)
+        e_single = [tile([P, 1, P, PACK], BF16, "e_single%d" % t)[:] for t in range(2)]
+        woven["e", 1] = tile([P, 2, P, PACK], BF16, "e_woven1", tag="y_codes1")[:]
+        for t in range(2):
+            weave(e_single[t], "e", slice(t, t + 1), slice(0, PACK), nc.vector.tensor_copy)
+        weave(woven["e", 1], "e", pairs[1], slice(0, PACK), nc.scalar.copy)
+        for t in range(2):
+            nc.vector.quantize_mx(out=w_codes["e", 0][:, halves[t]].bitcast(FP8X4), scales=w_scales["e"][:, halves[t]],
+                                  in_=e_single[t].rearrange("p t m j -> p (t m j)"))
+        query_late = tile([P, 2, V], F32, "query_late", tag="e_single0")
+        query = query + [query_late[:, t, :] for t in range(2)]
+        gather_query(2)
+        gather_query(3)
+        quantise("e", 1)
+        prod = [tile([P, 2, V], F32, "prod%d" % t, tag="w2_raw" if t == 0 else None) for t in range(PACK)]
         tanhs = [tile([P, 2, V], F32, "tanhs%d" % t) for t in range(PACK)]
         diffs = [tile([P, V], F32, "diffs%d" % t) for t in range(PACK)]
         gates = [tile([P, 2, V], F32, "gates%d" % t) for t in range(PACK)]
@@ -164,27 +182,32 @@ def tile_picked_zpt_mul_p_kernel(tc, x_words, x_scales, w1, w2, w3, w4, offs, ce
             multiply("h", 2 * pair)
             multiply("h", 2 * pair + 1)
 
-        for t in range(PACK - 1):
+        def keys(t):
+            multiply("e", t)
+            empty("e", t)
             gather_keys(t)
-        values(0)
-        tanh(0)
-        difference(0)
-        prod.append(tile([P, 2, V], F32, "prod_last", tag="prod0"))
-        gather_keys(PACK - 1)
-        values(1)
-        for t in range(1, PACK - 1):
+
+        def scores(t):
             tanh(t)
             difference(t)
+
+        keys(0)
+        keys(1)
+        weave_values(1, nc.scalar.copy)
+        values(0)
+        keys(2)
+        scores(0)
+        keys(3)
+        values(1)
         for t in range(PACK):
-            sigmoid(t)
+            if t < PACK - 1:
+                scores(t + 1)
             empty("h", t)
-            if t == 0:
-                tanh(PACK - 1)
-                difference(PACK - 1)
+            sigmoid(t)
             if t < PACK - 1:
                 gather_values(t, 0, V)
 
-        w4_woven = tile([P, N, PACK], BF16, "w4_woven", tag="prod0")
+        w4_woven = tile([P, N, PACK], BF16, "w4_woven", tag="diffs2")
         w4_codes = tile([P, N], U32, "w4_codes")
         w4_scales = tile([P, N], U8, "w4_scales")
         z_woven = tile([P, V, PACK], BF16, "z_woven")

@@ -135,10 +135,9 @@ def tile_picked_zpt_mul_p_kernel(tc, x_words, x_scales, w1, w2, w3, w4, offs, ce
             nc.vector.tensor_copy(out=query[t], in_=rows["y", t].indirect(cen_list[:]))
 
         weave_values(0, nc.vector.tensor_copy)
-        query_early = tile([P, 2, V], F32, "query_early", tag="w3_raw0")
-        query = [query_early[:, t, :] for t in range(2)]
+        query_early = tile([P, 1, V], F32, "query_early", tag="w3_raw0")
+        query = [query_early[:, 0, :]]
         gather_query(0)
-        gather_query(1)
         e_single = [tile([P, 1, P, PACK], BF16, "e_single%d" % t)[:] for t in range(2)]
         woven["e", 1] = tile([P, 2, P, PACK], BF16, "e_woven1", tag="y_codes1")[:]
         for t in range(2):
@@ -147,8 +146,9 @@ def tile_picked_zpt_mul_p_kernel(tc, x_words, x_scales, w1, w2, w3, w4, offs, ce
         for t in range(2):
             nc.vector.quantize_mx(out=w_codes["e", 0][:, halves[t]].bitcast(FP8X4), scales=w_scales["e"][:, halves[t]],
                                   in_=e_single[t].rearrange("p t m j -> p (t m j)"))
-        query_late = tile([P, 2, V], F32, "query_late", tag="e_single0")
-        query = query + [query_late[:, t, :] for t in range(2)]
+        query_late = tile([P, 3, V], F32, "query_late", tag="e_single0")
+        query = query + [query_late[:, t, :] for t in range(3)]
+        gather_query(1)
         gather_query(2)
         gather_query(3)
         quantise("e", 1)

@@ -1,10 +1,13 @@
 from contextlib import ExitStack
 
 import concourse.mybir as mybir
+from concourse.masks import make_identity
 
 K, T, S, V, H, N = 512, 2048, 512, 256, 512, 256
 P = 128
 PACK = 4
+LIST_ROWS = 16
+DEAL = 16
 EARLY = 192
 FLOPS = 2 * K * S * H * 3 + 2 * H * N * V
 
@@ -39,7 +42,9 @@ def tile_picked_zpt_mul_p_kernel(tc, x_words, x_scales, w1, w2, w3, w4, offs, ce
         def k_rows(w):
             return w.rearrange("(p j) c -> p j c", j=PACK)
 
-        pairs = [slice(0, 2), slice(2, 4)]
+        tile_pairs = [slice(0, 2), slice(2, 4)]
+        halves = [slice(0, P), slice(P, 2 * P)]
+        last = PACK - 1
 
         scale_table = tile([P, T], U8, "scale_table")
         nc.vector.memset(scale_table[:, : T // 2].bitcast(I32), 0)
@@ -58,7 +63,7 @@ def tile_picked_zpt_mul_p_kernel(tc, x_words, x_scales, w1, w2, w3, w4, offs, ce
         w1_raw = tile([P, PACK, H], F32, "w1_raw")
         nc.sync.dma_start(out=w1_raw[:], in_=k_rows(w1))
         w3_cols = [slice(0, EARLY), slice(EARLY, H)]
-        w3_raw = [tile([P, PACK, cols.stop - cols.start], F32, "w3_raw%d" % half) for half, cols in enumerate(w3_cols)]
+        w3_raw = [tile([P, PACK, cols.stop - cols.start], F32, "w3_raw%d" % piece) for piece, cols in enumerate(w3_cols)]
         nc.sync.dma_start(out=w3_raw[0][:], in_=k_rows(w3)[:, :, w3_cols[0]])
         w2_raw = tile([P, PACK, H], F32, "w2_raw")
         nc.sync.dma_start(out=w2_raw[:], in_=k_rows(w2))
@@ -70,23 +75,28 @@ def tile_picked_zpt_mul_p_kernel(tc, x_words, x_scales, w1, w2, w3, w4, offs, ce
         for t in range(PACK):
             nc.sync.dma_start(out=w4_raw[:, t, :], in_=w4_rows[t])
 
+        identity = tile([P, P], F32, "identity")
+        make_identity(nc, identity[:])
         x_codes = tile([P, S], U32, "x_codes")
         x_bytes = tile([P, S], U8, "x_bytes")
         woven = {("y", pair): tile([P, 2, P, PACK], BF16, "y_woven%d" % pair)[:] for pair in range(2)}
         w_scales = {name: tile([P, H], U8, name + "_scales") for name in "yeh"}
         w_codes = {(name, pair): tile([P, 2 * P], U32, name + "_codes%d" % pair) for name in "yeh" for pair in range(2)}
         rows = {(name, t): tile([P, S], F32, name + "_rows%d" % t)[:] for name in "yeh" for t in range(PACK)}
-        halves = [slice(0, P), slice(P, 2 * P)]
         signs = [1.0, -1.0]
         sums = {}
 
-        def weave(dst, name, ts, js, copy):
-            copy(out=dst.rearrange("p t (m r) j -> p m t j r", r=4)[:, :, :, js, :],
-                 in_=raw[name].rearrange("p j (m t r) -> p m t j r", t=PACK, r=4)[:, :, ts, js, :])
+        def weave(dst, name, tiles, copy):
+            copy(out=dst.rearrange("p t (m r) j -> p m t j r", r=4),
+                 in_=raw[name].rearrange("p j (m t r) -> p m t j r", t=PACK, r=4)[:, :, tiles, :, :])
 
-        def quantise(name, pair):
+        def quantise_pair(name, pair):
             nc.vector.quantize_mx(out=w_codes[name, pair][:].bitcast(FP8X4), scales=w_scales[name][:, 2 * P * pair : 2 * P * (pair + 1)],
                                   in_=woven[name, pair].rearrange("p t m j -> p (t m j)"))
+
+        def quantise_single(name, t, src):
+            nc.vector.quantize_mx(out=w_codes[name, 0][:, halves[t]].bitcast(FP8X4), scales=w_scales[name][:, halves[t]],
+                                  in_=src.rearrange("p t m j -> p (t m j)"))
 
         def multiply(name, t):
             sums[name, t] = bank([P, S], "sums", t + PACK if name == "e" else t)
@@ -99,20 +109,17 @@ def tile_picked_zpt_mul_p_kernel(tc, x_words, x_scales, w1, w2, w3, w4, offs, ce
 
         nc.vector.tensor_copy(out=x_codes[:], in_=word_table[:].bitcast(U32).indirect(offs_list[:]))
         nc.vector.tensor_copy(out=x_bytes[:], in_=scale_table[:].indirect(offs_list[:]))
-        def weave_y(t, copy):
-            weave(woven["y", t // 2][:, t % 2 : t % 2 + 1], "y", slice(t, t + 1), slice(0, PACK), copy)
 
-        def quantise_y(t):
-            nc.vector.quantize_mx(out=w_codes["y", 0][:, halves[t]].bitcast(FP8X4), scales=w_scales["y"][:, halves[t]],
-                                  in_=woven["y", 0][:, t].rearrange("p m j -> p (m j)"))
+        def y_woven(t):
+            return woven["y", t // 2][:, t % 2 : t % 2 + 1]
 
-        weave_y(0, nc.vector.tensor_copy)
-        weave_y(1, nc.scalar.copy)
-        weave_y(3, nc.scalar.copy)
-        quantise_y(0)
-        weave_y(2, nc.vector.tensor_copy)
-        quantise_y(1)
-        quantise("y", 1)
+        weave(y_woven(0), "y", slice(0, 1), nc.vector.tensor_copy)
+        weave(y_woven(1), "y", slice(1, 2), nc.scalar.copy)
+        weave(y_woven(3), "y", slice(3, 4), nc.scalar.copy)
+        quantise_single("y", 0, y_woven(0))
+        weave(y_woven(2), "y", slice(2, 3), nc.vector.tensor_copy)
+        quantise_single("y", 1, y_woven(1))
+        quantise_pair("y", 1)
         for part in range(2):
             cols = slice(part * S // 2, (part + 1) * S // 2)
             half_sums = bank([P, S // 2], "half_sums", PACK * (1 - part))
@@ -124,88 +131,95 @@ def tile_picked_zpt_mul_p_kernel(tc, x_words, x_scales, w1, w2, w3, w4, offs, ce
             empty("y", t)
 
         h_woven = tile([P, PACK, P, PACK], BF16, "h_woven")
-        for half in range(2):
-            woven["h", half] = h_woven[:, pairs[half]]
+        for pair in range(2):
+            woven["h", pair] = h_woven[:, tile_pairs[pair]]
 
-        def weave_values(half, copy):
-            copy(out=h_woven[:].rearrange("p t (m r) j -> p m t j r", r=4)[:, w3_cols[half].start // 16 : w3_cols[half].stop // 16],
-                 in_=w3_raw[half][:].rearrange("p j (m t r) -> p m t j r", t=PACK, r=4))
+        def weave_w3(piece, copy):
+            copy(out=h_woven[:].rearrange("p t (m r) j -> p m t j r", r=4)[:, w3_cols[piece].start // DEAL : w3_cols[piece].stop // DEAL],
+                 in_=w3_raw[piece][:].rearrange("p j (m t r) -> p m t j r", t=PACK, r=4))
 
         def gather_query(t):
             nc.vector.tensor_copy(out=query[t], in_=rows["y", t].indirect(cen_list[:]))
 
-        weave_values(0, nc.vector.tensor_copy)
-        query_early = tile([P, 1, V], F32, "query_early", tag="w3_raw0")
-        query = [query_early[:, 0, :]]
+        weave_w3(0, nc.vector.tensor_copy)
+        query_first = tile([P, 1, V], F32, "query_first", tag="w3_raw0")
+        query = [query_first[:, 0, :]]
         gather_query(0)
         e_single = [tile([P, 1, P, PACK], BF16, "e_single%d" % t)[:] for t in range(2)]
         woven["e", 1] = tile([P, 2, P, PACK], BF16, "e_woven1", tag="y_codes1")[:]
         for t in range(2):
-            weave(e_single[t], "e", slice(t, t + 1), slice(0, PACK), nc.vector.tensor_copy)
-        weave(woven["e", 1], "e", pairs[1], slice(0, PACK), nc.scalar.copy)
+            weave(e_single[t], "e", slice(t, t + 1), nc.vector.tensor_copy)
+        weave(woven["e", 1], "e", tile_pairs[1], nc.scalar.copy)
         for t in range(2):
-            nc.vector.quantize_mx(out=w_codes["e", 0][:, halves[t]].bitcast(FP8X4), scales=w_scales["e"][:, halves[t]],
-                                  in_=e_single[t].rearrange("p t m j -> p (t m j)"))
-        query_late = tile([P, 3, V], F32, "query_late", tag="e_single0")
-        query = query + [query_late[:, t, :] for t in range(3)]
-        gather_query(1)
-        gather_query(2)
-        gather_query(3)
-        quantise("e", 1)
+            quantise_single("e", t, e_single[t])
+        query_rest = tile([P, last, V], F32, "query_rest", tag="e_single0")
+        query = query + [query_rest[:, t, :] for t in range(last)]
+        for t in range(1, PACK):
+            gather_query(t)
+        quantise_pair("e", 1)
+
         prod = [tile([P, 2, V], F32, "prod%d" % t, tag="w2_raw" if t == 0 else None) for t in range(PACK)]
         tanhs = [tile([P, 2, V], F32, "tanhs%d" % t) for t in range(PACK)]
-        diffs = [tile([P, V], F32, "diffs%d" % t) for t in range(PACK)]
+        diffs = [tile([P, V], F32, "diffs%d" % t)[:] for t in range(last)]
         gates = [tile([P, 2, V], F32, "gates%d" % t) for t in range(PACK)]
         parts = [tile([P, PACK, V], F32, "parts%d" % side) for side in range(2)]
-
-        def gather_keys(t):
-            for side in range(2):
-                nc.vector.tensor_tensor(prod[t][:, side, :], rows["e", t].indirect(pos_lists[side][:]), query[t], ALU.mult)
-
-        def tanh(t):
-            nc.scalar.activation(tanhs[t][:], prod[t][:], ACT.Tanh)
-
-        def difference(t):
-            nc.vector.tensor_tensor(diffs[t][:], tanhs[t][:, 0, :], tanhs[t][:, 1, :], ALU.subtract)
-
-        def sigmoid(t):
-            for side in range(2):
-                nc.scalar.activation(gates[t][:, side, :], diffs[t][:], ACT.Sigmoid, scale=signs[side])
-
-        def gather_values(t, v0, v1):
-            for side in range(2):
-                nc.vector.tensor_tensor(parts[side][:, t, v0:v1], rows["h", t].indirect(pos_lists[side][:, v0 // 16 : v1 // 16]),
-                                        gates[t][:, side, v0:v1], ALU.mult)
-
-        def values(pair):
-            quantise("h", pair)
-            multiply("h", 2 * pair)
-            multiply("h", 2 * pair + 1)
 
         def keys(t):
             multiply("e", t)
             empty("e", t)
-            gather_keys(t)
+            for side in range(2):
+                nc.vector.tensor_tensor(prod[t][:, side, :], rows["e", t].indirect(pos_lists[side][:]), query[t], ALU.mult)
 
         def scores(t):
-            tanh(t)
-            difference(t)
+            nc.scalar.activation(tanhs[t][:], prod[t][:], ACT.Tanh)
+            nc.vector.tensor_tensor(diffs[t], tanhs[t][:, 0, :], tanhs[t][:, 1, :], ALU.subtract)
+
+        def scores_turned(t):
+            turned = bank([P, 2, V], "turned", PACK + t)
+            for side in range(2):
+                for cols in halves:
+                    nc.tensor.transpose(turned[:, side, cols], prod[t][:, side, cols], identity[:])
+            for side in range(2):
+                nc.scalar.activation(tanhs[t][:, side, :], turned[:, side, :], ACT.Tanh, scale=signs[side])
+            turned_back = bank([P, V], "turned_back", PACK + t)
+            for cols in halves:
+                for side in range(2):
+                    nc.tensor.matmul(turned_back[:, cols], lhsT=tanhs[t][:, side, cols], rhs=identity[:], is_transpose=True,
+                                     start=side == 0, stop=side == 1)
+            diffs.append(turned_back[:])
+
+        def sigmoid(t):
+            for side in range(2):
+                nc.scalar.activation(gates[t][:, side, :], diffs[t], ACT.Sigmoid, scale=signs[side])
+
+        def gather_values(t, cols):
+            for side in range(2):
+                entries = pos_lists[side][:, cols.start // LIST_ROWS : cols.stop // LIST_ROWS]
+                nc.vector.tensor_tensor(parts[side][:, t, cols], rows["h", t].indirect(entries), gates[t][:, side, cols], ALU.mult)
+
+        def values(pair):
+            quantise_pair("h", pair)
+            multiply("h", 2 * pair)
+            multiply("h", 2 * pair + 1)
 
         keys(0)
         keys(1)
-        weave_values(1, nc.scalar.copy)
+        weave_w3(1, nc.scalar.copy)
         values(0)
         keys(2)
         scores(0)
         keys(3)
         values(1)
-        for t in range(PACK):
-            if t < PACK - 1:
+        for t in range(last):
+            if t + 1 < last:
                 scores(t + 1)
+            else:
+                scores_turned(last)
             empty("h", t)
             sigmoid(t)
-            if t < PACK - 1:
-                gather_values(t, 0, V)
+            gather_values(t, slice(0, V))
+        empty("h", last)
+        sigmoid(last)
 
         w4_woven = tile([P, N, PACK], BF16, "w4_woven", tag="diffs2")
         w4_codes = tile([P, N], U32, "w4_codes")
@@ -216,7 +230,7 @@ def tile_picked_zpt_mul_p_kernel(tc, x_words, x_scales, w1, w2, w3, w4, offs, ce
         nc.scalar.copy(out=w4_woven[:].rearrange("p (c i) t -> p c t i", i=4), in_=w4_raw.rearrange("p t (c i) -> p c t i", i=4))
         nc.vector.quantize_mx(out=w4_codes[:].bitcast(FP8X4), scales=w4_scales[:], in_=w4_woven[:].rearrange("p m t -> p (m t)"))
         for half, cols in enumerate(halves):
-            gather_values(PACK - 1, cols.start, cols.stop)
+            gather_values(last, cols)
             nc.vector.tensor_tensor(z_woven[:, cols, :].rearrange("p (c i) t -> p c t i", i=4),
                                     parts[0][:, :, cols].rearrange("p t (c i) -> p c t i", i=4),
                                     parts[1][:, :, cols].rearrange("p t (c i) -> p c t i", i=4), ALU.add)

@@ -56,7 +56,6 @@ def tile_picked_zpt_mul_p_kernel(tc, x_words, x_scales, w1, w2, w3, w4, offs, ce
         word_table = tile([P, T], I32, "word_table")
         nc.sync.dma_start(out=word_table[:], in_=x_words[0].rearrange("p n j -> p (n j)").bitcast(I32))
         offs_list = load_list(offs, "offs_list")
-        cen_list = load_list(cen, "cen_list")
         scale_rows = x_scales[0].rearrange("(q r) c -> r q c", r=4)
         for r in range(4):
             nc.sync.dma_start(out=scale_table[r:P:32, :].bitcast(I32), in_=scale_rows[r].bitcast(I32))
@@ -65,6 +64,7 @@ def tile_picked_zpt_mul_p_kernel(tc, x_words, x_scales, w1, w2, w3, w4, offs, ce
         w3_cols = [slice(0, EARLY), slice(EARLY, H)]
         w3_raw = [tile([P, PACK, cols.stop - cols.start], F32, "w3_raw%d" % piece) for piece, cols in enumerate(w3_cols)]
         nc.sync.dma_start(out=w3_raw[0][:], in_=k_rows(w3)[:, :, w3_cols[0]])
+        cen_list = load_list(cen, "cen_list")
         w2_raw = tile([P, PACK, H], F32, "w2_raw")
         nc.sync.dma_start(out=w2_raw[:], in_=k_rows(w2))
         nc.sync.dma_start(out=w3_raw[1][:], in_=k_rows(w3)[:, :, w3_cols[1]])
@@ -81,8 +81,9 @@ def tile_picked_zpt_mul_p_kernel(tc, x_words, x_scales, w1, w2, w3, w4, offs, ce
         x_bytes = tile([P, S], U8, "x_bytes")
         woven = {("y", pair): tile([P, 2, P, PACK], BF16, "y_woven%d" % pair)[:] for pair in range(2)}
         w_scales = {name: tile([P, H], U8, name + "_scales") for name in "yeh"}
-        w_codes = {(name, pair): tile([P, 2 * P], U32, name + "_codes%d" % pair) for name in "yeh" for pair in range(2)}
+        w_codes = {(name, pair): tile([P, 2 * P], U32, name + "_codes%d" % pair) for name in "yeh" for pair in range(2) if (name, pair) != ("e", 0)}
         rows = {(name, t): tile([P, S], F32, name + "_rows%d" % t)[:] for name in "yeh" for t in range(PACK)}
+        e_first_codes = [tile([P, P], U32, "e_first_codes%d" % t) for t in range(2)]
         signs = [1.0, -1.0]
         sums = {}
 
@@ -94,13 +95,16 @@ def tile_picked_zpt_mul_p_kernel(tc, x_words, x_scales, w1, w2, w3, w4, offs, ce
             nc.vector.quantize_mx(out=w_codes[name, pair][:].bitcast(FP8X4), scales=w_scales[name][:, 2 * P * pair : 2 * P * (pair + 1)],
                                   in_=woven[name, pair].rearrange("p t m j -> p (t m j)"))
 
+        def codes_of(name, t):
+            return e_first_codes[t][:] if name == "e" and t < 2 else w_codes[name, t // 2][:, halves[t % 2]]
+
         def quantise_single(name, t, src):
-            nc.vector.quantize_mx(out=w_codes[name, 0][:, halves[t]].bitcast(FP8X4), scales=w_scales[name][:, halves[t]],
+            nc.vector.quantize_mx(out=codes_of(name, t).bitcast(FP8X4), scales=w_scales[name][:, halves[t]],
                                   in_=src.rearrange("p t m j -> p (t m j)"))
 
         def multiply(name, t):
             sums[name, t] = bank([P, S], "sums", t + PACK if name == "e" else t)
-            nc.tensor.matmul_mx(out=sums[name, t][:], lhsT=w_codes[name, t // 2][:, halves[t % 2]].bitcast(FP8X4),
+            nc.tensor.matmul_mx(out=sums[name, t][:], lhsT=codes_of(name, t).bitcast(FP8X4),
                                 lhsT_scale=w_scales[name][:, P * t : P * t + P],
                                 rhs=x_codes[:].bitcast(FP8X4), rhs_scale=x_bytes[:], start=True, stop=True)
 
@@ -146,35 +150,35 @@ def tile_picked_zpt_mul_p_kernel(tc, x_words, x_scales, w1, w2, w3, w4, offs, ce
         query = [query_first[:, 0, :]]
         gather_query(0)
         e_single = [tile([P, 1, P, PACK], BF16, "e_single%d" % t)[:] for t in range(2)]
-        woven["e", 1] = tile([P, 2, P, PACK], BF16, "e_woven1", tag="y_codes1")[:]
+        woven["e", 1] = tile([P, 2, P, PACK], BF16, "e_woven1")[:]
         for t in range(2):
             weave(e_single[t], "e", slice(t, t + 1), nc.vector.tensor_copy)
-        weave(woven["e", 1], "e", tile_pairs[1], nc.scalar.copy)
-        for t in range(2):
-            quantise_single("e", t, e_single[t])
-        query_rest = tile([P, last, V], F32, "query_rest", tag="e_single0")
-        query = query + [query_rest[:, t, :] for t in range(last)]
-        for t in range(1, PACK):
-            gather_query(t)
+        quantise_single("e", 0, e_single[0])
+        weave(woven["e", 1], "e", tile_pairs[1], nc.vector.tensor_copy)
+        quantise_single("e", 1, e_single[1])
         quantise_pair("e", 1)
 
-        prod = [tile([P, 2, V], F32, "prod%d" % t, tag="w2_raw" if t == 0 else None) for t in range(PACK)]
-        tanhs = [tile([P, 2, V], F32, "tanhs%d" % t) for t in range(PACK)]
-        diffs = [tile([P, V], F32, "diffs%d" % t)[:] for t in range(last)]
+        def scalar_query(t, tag):
+            query.append(tile([P, V], F32, "query%d" % t, tag=tag)[:])
+            nc.scalar.activation(query[t], rows["y", t].indirect(cen_list[:]), ACT.Copy)
+
+        scalar_query(1, None)
+
+        prod = {}
+        prod_tags = ["w2_raw", "w3_raw1", "h_woven", None]
+        tanhs, turned_diffs, bank_gates = {}, {}, {}
+        tanh_tags = ["h_codes0", "h_codes1", None, None]
+        diffs = {}
         gates = [tile([P, 2, V], F32, "gates%d" % t) for t in range(PACK)]
         parts = [tile([P, PACK, V], F32, "parts%d" % side) for side in range(2)]
 
         def keys(t):
-            multiply("e", t)
-            empty("e", t)
+            prod[t] = tile([P, 2, V], F32, "prod%d" % t, tag=prod_tags[t])
             for side in range(2):
                 nc.vector.tensor_tensor(prod[t][:, side, :], rows["e", t].indirect(pos_lists[side][:]), query[t], ALU.mult)
 
-        def scores(t):
-            nc.scalar.activation(tanhs[t][:], prod[t][:], ACT.Tanh)
-            nc.vector.tensor_tensor(diffs[t], tanhs[t][:, 0, :], tanhs[t][:, 1, :], ALU.subtract)
-
         def scores_turned(t):
+            tanhs[t] = tile([P, 2, V], F32, "tanhs%d" % t)
             turned = bank([P, 2, V], "turned", PACK + t)
             for side in range(2):
                 for cols in halves:
@@ -186,56 +190,104 @@ def tile_picked_zpt_mul_p_kernel(tc, x_words, x_scales, w1, w2, w3, w4, offs, ce
                 for side in range(2):
                     nc.tensor.matmul(turned_back[:, cols], lhsT=tanhs[t][:, side, cols], rhs=identity[:], is_transpose=True,
                                      start=side == 0, stop=side == 1)
-            diffs.append(turned_back[:])
+            diffs[t] = turned_back[:]
 
-        def sigmoid(t):
-            for side in range(2):
-                nc.scalar.activation(gates[t][:, side, :], diffs[t], ACT.Sigmoid, scale=signs[side])
+        def first_gate(t):
+            nc.scalar.activation(gates[t][:, 0, :], diffs[t], ACT.Sigmoid)
 
-        def gather_values(t, cols):
+        def vector_second(t):
+            nc.vector.tensor_copy(out=parts[1][:, t, :], in_=rows["h", t].indirect(pos_lists[1][:]))
+
+        def entries(side, cols):
+            return pos_lists[side][:, cols.start // LIST_ROWS : cols.stop // LIST_ROWS]
+
+        def second_values(t, cols=slice(0, V)):
+            nc.scalar.activation(parts[1][:, t, cols], rows["h", t].indirect(entries(1, cols)), ACT.Copy)
+
+        def spread_values(t, cols=slice(0, V)):
+            nc.vector.tensor_tensor(gates[t][:, 1, cols], rows["h", t].indirect(entries(0, cols)), parts[1][:, t, cols], ALU.subtract)
+
+        def weigh(t):
+            nc.vector.tensor_tensor(parts[0][:, t, :], gates[t][:, 1, :], bank_gates[t][:] if t in bank_gates else gates[t][:, 0, :], ALU.mult)
+
+        def scores_added(t):
+            tanhs[t] = tile([P, 2, V], F32, "tanhs%d" % t, tag=tanh_tags[t])
             for side in range(2):
-                entries = pos_lists[side][:, cols.start // LIST_ROWS : cols.stop // LIST_ROWS]
-                nc.vector.tensor_tensor(parts[side][:, t, cols], rows["h", t].indirect(entries), gates[t][:, side, cols], ALU.mult)
+                nc.scalar.activation(tanhs[t][:, side, :], prod[t][:, side, :], ACT.Tanh, scale=signs[side])
+            turned_diffs[t] = bank([P, 2, P], "turned_diffs", PACK + t)
+            for half, cols in enumerate(halves):
+                for side in range(2):
+                    nc.tensor.matmul(turned_diffs[t][:, half, :], lhsT=tanhs[t][:, side, cols], rhs=identity[:], is_transpose=True,
+                                     start=side == 0, stop=side == 1)
+
+        def turned_gate(t):
+            turned = tile([P, 2, P], F32, "turned_gate%d" % t)
+            nc.scalar.activation(turned[:], turned_diffs[t][:], ACT.Sigmoid)
+            bank_gates[t] = bank([P, V], "bank_gates", t)
+            for half, cols in enumerate(halves):
+                nc.tensor.transpose(bank_gates[t][:, cols], turned[:, half, :], identity[:])
 
         def values(pair):
             quantise_pair("h", pair)
             multiply("h", 2 * pair)
             multiply("h", 2 * pair + 1)
 
+        for t in range(PACK):
+            multiply("e", t)
+        empty("e", 0)
+        scalar_query(2, "e_first_codes0")
         keys(0)
-        keys(1)
-        weave_w3(1, nc.scalar.copy)
+        empty("e", 1)
+        scalar_query(3, "e_first_codes1")
+        weave_w3(1, nc.vector.tensor_copy)
         values(0)
-        keys(2)
-        scores(0)
-        keys(3)
         values(1)
-        for t in range(last):
-            if t + 1 < last:
-                scores(t + 1)
-            else:
-                scores_turned(last)
-            empty("h", t)
-            sigmoid(t)
-            gather_values(t, slice(0, V))
+        keys(1)
+        empty("e", 2)
+        empty("e", 3)
+        keys(2)
+        scores_added(0)
+        keys(3)
+        empty("h", 0)
+        second_values(0)
+        scores_added(1)
+        empty("h", 1)
+        turned_gate(0)
+        spread_values(0)
+        second_values(1)
+        scores_turned(2)
+        weigh(0)
+        empty("h", 2)
+        spread_values(1)
+        turned_gate(1)
+        vector_second(2)
         empty("h", last)
-        sigmoid(last)
+        scores_turned(last)
+        weigh(1)
+        spread_values(2)
+        second_values(last)
+        first_gate(2)
+        first_gate(last)
+        spread_values(last)
+        weigh(2)
+        for cols in halves:
+            nc.vector.tensor_tensor(parts[0][:, last, cols], gates[last][:, 1, cols], gates[last][:, 0, cols], ALU.mult)
 
-        w4_woven = tile([P, N, PACK], BF16, "w4_woven", tag="diffs2")
+        w4_woven = tile([P, N, PACK], BF16, "w4_woven", tag="tanhs3")
         w4_codes = tile([P, N], U32, "w4_codes")
         w4_scales = tile([P, N], U8, "w4_scales")
-        z_woven = tile([P, V, PACK], BF16, "z_woven")
         z_codes = tile([P, V], U32, "z_codes")
         z_scales = tile([P, V], U8, "z_scales")
         nc.scalar.copy(out=w4_woven[:].rearrange("p (c i) t -> p c t i", i=4), in_=w4_raw.rearrange("p t (c i) -> p c t i", i=4))
-        nc.vector.quantize_mx(out=w4_codes[:].bitcast(FP8X4), scales=w4_scales[:], in_=w4_woven[:].rearrange("p m t -> p (m t)"))
         for half, cols in enumerate(halves):
-            gather_values(last, cols)
-            nc.vector.tensor_tensor(z_woven[:, cols, :].rearrange("p (c i) t -> p c t i", i=4),
+            z_woven = tile([P, P, PACK], BF16, "z_woven%d" % half, tag="tanhs3" if half == 1 else None)
+            nc.vector.tensor_tensor(z_woven[:].rearrange("p (c i) t -> p c t i", i=4),
                                     parts[0][:, :, cols].rearrange("p t (c i) -> p c t i", i=4),
                                     parts[1][:, :, cols].rearrange("p t (c i) -> p c t i", i=4), ALU.add)
+            if half == 0:
+                nc.vector.quantize_mx(out=w4_codes[:].bitcast(FP8X4), scales=w4_scales[:], in_=w4_woven[:].rearrange("p m t -> p (m t)"))
             nc.vector.quantize_mx(out=z_codes[:, cols].bitcast(FP8X4), scales=z_scales[:, cols],
-                                  in_=z_woven[:, cols, :].rearrange("p v t -> p (v t)"))
+                                  in_=z_woven[:].rearrange("p v t -> p (v t)"))
             for block, out_rows in enumerate(halves):
                 result = bank([P, P], "result", PACK + 2 * half + block)
                 nc.tensor.matmul_mx(out=result[:], lhsT=w4_codes[:, out_rows].bitcast(FP8X4), lhsT_scale=w4_scales[:, out_rows],

@@ -138,14 +138,14 @@ def tile_picked_zpt_mul_p_kernel(tc, x_words, x_scales, w1, w2, w3, w4, offs, ce
         for pair in range(2):
             woven["h", pair] = h_woven[:, tile_pairs[pair]]
 
-        def weave_w3(piece, copy):
-            copy(out=h_woven[:].rearrange("p t (m r) j -> p m t j r", r=4)[:, w3_cols[piece].start // DEAL : w3_cols[piece].stop // DEAL],
-                 in_=w3_raw[piece][:].rearrange("p j (m t r) -> p m t j r", t=PACK, r=4))
+        def weave_w3(piece, tiles, copy):
+            copy(out=h_woven[:].rearrange("p t (m r) j -> p m t j r", r=4)[:, w3_cols[piece].start // DEAL : w3_cols[piece].stop // DEAL, tiles],
+                 in_=w3_raw[piece][:].rearrange("p j (m t r) -> p m t j r", t=PACK, r=4)[:, :, tiles])
 
         def gather_query(t):
             nc.vector.tensor_copy(out=query[t], in_=rows["y", t].indirect(cen_list[:]))
 
-        weave_w3(0, nc.vector.tensor_copy)
+        weave_w3(0, slice(0, PACK), nc.vector.tensor_copy)
         query_first = tile([P, 1, V], F32, "query_first", tag="w3_raw0")
         query = [query_first[:, 0, :]]
         gather_query(0)
@@ -165,7 +165,7 @@ def tile_picked_zpt_mul_p_kernel(tc, x_words, x_scales, w1, w2, w3, w4, offs, ce
         scalar_query(1, None)
 
         prod = {}
-        prod_tags = ["w2_raw", "w3_raw1", "h_woven", None]
+        prod_tags = ["w3_raw1", "h_woven", None, None]
         tanhs, turned_diffs, bank_gates = {}, {}, {}
         tanh_tags = ["h_codes0", "h_codes1", None, None]
         diffs = {}
@@ -234,14 +234,15 @@ def tile_picked_zpt_mul_p_kernel(tc, x_words, x_scales, w1, w2, w3, w4, offs, ce
 
         for t in range(PACK):
             multiply("e", t)
+        scalar_query(2, None)
         empty("e", 0)
-        scalar_query(2, "e_first_codes0")
+        for pair in range(2):
+            weave_w3(1, tile_pairs[pair], nc.vector.tensor_copy)
+        values(0)
+        values(1)
         keys(0)
         empty("e", 1)
         scalar_query(3, "e_first_codes1")
-        weave_w3(1, nc.vector.tensor_copy)
-        values(0)
-        values(1)
         keys(1)
         empty("e", 2)
         empty("e", 3)

@@ -275,26 +275,31 @@ def tile_picked_zpt_mul_p_kernel(tc, x_words, x_scales, w1, w2, w3, w4, offs, ce
             nc.vector.tensor_tensor(parts[0][:, last, cols], gates[last][:, 1, cols], gates[last][:, 0, cols], ALU.mult)
 
         w4_woven = tile([P, N, PACK], BF16, "w4_woven", tag="tanhs3")
-        w4_codes = tile([P, N], U32, "w4_codes")
+        w4_codes = tile([P, N], U32, "w4_codes", tag="gates3")
         w4_scales = tile([P, N], U8, "w4_scales")
         z_codes = tile([P, V], U32, "z_codes")
         z_scales = tile([P, V], U8, "z_scales")
         nc.scalar.copy(out=w4_woven[:].rearrange("p (c i) t -> p c t i", i=4), in_=w4_raw.rearrange("p t (c i) -> p c t i", i=4))
-        for half, cols in enumerate(halves):
-            z_woven = tile([P, P, PACK], BF16, "z_woven%d" % half, tag="tanhs3" if half == 1 else None)
-            nc.vector.tensor_tensor(z_woven[:].rearrange("p (c i) t -> p c t i", i=4),
+        z_woven = tile([P, V, PACK], BF16, "z_woven")
+        for cols in halves:
+            nc.vector.tensor_tensor(z_woven[:, cols, :].rearrange("p (c i) t -> p c t i", i=4),
                                     parts[0][:, :, cols].rearrange("p t (c i) -> p c t i", i=4),
                                     parts[1][:, :, cols].rearrange("p t (c i) -> p c t i", i=4), ALU.add)
-            if half == 0:
-                nc.vector.quantize_mx(out=w4_codes[:].bitcast(FP8X4), scales=w4_scales[:], in_=w4_woven[:].rearrange("p m t -> p (m t)"))
+
+        def quantise_z(cols):
             nc.vector.quantize_mx(out=z_codes[:, cols].bitcast(FP8X4), scales=z_scales[:, cols],
-                                  in_=z_woven[:].rearrange("p v t -> p (v t)"))
+                                  in_=z_woven[:, cols, :].rearrange("p v t -> p (v t)"))
+
+        quantise_z(halves[0])
+        nc.vector.quantize_mx(out=w4_codes[:].bitcast(FP8X4), scales=w4_scales[:], in_=w4_woven[:].rearrange("p m t -> p (m t)"))
+        quantise_z(halves[1])
+        for half, cols in enumerate(halves):
             for block, out_rows in enumerate(halves):
                 result = bank([P, P], "result", PACK + 2 * half + block)
                 nc.tensor.matmul_mx(out=result[:], lhsT=w4_codes[:, out_rows].bitcast(FP8X4), lhsT_scale=w4_scales[:, out_rows],
                                     rhs=z_codes[:, cols].bitcast(FP8X4), rhs_scale=z_scales[:, cols], start=True, stop=True)
                 staged = tile([P, P], F32, "staged%d%d" % (half, block))
-                if (half, block) == (1, 1):
+                if block == 1:
                     nc.vector.tensor_copy(out=staged[:], in_=result[:])
                 else:
                     nc.scalar.copy(out=staged[:], in_=result[:])

@@ -178,7 +178,7 @@ def tile_picked_zpt_mul_p_kernel(tc, x_words, x_scales, w1, w2, w3, w4, offs, ce
                 nc.vector.tensor_tensor(prod[t][:, side, :], rows["e", t].indirect(pos_lists[side][:]), query[t], ALU.mult)
 
         def scores_turned(t):
-            tanhs[t] = tile([P, 2, V], F32, "tanhs%d" % t)
+            tanhs[t] = tile([P, 2, V], F32, "tanhs%d" % t, tag=tanh_tags[t])
             turned = bank([P, 2, V], "turned", PACK + t)
             for side in range(2):
                 for cols in halves:
@@ -251,7 +251,7 @@ def tile_picked_zpt_mul_p_kernel(tc, x_words, x_scales, w1, w2, w3, w4, offs, ce
         keys(3)
         empty("h", 0)
         second_values(0)
-        scores_added(1)
+        scores_turned(1)
         empty("h", 1)
         turned_gate(0)
         spread_values(0)
@@ -260,16 +260,16 @@ def tile_picked_zpt_mul_p_kernel(tc, x_words, x_scales, w1, w2, w3, w4, offs, ce
         weigh(0)
         empty("h", 2)
         spread_values(1)
-        turned_gate(1)
         vector_second(2)
         empty("h", last)
         scores_turned(last)
-        weigh(1)
         spread_values(2)
         second_values(last)
+        first_gate(1)
         first_gate(2)
         first_gate(last)
         spread_values(last)
+        weigh(1)
         weigh(2)
         for cols in halves:
             nc.vector.tensor_tensor(parts[0][:, last, cols], gates[last][:, 1, cols], gates[last][:, 0, cols], ALU.mult)

@@ -251,16 +251,16 @@ def tile_picked_zpt_mul_p_kernel(tc, x_words, x_scales, w1, w2, w3, w4, offs, ce
         keys(3)
         empty("h", 0)
         second_values(0)
-        scores_turned(1)
         empty("h", 1)
+        scores_turned(1)
         turned_gate(0)
         spread_values(0)
         second_values(1)
-        scores_turned(2)
-        weigh(0)
         empty("h", 2)
         spread_values(1)
+        scores_turned(2)
         vector_second(2)
+        weigh(0)
         empty("h", last)
         scores_turned(last)
         spread_values(2)

@@ -7,8 +7,6 @@ K, T, S, V, H, N = 512, 2048, 512, 256, 512, 256
 P = 128
 PACK = 4
 LIST_ROWS = 16
-DEAL = 16
-EARLY = 192
 FLOPS = 2 * K * S * H * 3 + 2 * H * N * V
 
 F32 = mybir.dt.float32
@@ -26,10 +24,14 @@ def tile_picked_zpt_mul_p_kernel(tc, x_words, x_scales, w1, w2, w3, w4, offs, ce
     nc = tc.nc
     with ExitStack() as ctx:
         sb = ctx.enter_context(tc.tile_pool(name="sb", bufs=1))
+        laid = ctx.enter_context(tc.tile_pool(name="laid", bufs=1))
         ps = ctx.enter_context(tc.psum_pool(name="ps", bufs=1))
 
         def tile(shape, dtype, name, tag=None):
             return sb.tile(shape, dtype, name=name, tag=tag or name, align_bytes=64)
+
+        def placed(shape, dtype, name, offset):
+            return laid.tile(shape, dtype, name=name, offset=offset, align_bytes=64)
 
         def bank(shape, name, number):
             return ps.tile(shape, F32, name=name, tag="bank%d" % number)
@@ -39,11 +41,13 @@ def tile_picked_zpt_mul_p_kernel(tc, x_words, x_scales, w1, w2, w3, w4, offs, ce
             nc.sync.dma_start(lst[:], src)
             return lst
 
-        def k_rows(w):
-            return w.rearrange("(p j) c -> p j c", j=PACK)
+        def load_weight(w, name, cols=slice(0, H)):
+            raw_tile = tile([P, PACK, cols.stop - cols.start], F32, name)
+            nc.sync.dma_start(out=raw_tile[:], in_=w.rearrange("(p j) c -> p j c", j=PACK)[:, :, cols])
+            return raw_tile[:]
 
-        tile_pairs = [slice(0, 2), slice(2, 4)]
         halves = [slice(0, P), slice(P, 2 * P)]
+        point_halves = [slice(0, S // 2), slice(S // 2, S)]
         last = PACK - 1
 
         scale_table = tile([P, T], U8, "scale_table")
@@ -59,17 +63,11 @@ def tile_picked_zpt_mul_p_kernel(tc, x_words, x_scales, w1, w2, w3, w4, offs, ce
         scale_rows = x_scales[0].rearrange("(q r) c -> r q c", r=4)
         for r in range(4):
             nc.sync.dma_start(out=scale_table[r:P:32, :].bitcast(I32), in_=scale_rows[r].bitcast(I32))
-        w1_raw = tile([P, PACK, H], F32, "w1_raw")
-        nc.sync.dma_start(out=w1_raw[:], in_=k_rows(w1))
-        w3_cols = [slice(0, EARLY), slice(EARLY, H)]
-        w3_raw = [tile([P, PACK, cols.stop - cols.start], F32, "w3_raw%d" % piece) for piece, cols in enumerate(w3_cols)]
-        nc.sync.dma_start(out=w3_raw[0][:], in_=k_rows(w3)[:, :, w3_cols[0]])
+        raw = {"y": load_weight(w1, "w1_raw")}
         cen_list = load_list(cen, "cen_list")
-        w2_raw = tile([P, PACK, H], F32, "w2_raw")
-        nc.sync.dma_start(out=w2_raw[:], in_=k_rows(w2))
-        nc.sync.dma_start(out=w3_raw[1][:], in_=k_rows(w3)[:, :, w3_cols[1]])
+        raw["e"] = load_weight(w2, "w2_raw")
+        raw["h"] = load_weight(w3, "w3_raw")
         pos_lists = [load_list(pos1, "pos1_list"), load_list(pos2, "pos2_list")]
-        raw = {"y": w1_raw[:], "e": w2_raw[:]}
         w4_raw = tile([P, PACK, N], F32, "w4_raw")[:]
         w4_rows = w4.rearrange("(m t r) n -> t m r n", t=PACK, r=4)
         for t in range(PACK):
@@ -79,200 +77,208 @@ def tile_picked_zpt_mul_p_kernel(tc, x_words, x_scales, w1, w2, w3, w4, offs, ce
         make_identity(nc, identity[:])
         x_codes = tile([P, S], U32, "x_codes")
         x_bytes = tile([P, S], U8, "x_bytes")
-        woven = {("y", pair): tile([P, 2, P, PACK], BF16, "y_woven%d" % pair)[:] for pair in range(2)}
         w_scales = {name: tile([P, H], U8, name + "_scales") for name in "yeh"}
-        w_codes = {(name, pair): tile([P, 2 * P], U32, name + "_codes%d" % pair) for name in "yeh" for pair in range(2) if (name, pair) != ("e", 0)}
-        rows = {(name, t): tile([P, S], F32, name + "_rows%d" % t)[:] for name in "yeh" for t in range(PACK)}
-        e_first_codes = [tile([P, P], U32, "e_first_codes%d" % t) for t in range(2)]
+        woven, codes, rows, sums, query = {}, {}, {}, {}, {}
         signs = [1.0, -1.0]
-        sums = {}
+        on_vector, on_scalar = nc.vector.tensor_copy, nc.scalar.copy
 
-        def weave(dst, name, tiles, copy):
+        def weave(dst, src, first, stop, copy):
             copy(out=dst.rearrange("p t (m r) j -> p m t j r", r=4),
-                 in_=raw[name].rearrange("p j (m t r) -> p m t j r", t=PACK, r=4)[:, :, tiles, :, :])
+                 in_=raw[src].rearrange("p j (m t r) -> p m t j r", t=PACK, r=4)[:, :, first:stop])
 
-        def quantise_pair(name, pair):
-            nc.vector.quantize_mx(out=w_codes[name, pair][:].bitcast(FP8X4), scales=w_scales[name][:, 2 * P * pair : 2 * P * (pair + 1)],
-                                  in_=woven[name, pair].rearrange("p t m j -> p (t m j)"))
-
-        def codes_of(name, t):
-            return e_first_codes[t][:] if name == "e" and t < 2 else w_codes[name, t // 2][:, halves[t % 2]]
-
-        def quantise_single(name, t, src):
-            nc.vector.quantize_mx(out=codes_of(name, t).bitcast(FP8X4), scales=w_scales[name][:, halves[t]],
+        def quantise(name, first, stop, src, tag=None):
+            made = tile([P, P * (stop - first)], U32, name + "_codes%d" % first, tag=tag)
+            nc.vector.quantize_mx(out=made[:].bitcast(FP8X4), scales=w_scales[name][:, P * first : P * stop],
                                   in_=src.rearrange("p t m j -> p (t m j)"))
+            for t in range(first, stop):
+                codes[name, t] = made[:, P * (t - first) : P * (t - first + 1)]
 
-        def multiply(name, t):
-            sums[name, t] = bank([P, S], "sums", t + PACK if name == "e" else t)
-            nc.tensor.matmul_mx(out=sums[name, t][:], lhsT=codes_of(name, t).bitcast(FP8X4),
+        def multiply(name, t, number, cols=slice(0, S)):
+            sums[name, t, cols.start] = bank([P, cols.stop - cols.start], "sums", number)
+            nc.tensor.matmul_mx(out=sums[name, t, cols.start][:], lhsT=codes[name, t].bitcast(FP8X4),
                                 lhsT_scale=w_scales[name][:, P * t : P * t + P],
-                                rhs=x_codes[:].bitcast(FP8X4), rhs_scale=x_bytes[:], start=True, stop=True)
+                                rhs=x_codes[:, cols].bitcast(FP8X4), rhs_scale=x_bytes[:, cols], start=True, stop=True)
 
-        def empty(name, t):
-            nc.scalar.copy(out=rows[name, t], in_=sums[name, t][:])
+        def empty(name, t, cols=slice(0, S), copy=nc.scalar.copy, tag=None):
+            if (name, t) not in rows:
+                rows[name, t] = tile([P, S], F32, name + "_rows%d" % t, tag=tag)[:]
+            copy(out=rows[name, t][:, cols], in_=sums[name, t, cols.start][:])
+
+        def scalar_gather(dst, window, lst):
+            nc.scalar.activation(dst, window.indirect(lst), ACT.Copy)
+
+        def vector_gather(dst, window, lst):
+            nc.vector.tensor_copy(out=dst, in_=window.indirect(lst))
+
+        def gather_query(t, gather, tag=None):
+            query[t] = tile([P, V], F32, "query%d" % t, tag=tag)[:]
+            gather(query[t], rows["y", t], cen_list[:])
+
+        groups = [(0, 1), (2, 3)]
+        group_of = {t: (group, t - group[0]) for group in groups for t in group}
+        prod, turned, tanhs, diffs, gates, turned_gates = {}, {}, {}, {}, {}, {}
+        spreads = tile([P, PACK, V], F32, "spreads")
+        weighted = tile([P, PACK, V], F32, "weighted")
+        seconds = tile([P, PACK, V], F32, "seconds")
+
+        def keys(t, side, tag=None):
+            group, place = group_of[t]
+            if group not in prod:
+                prod[group] = tile([P, 2, len(group), V], F32, "prod%d" % group[0], tag=tag)
+            nc.vector.tensor_tensor(prod[group][:, side, place, :], rows["e", t].indirect(pos_lists[side][:]), query[t], ALU.mult)
+
+        def turn_products(group, sides, number):
+            made = bank([P, len(sides), len(group), V], "turned", number)
+            for place_of_side, side in enumerate(sides):
+                turned[group, side] = made[:, place_of_side]
+                for place in range(len(group)):
+                    for cols in halves:
+                        nc.tensor.transpose(turned[group, side][:, place, cols], prod[group][:, side, place, cols], identity[:])
+
+        def squash(group, side, src, tag=None):
+            if group not in tanhs:
+                tanhs[group] = tile([P, 2, len(group), V], F32, "tanhs%d" % group[0], tag=tag)
+            nc.scalar.activation(tanhs[group][:, side], src, ACT.Tanh, scale=signs[side])
+
+        def subtract(group, number):
+            diffs[group] = bank([P, len(group), V], "diffs", number)
+            for place in range(len(group)):
+                for cols in halves:
+                    for side in range(2):
+                        nc.tensor.matmul(diffs[group][:, place, cols], lhsT=tanhs[group][:, side, place, cols], rhs=identity[:],
+                                         is_transpose=True, start=side == 0, stop=side == 1)
+
+        def gate(group):
+            gates[group] = tile([P, len(group), V], F32, "gates%d" % group[0])
+            nc.scalar.activation(gates[group][:], diffs[group][:], ACT.Sigmoid)
+
+        def turn_gates(group, number):
+            turned_gates[group] = bank([P, len(group), V], "turned_gates", number)
+            for place in range(len(group)):
+                for cols in halves:
+                    nc.tensor.transpose(turned_gates[group][:, place, cols], gates[group][:, place, cols], identity[:])
+
+        def second_values(t, gather):
+            gather(seconds[:, t, :], rows["h", t], pos_lists[1][:])
+
+        def spread(t):
+            nc.vector.tensor_tensor(spreads[:, t, :], rows["h", t].indirect(pos_lists[0][:]), seconds[:, t, :], ALU.subtract)
+
+        def weigh(group, cols=slice(0, V)):
+            tiles = slice(group[0], group[-1] + 1)
+            nc.vector.tensor_tensor(weighted[:, tiles, cols], spreads[:, tiles, cols], turned_gates.get(group, gates[group])[:, :, cols], ALU.mult)
 
         nc.vector.tensor_copy(out=x_codes[:], in_=word_table[:].bitcast(U32).indirect(offs_list[:]))
         nc.vector.tensor_copy(out=x_bytes[:], in_=scale_table[:].indirect(offs_list[:]))
-
-        def y_woven(t):
-            return woven["y", t // 2][:, t % 2 : t % 2 + 1]
-
-        weave(y_woven(0), "y", slice(0, 1), nc.vector.tensor_copy)
-        weave(y_woven(1), "y", slice(1, 2), nc.scalar.copy)
-        weave(y_woven(3), "y", slice(3, 4), nc.scalar.copy)
-        quantise_single("y", 0, y_woven(0))
-        weave(y_woven(2), "y", slice(2, 3), nc.vector.tensor_copy)
-        quantise_single("y", 1, y_woven(1))
-        quantise_pair("y", 1)
-        for part in range(2):
-            cols = slice(part * S // 2, (part + 1) * S // 2)
-            half_sums = bank([P, S // 2], "half_sums", PACK * (1 - part))
-            nc.tensor.matmul_mx(out=half_sums[:], lhsT=w_codes["y", 0][:, halves[0]].bitcast(FP8X4), lhsT_scale=w_scales["y"][:, halves[0]],
-                                rhs=x_codes[:, cols].bitcast(FP8X4), rhs_scale=x_bytes[:, cols], start=True, stop=True)
-            nc.scalar.copy(out=rows["y", 0][:, cols], in_=half_sums[:])
+        y_woven = [tile([P, 2, P, PACK], BF16, "y_woven0")[:], placed([P, 2, P, PACK], BF16, "y_woven1", 512)[:]]
+        weave(y_woven[0][:, 0:1], "y", 0, 1, on_vector)
+        weave(y_woven[0][:, 1:2], "y", 1, 2, on_scalar)
+        weave(y_woven[1][:, 1:2], "y", 3, 4, on_scalar)
+        quantise("y", 0, 1, y_woven[0][:, 0:1])
+        weave(y_woven[1][:, 0:1], "y", 2, 3, on_vector)
+        quantise("y", 1, 2, y_woven[0][:, 1:2])
+        quantise("y", 2, 4, y_woven[1])
+        for part, cols in enumerate(point_halves):
+            multiply("y", 0, PACK * (1 - part), cols)
+            empty("y", 0, cols)
         for t in range(1, PACK):
-            multiply("y", t)
-            empty("y", t)
-
-        h_woven = tile([P, PACK, P, PACK], BF16, "h_woven")
-        for pair in range(2):
-            woven["h", pair] = h_woven[:, tile_pairs[pair]]
-
-        def weave_w3(piece, tiles, copy):
-            copy(out=h_woven[:].rearrange("p t (m r) j -> p m t j r", r=4)[:, w3_cols[piece].start // DEAL : w3_cols[piece].stop // DEAL, tiles],
-                 in_=w3_raw[piece][:].rearrange("p j (m t r) -> p m t j r", t=PACK, r=4)[:, :, tiles])
-
-        def gather_query(t):
-            nc.vector.tensor_copy(out=query[t], in_=rows["y", t].indirect(cen_list[:]))
-
-        weave_w3(0, slice(0, PACK), nc.vector.tensor_copy)
-        query_first = tile([P, 1, V], F32, "query_first", tag="w3_raw0")
-        query = [query_first[:, 0, :]]
-        gather_query(0)
-        e_single = [tile([P, 1, P, PACK], BF16, "e_single%d" % t)[:] for t in range(2)]
-        woven["e", 1] = tile([P, 2, P, PACK], BF16, "e_woven1")[:]
-        for t in range(2):
-            weave(e_single[t], "e", slice(t, t + 1), nc.vector.tensor_copy)
-        quantise_single("e", 0, e_single[0])
-        weave(woven["e", 1], "e", tile_pairs[1], nc.vector.tensor_copy)
-        quantise_single("e", 1, e_single[1])
-        quantise_pair("e", 1)
-
-        def scalar_query(t, tag):
-            query.append(tile([P, V], F32, "query%d" % t, tag=tag)[:])
-            nc.scalar.activation(query[t], rows["y", t].indirect(cen_list[:]), ACT.Copy)
-
-        scalar_query(1, None)
-
-        prod = {}
-        prod_tags = ["w3_raw1", "h_woven", None, None]
-        tanhs, turned_diffs, bank_gates = {}, {}, {}
-        tanh_tags = ["h_codes0", "h_codes1", None, None]
-        diffs = {}
-        gates = [tile([P, 2, V], F32, "gates%d" % t) for t in range(PACK)]
-        parts = [tile([P, PACK, V], F32, "parts%d" % side) for side in range(2)]
-
-        def keys(t):
-            prod[t] = tile([P, 2, V], F32, "prod%d" % t, tag=prod_tags[t])
-            for side in range(2):
-                nc.vector.tensor_tensor(prod[t][:, side, :], rows["e", t].indirect(pos_lists[side][:]), query[t], ALU.mult)
-
-        def scores_turned(t):
-            tanhs[t] = tile([P, 2, V], F32, "tanhs%d" % t, tag=tanh_tags[t])
-            turned = bank([P, 2, V], "turned", PACK + t)
-            for side in range(2):
-                for cols in halves:
-                    nc.tensor.transpose(turned[:, side, cols], prod[t][:, side, cols], identity[:])
-            for side in range(2):
-                nc.scalar.activation(tanhs[t][:, side, :], turned[:, side, :], ACT.Tanh, scale=signs[side])
-            turned_back = bank([P, V], "turned_back", PACK + t)
-            for cols in halves:
-                for side in range(2):
-                    nc.tensor.matmul(turned_back[:, cols], lhsT=tanhs[t][:, side, cols], rhs=identity[:], is_transpose=True,
-                                     start=side == 0, stop=side == 1)
-            diffs[t] = turned_back[:]
-
-        def first_gate(t):
-            nc.scalar.activation(gates[t][:, 0, :], diffs[t], ACT.Sigmoid)
-
-        def vector_second(t):
-            nc.vector.tensor_copy(out=parts[1][:, t, :], in_=rows["h", t].indirect(pos_lists[1][:]))
-
-        def entries(side, cols):
-            return pos_lists[side][:, cols.start // LIST_ROWS : cols.stop // LIST_ROWS]
-
-        def second_values(t, cols=slice(0, V)):
-            nc.scalar.activation(parts[1][:, t, cols], rows["h", t].indirect(entries(1, cols)), ACT.Copy)
-
-        def spread_values(t, cols=slice(0, V)):
-            nc.vector.tensor_tensor(gates[t][:, 1, cols], rows["h", t].indirect(entries(0, cols)), parts[1][:, t, cols], ALU.subtract)
-
-        def weigh(t):
-            nc.vector.tensor_tensor(parts[0][:, t, :], gates[t][:, 1, :], bank_gates[t][:] if t in bank_gates else gates[t][:, 0, :], ALU.mult)
-
-        def scores_added(t):
-            tanhs[t] = tile([P, 2, V], F32, "tanhs%d" % t, tag=tanh_tags[t])
-            for side in range(2):
-                nc.scalar.activation(tanhs[t][:, side, :], prod[t][:, side, :], ACT.Tanh, scale=signs[side])
-            turned_diffs[t] = bank([P, 2, P], "turned_diffs", PACK + t)
-            for half, cols in enumerate(halves):
-                for side in range(2):
-                    nc.tensor.matmul(turned_diffs[t][:, half, :], lhsT=tanhs[t][:, side, cols], rhs=identity[:], is_transpose=True,
-                                     start=side == 0, stop=side == 1)
-
-        def turned_gate(t):
-            turned = tile([P, 2, P], F32, "turned_gate%d" % t)
-            nc.scalar.activation(turned[:], turned_diffs[t][:], ACT.Sigmoid)
-            bank_gates[t] = bank([P, V], "bank_gates", t)
-            for half, cols in enumerate(halves):
-                nc.tensor.transpose(bank_gates[t][:, cols], turned[:, half, :], identity[:])
-
-        def values(pair):
-            quantise_pair("h", pair)
-            multiply("h", 2 * pair)
-            multiply("h", 2 * pair + 1)
-
+            multiply("y", t, t)
+        e_woven = [placed([P, count, P, PACK], BF16, "e_woven%d" % n, 1024 * n)[:] for n, count in enumerate((1, 1, 2))]
+        weave(e_woven[0], "e", 0, 1, on_vector)
+        weave(e_woven[1], "e", 1, 2, on_vector)
+        quantise("e", 0, 1, e_woven[0])
+        weave(e_woven[2], "e", 2, 4, on_vector)
+        quantise("e", 1, 2, e_woven[1])
+        quantise("e", 2, 4, e_woven[2])
+        empty("y", 1)
+        gather_query(0, scalar_gather)
+        empty("y", 2)
+        empty("y", 3)
+        gather_query(1, vector_gather, tag="w2_raw")
         for t in range(PACK):
-            multiply("e", t)
-        scalar_query(2, None)
-        empty("e", 0)
+            multiply("e", t, PACK + t)
+        h_woven = placed([P, PACK, P, PACK], BF16, "h_woven", 2048)[:]
         for pair in range(2):
-            weave_w3(1, tile_pairs[pair], nc.vector.tensor_copy)
-        values(0)
-        values(1)
-        keys(0)
+            weave(h_woven[:, 2 * pair : 2 * pair + 2], "h", 2 * pair, 2 * pair + 2, on_vector)
+        for pair in range(2):
+            quantise("h", 2 * pair, 2 * pair + 2, h_woven[:, 2 * pair : 2 * pair + 2])
+        empty("e", 0)
         empty("e", 1)
-        scalar_query(3, "e_first_codes1")
-        keys(1)
+        gather_query(2, scalar_gather, tag="e_codes0")
         empty("e", 2)
+        gather_query(3, scalar_gather, tag="e_codes1")
         empty("e", 3)
-        keys(2)
-        scores_added(0)
-        keys(3)
+        for t in range(PACK):
+            multiply("h", t, t)
+        prod[groups[1]] = placed([P, 2, 2, V], F32, "prod2", 2048)
+        for pair in groups:
+            for side in range(2):
+                for n in pair:
+                    keys(n, side, tag="w3_raw")
+
+        dealt = [tile([P, 2, 2, 2, P], F32, "tanhs%d" % (2 * u + 1)) for u in range(2)]
+        second_sides = {}
+
+        def turn_second_side(n, number):
+            second_sides[n] = bank([P, V], "second_side", number)
+            for cols in halves:
+                nc.tensor.transpose(second_sides[n][:, cols], prod[groups[n // 2]][:, 1, n % 2, cols], identity[:])
+
+        def squash_first_sides(u):
+            nc.scalar.activation(dealt[u][:, 0].rearrange("p c t x -> p t c x"),
+                                 turned[groups[u], 0].rearrange("p t (c x) -> p t c x", x=P), ACT.Tanh, scale=signs[0])
+
+        def squash_second_side(n):
+            nc.scalar.activation(dealt[n // 2][:, 1, :, n % 2, :],
+                                 second_sides[n][:].rearrange("p (c x) -> p c x", x=P), ACT.Tanh, scale=signs[1])
+
+        def turn_back(dst, u, side, which):
+            for half in which:
+                for place in range(2):
+                    nc.tensor.matmul(dst[:, place, slice(0, P) if len(which) == 1 else halves[half]],
+                                     lhsT=dealt[u][:, side, half, place], rhs=identity[:], is_transpose=True,
+                                     start=(side, half, place) == (0, which[0], 0), stop=(side, half, place) == (1, which[-1], 1))
+
+        first, final = groups
         empty("h", 0)
-        second_values(0)
         empty("h", 1)
-        scores_turned(1)
-        turned_gate(0)
-        spread_values(0)
-        second_values(1)
+        turn_products(first, [0], 4)
+        turn_second_side(0, 5)
+        second_values(0, scalar_gather)
+        squash_first_sides(0)
+        turn_second_side(1, 7)
+        diffs[first] = bank([P, 2, V], "diffs", 0)
+        turn_back(diffs[first], 0, 0, (0, 1))
+        second_values(1, scalar_gather)
+        squash_second_side(0)
+        squash_second_side(1)
+        turn_products(final, [0], 6)
+        turn_second_side(2, 4)
+        turn_back(diffs[first], 0, 1, (0, 1))
+        turn_second_side(3, 5)
         empty("h", 2)
-        spread_values(1)
-        scores_turned(2)
-        vector_second(2)
-        weigh(0)
-        empty("h", last)
-        scores_turned(last)
-        spread_values(2)
-        second_values(last)
-        first_gate(1)
-        first_gate(2)
-        first_gate(last)
-        spread_values(last)
-        weigh(1)
-        weigh(2)
+        squash_first_sides(1)
+        half_diffs = [bank([P, 2, P], "half_diffs", number) for number in (1, 6)]
+        for half in range(2):
+            turn_back(half_diffs[half], 1, 0, (half,))
+        spread(0)
+        second_values(2, vector_gather)
+        spread(1)
+        empty("h", 3)
+        squash_second_side(2)
+        squash_second_side(3)
+        for half in range(2):
+            turn_back(half_diffs[half], 1, 1, (half,))
+        spread(2)
+        second_values(3, scalar_gather)
+        gate(first)
+        gates[final] = tile([P, 2, V], F32, "gates3")
+        for half, cols in enumerate(halves):
+            nc.scalar.activation(gates[final][:, :, cols], half_diffs[half][:], ACT.Sigmoid)
+        spread(3)
+        weigh(first)
         for cols in halves:
-            nc.vector.tensor_tensor(parts[0][:, last, cols], gates[last][:, 1, cols], gates[last][:, 0, cols], ALU.mult)
+            weigh(final, cols)
 
         w4_woven = tile([P, N, PACK], BF16, "w4_woven", tag="tanhs3")
         w4_codes = tile([P, N], U32, "w4_codes", tag="gates3")
@@ -283,8 +289,8 @@ def tile_picked_zpt_mul_p_kernel(tc, x_words, x_scales, w1, w2, w3, w4, offs, ce
         z_woven = tile([P, V, PACK], BF16, "z_woven")
         for cols in halves:
             nc.vector.tensor_tensor(z_woven[:, cols, :].rearrange("p (c i) t -> p c t i", i=4),
-                                    parts[0][:, :, cols].rearrange("p t (c i) -> p c t i", i=4),
-                                    parts[1][:, :, cols].rearrange("p t (c i) -> p c t i", i=4), ALU.add)
+                                    weighted[:, :, cols].rearrange("p t (c i) -> p c t i", i=4),
+                                    seconds[:, :, cols].rearrange("p t (c i) -> p c t i", i=4), ALU.add)
 
         def quantise_z(cols):
             nc.vector.quantize_mx(out=z_codes[:, cols].bitcast(FP8X4), scales=z_scales[:, cols],

@@ -181,7 +181,10 @@ def tile_picked_zpt_mul_p_kernel(tc, x_words, x_scales, w1, w2, w3, w4, offs, ce
         for part, cols in enumerate(point_halves):
             multiply("y", 0, PACK * (1 - part), cols)
             empty("y", 0, cols)
-        for t in range(1, PACK):
+        for part, cols in enumerate(point_halves):
+            multiply("y", 1, 1 + PACK * (1 - part), cols)
+            empty("y", 1, cols)
+        for t in range(2, PACK):
             multiply("y", t, t)
         e_woven = [placed([P, count, P, PACK], BF16, "e_woven%d" % n, 1024 * n)[:] for n, count in enumerate((1, 1, 2))]
         weave(e_woven[0], "e", 0, 1, on_vector)
@@ -190,7 +193,6 @@ def tile_picked_zpt_mul_p_kernel(tc, x_words, x_scales, w1, w2, w3, w4, offs, ce
         weave(e_woven[2], "e", 2, 4, on_vector)
         quantise("e", 1, 2, e_woven[1])
         quantise("e", 2, 4, e_woven[2])
-        empty("y", 1)
         gather_query(0, scalar_gather)
         empty("y", 2)
         empty("y", 3)
@@ -224,9 +226,9 @@ def tile_picked_zpt_mul_p_kernel(tc, x_words, x_scales, w1, w2, w3, w4, offs, ce
             for cols in halves:
                 nc.tensor.transpose(second_sides[n][:, cols], prod[groups[n // 2]][:, 1, n % 2, cols], identity[:])
 
-        def squash_first_sides(u):
-            nc.scalar.activation(dealt[u][:, 0].rearrange("p c t x -> p t c x"),
-                                 turned[groups[u], 0].rearrange("p t (c x) -> p t c x", x=P), ACT.Tanh, scale=signs[0])
+        def squash_first_sides(u, side=0):
+            nc.scalar.activation(dealt[u][:, side].rearrange("p c t x -> p t c x"),
+                                 turned[groups[u], side].rearrange("p t (c x) -> p t c x", x=P), ACT.Tanh, scale=signs[side])
 
         def squash_second_side(n):
             nc.scalar.activation(dealt[n // 2][:, 1, :, n % 2, :],
@@ -243,19 +245,17 @@ def tile_picked_zpt_mul_p_kernel(tc, x_words, x_scales, w1, w2, w3, w4, offs, ce
         empty("h", 0)
         empty("h", 1)
         turn_products(first, [0], 4)
-        turn_second_side(0, 5)
+        turn_products(first, [1], 5)
         second_values(0, scalar_gather)
         squash_first_sides(0)
-        turn_second_side(1, 7)
         diffs[first] = bank([P, 2, V], "diffs", 0)
         turn_back(diffs[first], 0, 0, (0, 1))
         second_values(1, scalar_gather)
-        squash_second_side(0)
-        squash_second_side(1)
+        squash_first_sides(0, 1)
         turn_products(final, [0], 6)
         turn_second_side(2, 4)
         turn_back(diffs[first], 0, 1, (0, 1))
-        turn_second_side(3, 5)
+        turn_second_side(3, 7)
         empty("h", 2)
         squash_first_sides(1)
         half_diffs = [bank([P, 2, P], "half_diffs", number) for number in (1, 6)]

@@ -65,7 +65,10 @@ def tile_picked_zpt_mul_p_kernel(tc, x_words, x_scales, w1, w2, w3, w4, offs, ce
             nc.sync.dma_start(out=scale_table[r:P:32, :].bitcast(I32), in_=scale_rows[r].bitcast(I32))
         raw = {"y": load_weight(w1, "w1_raw")}
         cen_list = load_list(cen, "cen_list")
-        raw["e"] = load_weight(w2, "w2_raw")
+        w2_raw = tile([P, PACK, H], F32, "w2_raw")
+        for rows_of_k in (slice(0, 2), slice(2, PACK)):
+            nc.sync.dma_start(out=w2_raw[:, rows_of_k, :], in_=w2.rearrange("(p j) c -> p j c", j=PACK)[:, rows_of_k, :])
+        raw["e"] = w2_raw[:]
         raw["h"] = load_weight(w3, "w3_raw")
         pos_lists = [load_list(pos1, "pos1_list"), load_list(pos2, "pos2_list")]
         w4_raw = tile([P, PACK, N], F32, "w4_raw")[:]
@@ -82,9 +85,9 @@ def tile_picked_zpt_mul_p_kernel(tc, x_words, x_scales, w1, w2, w3, w4, offs, ce
         signs = [1.0, -1.0]
         on_vector, on_scalar = nc.vector.tensor_copy, nc.scalar.copy
 
-        def weave(dst, src, first, stop, copy):
-            copy(out=dst.rearrange("p t (m r) j -> p m t j r", r=4),
-                 in_=raw[src].rearrange("p j (m t r) -> p m t j r", t=PACK, r=4)[:, :, first:stop])
+        def weave(dst, src, first, stop, copy, planes=slice(0, PACK)):
+            copy(out=dst.rearrange("p t (m r) j -> p m t j r", r=4)[:, :, :, planes],
+                 in_=raw[src].rearrange("p j (m t r) -> p m t j r", t=PACK, r=4)[:, :, first:stop, planes])
 
         def quantise(name, first, stop, src, tag=None):
             made = tile([P, P * (stop - first)], U32, name + "_codes%d" % first, tag=tag)
@@ -186,11 +189,13 @@ def tile_picked_zpt_mul_p_kernel(tc, x_words, x_scales, w1, w2, w3, w4, offs, ce
             empty("y", 1, cols)
         for t in range(2, PACK):
             multiply("y", t, t)
-        e_woven = [placed([P, count, P, PACK], BF16, "e_woven%d" % n, 1024 * n)[:] for n, count in enumerate((1, 1, 2))]
-        weave(e_woven[0], "e", 0, 1, on_vector)
-        weave(e_woven[1], "e", 1, 2, on_vector)
+        e_all = placed([P, PACK, P, PACK], BF16, "e_woven", 0)
+        e_woven = [e_all[:, 0:1], e_all[:, 1:2], e_all[:, 2:4]]
+        weave(e_all[:], "e", 0, PACK, on_vector, slice(0, 2))
+        weave(e_woven[0], "e", 0, 1, on_vector, slice(2, PACK))
+        weave(e_woven[1], "e", 1, 2, on_vector, slice(2, PACK))
         quantise("e", 0, 1, e_woven[0])
-        weave(e_woven[2], "e", 2, 4, on_vector)
+        weave(e_woven[2], "e", 2, 4, on_vector, slice(2, PACK))
         quantise("e", 1, 2, e_woven[1])
         quantise("e", 2, 4, e_woven[2])
         gather_query(0, scalar_gather)

@@ -7,6 +7,7 @@ K, T, S, V, H, N = 512, 2048, 512, 256, 512, 256
 P = 128
 PACK = 4
 LIST_ROWS = 16
+ALIGN = 256
 FLOPS = 2 * K * S * H * 3 + 2 * H * N * V
 
 F32 = mybir.dt.float32
@@ -28,10 +29,10 @@ def tile_picked_zpt_mul_p_kernel(tc, x_words, x_scales, w1, w2, w3, w4, offs, ce
         ps = ctx.enter_context(tc.psum_pool(name="ps", bufs=1))
 
         def tile(shape, dtype, name, tag=None):
-            return sb.tile(shape, dtype, name=name, tag=tag or name, align_bytes=64)
+            return sb.tile(shape, dtype, name=name, tag=tag or name, align_bytes=ALIGN)
 
         def placed(shape, dtype, name, offset):
-            return laid.tile(shape, dtype, name=name, offset=offset, align_bytes=64)
+            return laid.tile(shape, dtype, name=name, offset=offset, align_bytes=ALIGN)
 
         def bank(shape, name, number):
             return ps.tile(shape, F32, name=name, tag="bank%d" % number)
@@ -41,14 +42,11 @@ def tile_picked_zpt_mul_p_kernel(tc, x_words, x_scales, w1, w2, w3, w4, offs, ce
             nc.sync.dma_start(lst[:], src)
             return lst
 
-        def load_weight(w, name, cols=slice(0, H)):
-            raw_tile = tile([P, PACK, cols.stop - cols.start], F32, name)
-            nc.sync.dma_start(out=raw_tile[:], in_=w.rearrange("(p j) c -> p j c", j=PACK)[:, :, cols])
-            return raw_tile[:]
+        def load_rows(name, w, rows_of_k):
+            nc.sync.dma_start(out=raw[name][:, rows_of_k, :], in_=w.rearrange("(p j) c -> p j c", j=PACK)[:, rows_of_k, :])
 
         halves = [slice(0, P), slice(P, 2 * P)]
-        point_halves = [slice(0, S // 2), slice(S // 2, S)]
-        last = PACK - 1
+        whole, row_pairs = slice(0, PACK), [slice(0, 2), slice(2, PACK)]
 
         scale_table = tile([P, T], U8, "scale_table")
         nc.vector.memset(scale_table[:, : T // 2].bitcast(I32), 0)
@@ -57,19 +55,19 @@ def tile_picked_zpt_mul_p_kernel(tc, x_words, x_scales, w1, w2, w3, w4, offs, ce
         nc.vector.memset(warm[:, 0:1], 0.0)
         nc.scalar.activation(warm[:, 1:2], warm[:, 0:1], ACT.Sigmoid)
 
-        word_table = tile([P, T], I32, "word_table")
-        nc.sync.dma_start(out=word_table[:], in_=x_words[0].rearrange("p n j -> p (n j)").bitcast(I32))
+        raw = {name: tile([P, PACK, H], F32, tag)[:] for name, tag in (("y", "w1_raw"), ("e", "w2_raw"), ("h", "w3_raw"))}
+        load_rows("y", w1, row_pairs[0])
         offs_list = load_list(offs, "offs_list")
         scale_rows = x_scales[0].rearrange("(q r) c -> r q c", r=4)
         for r in range(4):
             nc.sync.dma_start(out=scale_table[r:P:32, :].bitcast(I32), in_=scale_rows[r].bitcast(I32))
-        raw = {"y": load_weight(w1, "w1_raw")}
+        load_rows("y", w1, row_pairs[1])
+        word_table = tile([P, T], I32, "word_table")
+        nc.sync.dma_start(out=word_table[:], in_=x_words[0].rearrange("p n j -> p (n j)").bitcast(I32))
         cen_list = load_list(cen, "cen_list")
-        w2_raw = tile([P, PACK, H], F32, "w2_raw")
-        for rows_of_k in (slice(0, 2), slice(2, PACK)):
-            nc.sync.dma_start(out=w2_raw[:, rows_of_k, :], in_=w2.rearrange("(p j) c -> p j c", j=PACK)[:, rows_of_k, :])
-        raw["e"] = w2_raw[:]
-        raw["h"] = load_weight(w3, "w3_raw")
+        for rows_of_k in row_pairs:
+            load_rows("e", w2, rows_of_k)
+        load_rows("h", w3, whole)
         pos_lists = [load_list(pos1, "pos1_list"), load_list(pos2, "pos2_list")]
         w4_raw = tile([P, PACK, N], F32, "w4_raw")[:]
         w4_rows = w4.rearrange("(m t r) n -> t m r n", t=PACK, r=4)
@@ -78,10 +76,9 @@ def tile_picked_zpt_mul_p_kernel(tc, x_words, x_scales, w1, w2, w3, w4, offs, ce
 
         identity = tile([P, P], F32, "identity")
         make_identity(nc, identity[:])
-        x_codes = tile([P, S], U32, "x_codes")
         x_bytes = tile([P, S], U8, "x_bytes")
         w_scales = {name: tile([P, H], U8, name + "_scales") for name in "yeh"}
-        woven, codes, rows, sums, query = {}, {}, {}, {}, {}
+        codes, rows, sums, query = {}, {}, {}, {}
         signs = [1.0, -1.0]
         on_vector, on_scalar = nc.vector.tensor_copy, nc.scalar.copy
 
@@ -89,23 +86,25 @@ def tile_picked_zpt_mul_p_kernel(tc, x_words, x_scales, w1, w2, w3, w4, offs, ce
             copy(out=dst.rearrange("p t (m r) j -> p m t j r", r=4)[:, :, :, planes],
                  in_=raw[src].rearrange("p j (m t r) -> p m t j r", t=PACK, r=4)[:, :, first:stop, planes])
 
-        def quantise(name, first, stop, src, tag=None):
-            made = tile([P, P * (stop - first)], U32, name + "_codes%d" % first, tag=tag)
+        def quantise(name, first, stop, src, made=None):
+            if made is None:
+                made = tile([P, P * (stop - first)], U32, name + "_codes%d" % first)
             nc.vector.quantize_mx(out=made[:].bitcast(FP8X4), scales=w_scales[name][:, P * first : P * stop],
                                   in_=src.rearrange("p t m j -> p (t m j)"))
             for t in range(first, stop):
                 codes[name, t] = made[:, P * (t - first) : P * (t - first + 1)]
 
-        def multiply(name, t, number, cols=slice(0, S)):
-            sums[name, t, cols.start] = bank([P, cols.stop - cols.start], "sums", number)
-            nc.tensor.matmul_mx(out=sums[name, t, cols.start][:], lhsT=codes[name, t].bitcast(FP8X4),
-                                lhsT_scale=w_scales[name][:, P * t : P * t + P],
+        def product(dst, name, t, cols):
+            nc.tensor.matmul_mx(out=dst, lhsT=codes[name, t].bitcast(FP8X4), lhsT_scale=w_scales[name][:, P * t : P * t + P],
                                 rhs=x_codes[:, cols].bitcast(FP8X4), rhs_scale=x_bytes[:, cols], start=True, stop=True)
 
-        def empty(name, t, cols=slice(0, S), copy=nc.scalar.copy, tag=None):
-            if (name, t) not in rows:
-                rows[name, t] = tile([P, S], F32, name + "_rows%d" % t, tag=tag)[:]
-            copy(out=rows[name, t][:, cols], in_=sums[name, t, cols.start][:])
+        def multiply(name, t, number):
+            sums[name, t] = bank([P, S], "sums", number)
+            product(sums[name, t][:], name, t, slice(0, S))
+
+        def empty(name, t):
+            rows[name, t] = tile([P, S], F32, name + "_rows%d" % t)[:]
+            nc.scalar.copy(out=rows[name, t], in_=sums[name, t][:])
 
         def scalar_gather(dst, window, lst):
             nc.scalar.activation(dst, window.indirect(lst), ACT.Copy)
@@ -115,80 +114,31 @@ def tile_picked_zpt_mul_p_kernel(tc, x_words, x_scales, w1, w2, w3, w4, offs, ce
 
         def gather_query(t, gather, tag=None):
             query[t] = tile([P, V], F32, "query%d" % t, tag=tag)[:]
-            gather(query[t], rows["y", t], cen_list[:])
+            gather(query[t], y_rows[t // 2][:, t % 2, :], cen_list[:])
 
-        groups = [(0, 1), (2, 3)]
-        group_of = {t: (group, t - group[0]) for group in groups for t in group}
-        prod, turned, tanhs, diffs, gates, turned_gates = {}, {}, {}, {}, {}, {}
-        spreads = tile([P, PACK, V], F32, "spreads")
-        weighted = tile([P, PACK, V], F32, "weighted")
-        seconds = tile([P, PACK, V], F32, "seconds")
-
-        def keys(t, side, tag=None):
-            group, place = group_of[t]
-            if group not in prod:
-                prod[group] = tile([P, 2, len(group), V], F32, "prod%d" % group[0], tag=tag)
-            nc.vector.tensor_tensor(prod[group][:, side, place, :], rows["e", t].indirect(pos_lists[side][:]), query[t], ALU.mult)
-
-        def turn_products(group, sides, number):
-            made = bank([P, len(sides), len(group), V], "turned", number)
-            for place_of_side, side in enumerate(sides):
-                turned[group, side] = made[:, place_of_side]
-                for place in range(len(group)):
-                    for cols in halves:
-                        nc.tensor.transpose(turned[group, side][:, place, cols], prod[group][:, side, place, cols], identity[:])
-
-        def squash(group, side, src, tag=None):
-            if group not in tanhs:
-                tanhs[group] = tile([P, 2, len(group), V], F32, "tanhs%d" % group[0], tag=tag)
-            nc.scalar.activation(tanhs[group][:, side], src, ACT.Tanh, scale=signs[side])
-
-        def subtract(group, number):
-            diffs[group] = bank([P, len(group), V], "diffs", number)
-            for place in range(len(group)):
-                for cols in halves:
-                    for side in range(2):
-                        nc.tensor.matmul(diffs[group][:, place, cols], lhsT=tanhs[group][:, side, place, cols], rhs=identity[:],
-                                         is_transpose=True, start=side == 0, stop=side == 1)
-
-        def gate(group):
-            gates[group] = tile([P, len(group), V], F32, "gates%d" % group[0])
-            nc.scalar.activation(gates[group][:], diffs[group][:], ACT.Sigmoid)
-
-        def turn_gates(group, number):
-            turned_gates[group] = bank([P, len(group), V], "turned_gates", number)
-            for place in range(len(group)):
-                for cols in halves:
-                    nc.tensor.transpose(turned_gates[group][:, place, cols], gates[group][:, place, cols], identity[:])
-
-        def second_values(t, gather):
-            gather(seconds[:, t, :], rows["h", t], pos_lists[1][:])
-
-        def spread(t):
-            nc.vector.tensor_tensor(spreads[:, t, :], rows["h", t].indirect(pos_lists[0][:]), seconds[:, t, :], ALU.subtract)
-
-        def weigh(group, cols=slice(0, V)):
-            tiles = slice(group[0], group[-1] + 1)
-            nc.vector.tensor_tensor(weighted[:, tiles, cols], spreads[:, tiles, cols], turned_gates.get(group, gates[group])[:, :, cols], ALU.mult)
-
-        nc.vector.tensor_copy(out=x_codes[:], in_=word_table[:].bitcast(U32).indirect(offs_list[:]))
+        y_woven = placed([P, PACK, P, PACK], BF16, "y_woven", 2048)[:]
+        weave(y_woven[:, 0:2], "y", 0, 2, on_vector, row_pairs[0])
+        weave(y_woven[:, 2:4], "y", 2, 4, on_scalar, row_pairs[0])
         nc.vector.tensor_copy(out=x_bytes[:], in_=scale_table[:].indirect(offs_list[:]))
-        y_woven = [tile([P, 2, P, PACK], BF16, "y_woven0")[:], placed([P, 2, P, PACK], BF16, "y_woven1", 512)[:]]
-        weave(y_woven[0][:, 0:1], "y", 0, 1, on_vector)
-        weave(y_woven[0][:, 1:2], "y", 1, 2, on_scalar)
-        weave(y_woven[1][:, 1:2], "y", 3, 4, on_scalar)
-        quantise("y", 0, 1, y_woven[0][:, 0:1])
-        weave(y_woven[1][:, 0:1], "y", 2, 3, on_vector)
-        quantise("y", 1, 2, y_woven[0][:, 1:2])
-        quantise("y", 2, 4, y_woven[1])
-        for part, cols in enumerate(point_halves):
-            multiply("y", 0, PACK * (1 - part), cols)
-            empty("y", 0, cols)
-        for part, cols in enumerate(point_halves):
-            multiply("y", 1, 1 + PACK * (1 - part), cols)
-            empty("y", 1, cols)
-        for t in range(2, PACK):
-            multiply("y", t, t)
+        weave(y_woven[:, 0:2], "y", 0, 2, on_vector, row_pairs[1])
+        weave(y_woven[:, 2:4], "y", 2, 4, on_scalar, row_pairs[1])
+        quantise("y", 2, 4, y_woven[:, 2:4])
+        quantise("y", 0, 2, y_woven[:, 0:2])
+        x_codes = placed([P, S], U32, "x_codes", 4096)
+        point_pieces = [slice(0, P), slice(P, 2 * P), slice(2 * P, S)]
+        for cols in point_pieces:
+            nc.vector.tensor_copy(out=x_codes[:, cols], in_=word_table[:].bitcast(U32).indirect(
+                offs_list[:, cols.start // LIST_ROWS : cols.stop // LIST_ROWS]))
+        y_rows = [tile([P, 2, S], F32, "y_rows%d" % pair) for pair in range(2)]
+        point_halves = [slice(0, S // 2), slice(S // 2, S)]
+        y_steps = [(0, 0, point_pieces[:2]), (1, 0, point_halves[:1]), (0, 1, point_halves[1:]), (1, 1, point_halves[1:])]
+        for number, (pair, half, pieces) in enumerate(y_steps):
+            made = bank([P, 2, S // 2], "y_sums", number)
+            for cols in pieces:
+                for place in range(2):
+                    product(made[:, place, cols.start - half * S // 2 : cols.stop - half * S // 2], "y", 2 * pair + place, cols)
+            nc.scalar.copy(out=y_rows[pair][:, :, point_halves[half]], in_=made[:])
+
         e_all = placed([P, PACK, P, PACK], BF16, "e_woven", 0)
         e_woven = [e_all[:, 0:1], e_all[:, 1:2], e_all[:, 2:4]]
         weave(e_all[:], "e", 0, PACK, on_vector, slice(0, 2))
@@ -199,12 +149,10 @@ def tile_picked_zpt_mul_p_kernel(tc, x_words, x_scales, w1, w2, w3, w4, offs, ce
         quantise("e", 1, 2, e_woven[1])
         quantise("e", 2, 4, e_woven[2])
         gather_query(0, scalar_gather)
-        empty("y", 2)
-        empty("y", 3)
         gather_query(1, vector_gather, tag="w2_raw")
         for t in range(PACK):
             multiply("e", t, PACK + t)
-        h_woven = placed([P, PACK, P, PACK], BF16, "h_woven", 2048)[:]
+        h_woven = placed([P, PACK, P, PACK], BF16, "h_woven", 0)[:]
         for pair in range(2):
             weave(h_woven[:, 2 * pair : 2 * pair + 2], "h", 2 * pair, 2 * pair + 2, on_vector)
         for pair in range(2):
@@ -217,52 +165,65 @@ def tile_picked_zpt_mul_p_kernel(tc, x_words, x_scales, w1, w2, w3, w4, offs, ce
         empty("e", 3)
         for t in range(PACK):
             multiply("h", t, t)
-        prod[groups[1]] = placed([P, 2, 2, V], F32, "prod2", 2048)
-        for pair in groups:
+
+        prod = [tile([P, 2, 2, V], F32, "prod0", tag="w3_raw"), placed([P, 2, 2, V], F32, "prod1", 0)]
+        for pair in range(2):
             for side in range(2):
-                for n in pair:
-                    keys(n, side, tag="w3_raw")
+                for place in range(2):
+                    t = 2 * pair + place
+                    nc.vector.tensor_tensor(prod[pair][:, side, place, :], rows["e", t].indirect(pos_lists[side][:]), query[t], ALU.mult)
 
-        dealt = [tile([P, 2, 2, 2, P], F32, "tanhs%d" % (2 * u + 1)) for u in range(2)]
-        second_sides = {}
+        tanhs = [tile([P, 2, 2, 2, P], F32, "tanhs%d" % pair) for pair in range(2)]
+        gates = [tile([P, 2, V], F32, "gates%d" % pair) for pair in range(2)]
+        spreads = tile([P, PACK, V], F32, "spreads")
+        weighted = tile([P, PACK, V], F32, "weighted")
+        seconds = tile([P, PACK, V], F32, "seconds")
 
-        def turn_second_side(n, number):
-            second_sides[n] = bank([P, V], "second_side", number)
-            for cols in halves:
-                nc.tensor.transpose(second_sides[n][:, cols], prod[groups[n // 2]][:, 1, n % 2, cols], identity[:])
+        def turn(pair, side, places, number):
+            made = bank([P, len(places), V], "turned", number)
+            for n, place in enumerate(places):
+                for cols in halves:
+                    nc.tensor.transpose(made[:, n, cols], prod[pair][:, side, place, cols], identity[:])
+            return made
 
-        def squash_first_sides(u, side=0):
-            nc.scalar.activation(dealt[u][:, side].rearrange("p c t x -> p t c x"),
-                                 turned[groups[u], side].rearrange("p t (c x) -> p t c x", x=P), ACT.Tanh, scale=signs[side])
+        def squash(pair, side, places, src):
+            nc.scalar.activation(tanhs[pair][:, side, :, places[0] : places[-1] + 1, :].rearrange("p c t x -> p t c x"),
+                                 src[:].rearrange("p t (c x) -> p t c x", x=P), ACT.Tanh, scale=signs[side])
 
-        def squash_second_side(n):
-            nc.scalar.activation(dealt[n // 2][:, 1, :, n % 2, :],
-                                 second_sides[n][:].rearrange("p (c x) -> p c x", x=P), ACT.Tanh, scale=signs[1])
-
-        def turn_back(dst, u, side, which):
+        def turn_back(dst, pair, side, which):
             for half in which:
                 for place in range(2):
                     nc.tensor.matmul(dst[:, place, slice(0, P) if len(which) == 1 else halves[half]],
-                                     lhsT=dealt[u][:, side, half, place], rhs=identity[:], is_transpose=True,
+                                     lhsT=tanhs[pair][:, side, half, place], rhs=identity[:], is_transpose=True,
                                      start=(side, half, place) == (0, which[0], 0), stop=(side, half, place) == (1, which[-1], 1))
 
-        first, final = groups
+        def second_values(t, gather):
+            gather(seconds[:, t, :], rows["h", t], pos_lists[1][:])
+
+        def spread(t):
+            nc.vector.tensor_tensor(spreads[:, t, :], rows["h", t].indirect(pos_lists[0][:]), seconds[:, t, :], ALU.subtract)
+
+        def weigh(pair, cols):
+            tiles = slice(2 * pair, 2 * pair + 2)
+            nc.vector.tensor_tensor(weighted[:, tiles, cols], spreads[:, tiles, cols], gates[pair][:, :, cols], ALU.mult)
+
+        both = (0, 1)
         empty("h", 0)
         empty("h", 1)
-        turn_products(first, [0], 4)
-        turn_products(first, [1], 5)
+        turned_00 = turn(0, 0, both, 4)
+        turned_01 = turn(0, 1, both, 5)
         second_values(0, scalar_gather)
-        squash_first_sides(0)
-        diffs[first] = bank([P, 2, V], "diffs", 0)
-        turn_back(diffs[first], 0, 0, (0, 1))
+        squash(0, 0, both, turned_00)
+        diffs = bank([P, 2, V], "diffs", 0)
+        turn_back(diffs, 0, 0, both)
         second_values(1, scalar_gather)
-        squash_first_sides(0, 1)
-        turn_products(final, [0], 6)
-        turn_second_side(2, 4)
-        turn_back(diffs[first], 0, 1, (0, 1))
-        turn_second_side(3, 7)
+        squash(0, 1, both, turned_01)
+        turned_10 = turn(1, 0, both, 6)
+        turned_2 = turn(1, 1, (0,), 4)
+        turn_back(diffs, 0, 1, both)
+        turned_3 = turn(1, 1, (1,), 7)
         empty("h", 2)
-        squash_first_sides(1)
+        squash(1, 0, both, turned_10)
         half_diffs = [bank([P, 2, P], "half_diffs", number) for number in (1, 6)]
         for half in range(2):
             turn_back(half_diffs[half], 1, 0, (half,))
@@ -270,23 +231,22 @@ def tile_picked_zpt_mul_p_kernel(tc, x_words, x_scales, w1, w2, w3, w4, offs, ce
         second_values(2, vector_gather)
         spread(1)
         empty("h", 3)
-        squash_second_side(2)
-        squash_second_side(3)
+        squash(1, 1, (0,), turned_2)
+        squash(1, 1, (1,), turned_3)
         for half in range(2):
             turn_back(half_diffs[half], 1, 1, (half,))
         spread(2)
         second_values(3, scalar_gather)
-        gate(first)
-        gates[final] = tile([P, 2, V], F32, "gates3")
+        nc.scalar.activation(gates[0][:], diffs[:], ACT.Sigmoid)
         for half, cols in enumerate(halves):
-            nc.scalar.activation(gates[final][:, :, cols], half_diffs[half][:], ACT.Sigmoid)
+            nc.scalar.activation(gates[1][:, :, cols], half_diffs[half][:], ACT.Sigmoid)
         spread(3)
-        weigh(first)
+        weigh(0, slice(0, V))
         for cols in halves:
-            weigh(final, cols)
+            weigh(1, cols)
 
-        w4_woven = tile([P, N, PACK], BF16, "w4_woven", tag="tanhs3")
-        w4_codes = tile([P, N], U32, "w4_codes", tag="gates3")
+        w4_woven = tile([P, N, PACK], BF16, "w4_woven", tag="tanhs1")
+        w4_codes = tile([P, N], U32, "w4_codes", tag="gates1")
         w4_scales = tile([P, N], U8, "w4_scales")
         z_codes = tile([P, V], U32, "z_codes")
         z_scales = tile([P, V], U8, "z_scales")

@@ -197,8 +197,8 @@ def tile_picked_zpt_mul_p_kernel(tc, x_words, x_scales, w1, w2, w3, w4, offs, ce
                                      lhsT=tanhs[pair][:, side, half, place], rhs=identity[:], is_transpose=True,
                                      start=(side, half, place) == (0, which[0], 0), stop=(side, half, place) == (1, which[-1], 1))
 
-        def second_values(t, gather):
-            gather(seconds[:, t, :], rows["h", t], pos_lists[1][:])
+        def second_values(t, gather, cols=slice(0, V)):
+            gather(seconds[:, t, cols], rows["h", t], pos_lists[1][:, cols.start // LIST_ROWS : cols.stop // LIST_ROWS])
 
         def spread(t):
             nc.vector.tensor_tensor(spreads[:, t, :], rows["h", t].indirect(pos_lists[0][:]), seconds[:, t, :], ALU.subtract)
@@ -224,11 +224,12 @@ def tile_picked_zpt_mul_p_kernel(tc, x_words, x_scales, w1, w2, w3, w4, offs, ce
         turned_3 = turn(1, 1, (1,), 7)
         empty("h", 2)
         squash(1, 0, both, turned_10)
+        second_values(2, scalar_gather, halves[1])
         half_diffs = [bank([P, 2, P], "half_diffs", number) for number in (1, 6)]
         for half in range(2):
             turn_back(half_diffs[half], 1, 0, (half,))
         spread(0)
-        second_values(2, vector_gather)
+        second_values(2, vector_gather, halves[0])
         spread(1)
         empty("h", 3)
         squash(1, 1, (0,), turned_2)

@@ -55,20 +55,24 @@ def tile_picked_zpt_mul_p_kernel(tc, x_words, x_scales, w1, w2, w3, w4, offs, ce
         nc.vector.memset(warm[:, 0:1], 0.0)
         nc.scalar.activation(warm[:, 1:2], warm[:, 0:1], ACT.Sigmoid)
 
-        raw = {name: tile([P, PACK, H], F32, tag)[:] for name, tag in (("y", "w1_raw"), ("e", "w2_raw"), ("h", "w3_raw"))}
-        load_rows("y", w1, row_pairs[0])
+        def load_half(w, half, dst):
+            nc.sync.dma_start(out=dst, in_=w.rearrange("(p j) c -> p j c", j=PACK)[:, :, half * H // 2 : (half + 1) * H // 2])
+            return dst
+
+        w1_halves = [load_half(w1, 0, tile([P, PACK, H // 2], F32, "w1_raw0")[:])]
         offs_list = load_list(offs, "offs_list")
         scale_rows = x_scales[0].rearrange("(q r) c -> r q c", r=4)
         for r in range(4):
             nc.sync.dma_start(out=scale_table[r:P:32, :].bitcast(I32), in_=scale_rows[r].bitcast(I32))
-        load_rows("y", w1, row_pairs[1])
         word_table = tile([P, T], I32, "word_table")
         nc.sync.dma_start(out=word_table[:], in_=x_words[0].rearrange("p n j -> p (n j)").bitcast(I32))
         cen_list = load_list(cen, "cen_list")
-        for rows_of_k in row_pairs:
-            load_rows("e", w2, rows_of_k)
-        load_rows("h", w3, whole)
+        w2_halves = [load_half(w2, 0, tile([P, PACK, H // 2], F32, "w2_raw0")[:])]
+        w1_halves.append(load_half(w1, 1, placed([P, PACK, H // 2], F32, "w1_raw1", 8192)[:]))
+        w2_halves.append(load_half(w2, 1, placed([P, PACK, H // 2], F32, "w2_raw1", 12288)[:]))
         pos_lists = [load_list(pos1, "pos1_list"), load_list(pos2, "pos2_list")]
+        raw = {"h": tile([P, PACK, H], F32, "w3_raw")[:]}
+        load_rows("h", w3, whole)
         w4_raw = tile([P, PACK, N], F32, "w4_raw")[:]
         w4_rows = w4.rearrange("(m t r) n -> t m r n", t=PACK, r=4)
         for t in range(PACK):
@@ -85,6 +89,11 @@ def tile_picked_zpt_mul_p_kernel(tc, x_words, x_scales, w1, w2, w3, w4, offs, ce
         def weave(dst, src, first, stop, copy, planes=slice(0, PACK)):
             copy(out=dst.rearrange("p t (m r) j -> p m t j r", r=4)[:, :, :, planes],
                  in_=raw[src].rearrange("p j (m t r) -> p m t j r", t=PACK, r=4)[:, :, first:stop, planes])
+
+        def weave_scores(dst, src, first, copy, planes=slice(0, PACK)):
+            groups = slice(2 * first, 2 * (first + dst.shape[1]))
+            copy(out=dst.rearrange("p u (a m r) j -> p m (u a) j r", a=2, r=4)[:, :, :, planes],
+                 in_=src.rearrange("p j (m t r) -> p m t j r", t=PACK, r=4)[:, :, groups, planes])
 
         def quantise(name, first, stop, src, made=None):
             if made is None:
@@ -112,66 +121,84 @@ def tile_picked_zpt_mul_p_kernel(tc, x_words, x_scales, w1, w2, w3, w4, offs, ce
         def vector_gather(dst, window, lst):
             nc.vector.tensor_copy(out=dst, in_=window.indirect(lst))
 
-        def gather_query(t, gather, tag=None):
-            query[t] = tile([P, V], F32, "query%d" % t, tag=tag)[:]
-            gather(query[t], y_rows[t // 2][:, t % 2, :], cen_list[:])
+        def gather_query(t, gather, cols=slice(0, V)):
+            gather(query[t][:, cols], rows["y", t], cen_list[:, cols.start // LIST_ROWS : cols.stop // LIST_ROWS])
 
-        y_woven = placed([P, PACK, P, PACK], BF16, "y_woven", 2048)[:]
-        weave(y_woven[:, 0:2], "y", 0, 2, on_vector, row_pairs[0])
-        weave(y_woven[:, 2:4], "y", 2, 4, on_scalar, row_pairs[0])
+        def weave_and_quantise(name, half, src, woven):
+            for u in range(2):
+                weave_scores(woven[u], src, u, on_vector)
+            for u in range(2):
+                quantise(name, 2 * half + u, 2 * half + u + 1, woven[u])
+
+        def woven_pair(name, offsets):
+            return [placed([P, 1, P, PACK], BF16, name + "_woven%d" % u, offsets[u])[:] for u in range(2)]
+
+        y_woven = placed([P, 2, P, PACK], BF16, "y_woven", 3072)[:]
+        weave_scores(y_woven[:, 0:1], w1_halves[0], 0, on_vector)
+        weave_scores(y_woven[:, 1:2], w1_halves[0], 1, on_scalar)
         nc.vector.tensor_copy(out=x_bytes[:], in_=scale_table[:].indirect(offs_list[:]))
-        weave(y_woven[:, 0:2], "y", 0, 2, on_vector, row_pairs[1])
-        weave(y_woven[:, 2:4], "y", 2, 4, on_scalar, row_pairs[1])
-        quantise("y", 2, 4, y_woven[:, 2:4])
-        quantise("y", 0, 2, y_woven[:, 0:2])
-        x_codes = placed([P, S], U32, "x_codes", 4096)
-        point_pieces = [slice(0, P), slice(P, 2 * P), slice(2 * P, S)]
-        for cols in point_pieces:
+        quantise("y", 0, 2, y_woven)
+        x_codes = placed([P, S], U32, "x_codes", 4608)
+        point_halves = [slice(0, S // 2), slice(S // 2, S)]
+        for cols in point_halves:
             nc.vector.tensor_copy(out=x_codes[:, cols], in_=word_table[:].bitcast(U32).indirect(
                 offs_list[:, cols.start // LIST_ROWS : cols.stop // LIST_ROWS]))
-        y_rows = [tile([P, 2, S], F32, "y_rows%d" % pair) for pair in range(2)]
-        point_halves = [slice(0, S // 2), slice(S // 2, S)]
-        y_steps = [(0, 0, point_pieces[:2]), (1, 0, point_halves[:1]), (0, 1, point_halves[1:]), (1, 1, point_halves[1:])]
-        for number, (pair, half, pieces) in enumerate(y_steps):
-            made = bank([P, 2, S // 2], "y_sums", number)
-            for cols in pieces:
-                for place in range(2):
-                    product(made[:, place, cols.start - half * S // 2 : cols.stop - half * S // 2], "y", 2 * pair + place, cols)
-            nc.scalar.copy(out=y_rows[pair][:, :, point_halves[half]], in_=made[:])
-
-        e_all = placed([P, PACK, P, PACK], BF16, "e_woven", 0)
-        e_woven = [e_all[:, 0:1], e_all[:, 1:2], e_all[:, 2:4]]
-        weave(e_all[:], "e", 0, PACK, on_vector, slice(0, 2))
-        weave(e_woven[0], "e", 0, 1, on_vector, slice(2, PACK))
-        weave(e_woven[1], "e", 1, 2, on_vector, slice(2, PACK))
-        quantise("e", 0, 1, e_woven[0])
-        weave(e_woven[2], "e", 2, 4, on_vector, slice(2, PACK))
-        quantise("e", 1, 2, e_woven[1])
-        quantise("e", 2, 4, e_woven[2])
+        first_rows = tile([P, 2, S], F32, "y_rows0")
+        rows["y", 0], rows["y", 1] = first_rows[:, 0, :], first_rows[:, 1, :]
+        made = bank([P, 2, S // 2], "y_sums", 0)
+        for t in range(2):
+            product(made[:, t, :], "y", t, point_halves[0])
+        nc.scalar.copy(out=first_rows[:, :, point_halves[0]], in_=made[:])
+        for t, number in ((0, 1), (1, 7)):
+            made = bank([P, S // 2], "y_sums", number)
+            product(made[:], "y", t, point_halves[1])
+            nc.scalar.copy(out=rows["y", t][:, point_halves[1]], in_=made[:])
+        query[0] = tile([P, V], F32, "query0")[:]
         gather_query(0, scalar_gather)
-        gather_query(1, vector_gather, tag="w2_raw")
-        for t in range(PACK):
+        weave_and_quantise("e", 0, w2_halves[0], woven_pair("early_e", (2560, 3584)))
+        for t in range(2):
             multiply("e", t, PACK + t)
+            empty("e", t)
+        weave_and_quantise("y", 1, w1_halves[1], woven_pair("late_y", (2560, 3584)))
+        query[1] = placed([P, V], F32, "query1", 8192)[:]
+        gather_query(1, vector_gather)
+        for t in range(2, PACK):
+            multiply("y", t, t)
+        for t in range(2, PACK):
+            empty("y", t)
+        for t in range(2, PACK):
+            query[t] = tile([P, V], F32, "query%d" % t)[:]
+            gather_query(t, scalar_gather)
+        weave_and_quantise("e", 1, w2_halves[1], woven_pair("late_e", (1536 + 256, 2560 + 256)))
+        for t in range(2, PACK):
+            multiply("e", t, PACK + t)
+
+        prod = {(0, 0): placed([P, 2, V], F32, "prod00", 12288)}
+
+        def keys(pair, side, place):
+            t = 2 * place + pair
+            nc.vector.tensor_tensor(prod[pair, place][:, side, :], rows["e", t].indirect(pos_lists[side][:]), query[t], ALU.mult)
+
+        for side in range(2):
+            keys(0, side, 0)
         h_woven = placed([P, PACK, P, PACK], BF16, "h_woven", 0)[:]
-        for pair in range(2):
-            weave(h_woven[:, 2 * pair : 2 * pair + 2], "h", 2 * pair, 2 * pair + 2, on_vector)
-        for pair in range(2):
-            quantise("h", 2 * pair, 2 * pair + 2, h_woven[:, 2 * pair : 2 * pair + 2])
-        empty("e", 0)
-        empty("e", 1)
-        gather_query(2, scalar_gather, tag="e_codes0")
+        weave(h_woven[:, 0:1], "h", 0, 1, on_vector)
+        for t in range(1, PACK):
+            weave(h_woven[:, t : t + 1], "h", t, t + 1, on_vector)
+            quantise("h", t - 1, t, h_woven[:, t - 1 : t])
+        quantise("h", PACK - 1, PACK, h_woven[:, PACK - 1 :])
         empty("e", 2)
-        gather_query(3, scalar_gather, tag="e_codes1")
         empty("e", 3)
         for t in range(PACK):
             multiply("h", t, t)
-
-        prod = [tile([P, 2, 2, V], F32, "prod0", tag="w3_raw"), placed([P, 2, 2, V], F32, "prod1", 0)]
-        for pair in range(2):
-            for side in range(2):
-                for place in range(2):
-                    t = 2 * pair + place
-                    nc.vector.tensor_tensor(prod[pair][:, side, place, :], rows["e", t].indirect(pos_lists[side][:]), query[t], ALU.mult)
+        prod[0, 1] = tile([P, 2, V], F32, "prod01", tag="w3_raw")
+        for side in range(2):
+            keys(0, side, 1)
+        for place in range(2):
+            prod[1, place] = placed([P, 2, V], F32, "prod1%d" % place, 2048 * place)
+        for side in range(2):
+            for place in range(2):
+                keys(1, side, place)
 
         tanhs = [tile([P, 2, 2, 2, P], F32, "tanhs%d" % pair) for pair in range(2)]
         gates = [tile([P, 2, V], F32, "gates%d" % pair) for pair in range(2)]
@@ -183,12 +210,12 @@ def tile_picked_zpt_mul_p_kernel(tc, x_words, x_scales, w1, w2, w3, w4, offs, ce
             made = bank([P, len(places), V], "turned", number)
             for n, place in enumerate(places):
                 for cols in halves:
-                    nc.tensor.transpose(made[:, n, cols], prod[pair][:, side, place, cols], identity[:])
+                    nc.tensor.transpose(made[:, n, cols], prod[pair, place][:, side, cols], identity[:])
             return made
 
         def squash(pair, side, places, src):
-            nc.scalar.activation(tanhs[pair][:, side, :, places[0] : places[-1] + 1, :].rearrange("p c t x -> p t c x"),
-                                 src[:].rearrange("p t (c x) -> p t c x", x=P), ACT.Tanh, scale=signs[side])
+            nc.scalar.activation(tanhs[pair][:, side].rearrange("p c a (h x) -> p h (c a) x", h=2),
+                                 src[:].rearrange("p h (g x) -> p h g x", x=P // 2), ACT.Tanh, scale=signs[side])
 
         def turn_back(dst, pair, side, which):
             for half in which:
@@ -208,40 +235,37 @@ def tile_picked_zpt_mul_p_kernel(tc, x_words, x_scales, w1, w2, w3, w4, offs, ce
             nc.vector.tensor_tensor(weighted[:, tiles, cols], spreads[:, tiles, cols], gates[pair][:, :, cols], ALU.mult)
 
         both = (0, 1)
+        turned = {(0, side): turn(0, side, both, PACK + side) for side in range(2)}
         empty("h", 0)
         empty("h", 1)
-        turned_00 = turn(0, 0, both, 4)
-        turned_01 = turn(0, 1, both, 5)
         second_values(0, scalar_gather)
-        squash(0, 0, both, turned_00)
-        diffs = bank([P, 2, V], "diffs", 0)
-        turn_back(diffs, 0, 0, both)
-        second_values(1, scalar_gather)
-        squash(0, 1, both, turned_01)
-        turned_10 = turn(1, 0, both, 6)
-        turned_2 = turn(1, 1, (0,), 4)
-        turn_back(diffs, 0, 1, both)
-        turned_3 = turn(1, 1, (1,), 7)
         empty("h", 2)
-        squash(1, 0, both, turned_10)
+        diffs = bank([P, 2, V], "diffs", 0)
+        half_diffs = [bank([P, 2, P], "half_diffs", number) for number in (1, 2)]
+        squash(0, 0, both, turned[0, 0])
+        turn_back(diffs, 0, 0, both)
+        turned[1, 0] = turn(1, 0, both, PACK)
+        second_values(1, scalar_gather)
+        empty("h", 3)
+        turned[1, 1] = turn(1, 1, both, 3)
+        squash(0, 1, both, turned[0, 1])
+        turn_back(diffs, 0, 1, both)
         second_values(2, scalar_gather, halves[1])
-        half_diffs = [bank([P, 2, P], "half_diffs", number) for number in (1, 6)]
+        squash(1, 0, both, turned[1, 0])
         for half in range(2):
             turn_back(half_diffs[half], 1, 0, (half,))
-        spread(0)
-        second_values(2, vector_gather, halves[0])
-        spread(1)
-        empty("h", 3)
-        squash(1, 1, (0,), turned_2)
-        squash(1, 1, (1,), turned_3)
-        for half in range(2):
-            turn_back(half_diffs[half], 1, 1, (half,))
-        spread(2)
         second_values(3, scalar_gather)
+        for half, cols in enumerate(halves):
+            nc.scalar.activation(tanhs[1][:, 1, half].rearrange("p a (h x) -> p h a x", h=2),
+                                 turned[1, 1][:, :, cols].rearrange("p h (a x) -> p h a x", a=2), ACT.Tanh, scale=signs[1])
+            turn_back(half_diffs[half], 1, 1, (half,))
         nc.scalar.activation(gates[0][:], diffs[:], ACT.Sigmoid)
         for half, cols in enumerate(halves):
             nc.scalar.activation(gates[1][:, :, cols], half_diffs[half][:], ACT.Sigmoid)
-        spread(3)
+        spread(0)
+        second_values(2, vector_gather, halves[0])
+        for t in range(1, PACK):
+            spread(t)
         weigh(0, slice(0, V))
         for cols in halves:
             weigh(1, cols)

from contextlib import ExitStack

import concourse.mybir as mybir
from concourse.masks import make_identity

K, T, S, V, H, N = 512, 2048, 512, 256, 512, 256
P = 128
PACK = 4
LIST_ROWS = 16
ALIGN = 256
FLOPS = 2 * K * S * H * 3 + 2 * H * N * V

F32 = mybir.dt.float32
BF16 = mybir.dt.bfloat16
I32 = mybir.dt.int32
U32 = mybir.dt.uint32
U16 = mybir.dt.uint16
U8 = mybir.dt.uint8
FP8X4 = mybir.dt.float8_e4m3fn_x4
ALU = mybir.AluOpType
ACT = mybir.ActivationFunctionType


def tile_picked_zpt_mul_p_kernel(tc, x_words, x_scales, w1, w2, w3, w4, offs, cen, pos1, pos2, out):
    nc = tc.nc
    with ExitStack() as ctx:
        sb = ctx.enter_context(tc.tile_pool(name="sb", bufs=1))
        laid = ctx.enter_context(tc.tile_pool(name="laid", bufs=1))
        ps = ctx.enter_context(tc.psum_pool(name="ps", bufs=1))

        def tile(shape, dtype, name, tag=None):
            return sb.tile(shape, dtype, name=name, tag=tag or name, align_bytes=ALIGN)

        def placed(shape, dtype, name, offset):
            return laid.tile(shape, dtype, name=name, offset=offset, align_bytes=ALIGN)

        def bank(shape, name, number):
            return ps.tile(shape, F32, name=name, tag="bank%d" % number)

        def load_list(src, name):
            lst = sb.tile(list(src.shape), U16, name=name)
            nc.sync.dma_start(lst[:], src)
            return lst

        def load_rows(name, w, rows_of_k):
            nc.sync.dma_start(out=raw[name][:, rows_of_k, :], in_=w.rearrange("(p j) c -> p j c", j=PACK)[:, rows_of_k, :])

        halves = [slice(0, P), slice(P, 2 * P)]
        whole, row_pairs = slice(0, PACK), [slice(0, 2), slice(2, PACK)]

        scale_table = tile([P, T], U8, "scale_table")
        nc.vector.memset(scale_table[:, : T // 2].bitcast(I32), 0)
        nc.gpsimd.memset(scale_table[:, T // 2 :].bitcast(I32), 0)
        warm = tile([P, 2], F32, "warm")
        nc.vector.memset(warm[:, 0:1], 0.0)
        nc.scalar.activation(warm[:, 1:2], warm[:, 0:1], ACT.Sigmoid)

        def load_half(w, half, dst):
            nc.sync.dma_start(out=dst, in_=w.rearrange("(p j) c -> p j c", j=PACK)[:, :, half * H // 2 : (half + 1) * H // 2])
            return dst

        w1_halves = [load_half(w1, 0, tile([P, PACK, H // 2], F32, "w1_raw0")[:])]
        offs_list = load_list(offs, "offs_list")
        scale_rows = x_scales[0].rearrange("(q r) c -> r q c", r=4)
        for r in range(4):
            nc.sync.dma_start(out=scale_table[r:P:32, :].bitcast(I32), in_=scale_rows[r].bitcast(I32))
        word_table = tile([P, T], I32, "word_table")
        nc.sync.dma_start(out=word_table[:], in_=x_words[0].rearrange("p n j -> p (n j)").bitcast(I32))
        cen_list = load_list(cen, "cen_list")
        w2_halves = [load_half(w2, 0, tile([P, PACK, H // 2], F32, "w2_raw0")[:])]
        w1_halves.append(load_half(w1, 1, placed([P, PACK, H // 2], F32, "w1_raw1", 8192)[:]))
        w2_halves.append(load_half(w2, 1, placed([P, PACK, H // 2], F32, "w2_raw1", 12288)[:]))
        pos_lists = [load_list(pos1, "pos1_list"), load_list(pos2, "pos2_list")]
        raw = {"h": tile([P, PACK, H], F32, "w3_raw")[:]}
        load_rows("h", w3, whole)
        w4_raw = tile([P, PACK, N], F32, "w4_raw")[:]
        w4_rows = w4.rearrange("(m t r) n -> t m r n", t=PACK, r=4)
        for t in range(PACK):
            nc.sync.dma_start(out=w4_raw[:, t, :], in_=w4_rows[t])

        identity = tile([P, P], F32, "identity")
        make_identity(nc, identity[:])
        x_bytes = tile([P, S], U8, "x_bytes")
        w_scales = {name: tile([P, H], U8, name + "_scales") for name in "yeh"}
        codes, rows, sums, query = {}, {}, {}, {}
        signs = [1.0, -1.0]
        on_vector, on_scalar = nc.vector.tensor_copy, nc.scalar.copy

        def weave(dst, src, first, stop, copy, planes=slice(0, PACK)):
            copy(out=dst.rearrange("p t (m r) j -> p m t j r", r=4)[:, :, :, planes],
                 in_=raw[src].rearrange("p j (m t r) -> p m t j r", t=PACK, r=4)[:, :, first:stop, planes])

        def weave_scores(dst, src, first, copy, planes=slice(0, PACK)):
            groups = slice(2 * first, 2 * (first + dst.shape[1]))
            copy(out=dst.rearrange("p u (a m r) j -> p m (u a) j r", a=2, r=4)[:, :, :, planes],
                 in_=src.rearrange("p j (m t r) -> p m t j r", t=PACK, r=4)[:, :, groups, planes])

        def quantise(name, first, stop, src, made=None):
            if made is None:
                made = tile([P, P * (stop - first)], U32, name + "_codes%d" % first)
            nc.vector.quantize_mx(out=made[:].bitcast(FP8X4), scales=w_scales[name][:, P * first : P * stop],
                                  in_=src.rearrange("p t m j -> p (t m j)"))
            for t in range(first, stop):
                codes[name, t] = made[:, P * (t - first) : P * (t - first + 1)]

        def product(dst, name, t, cols):
            nc.tensor.matmul_mx(out=dst, lhsT=codes[name, t].bitcast(FP8X4), lhsT_scale=w_scales[name][:, P * t : P * t + P],
                                rhs=x_codes[:, cols].bitcast(FP8X4), rhs_scale=x_bytes[:, cols], start=True, stop=True)

        def multiply(name, t, number):
            sums[name, t] = bank([P, S], "sums", number)
            product(sums[name, t][:], name, t, slice(0, S))

        def empty(name, t):
            rows[name, t] = tile([P, S], F32, name + "_rows%d" % t)[:]
            nc.scalar.copy(out=rows[name, t], in_=sums[name, t][:])

        def scalar_gather(dst, window, lst):
            nc.scalar.activation(dst, window.indirect(lst), ACT.Copy)

        def vector_gather(dst, window, lst):
            nc.vector.tensor_copy(out=dst, in_=window.indirect(lst))

        def gather_query(t, gather, cols=slice(0, V)):
            gather(query[t][:, cols], rows["y", t], cen_list[:, cols.start // LIST_ROWS : cols.stop // LIST_ROWS])

        def weave_and_quantise(name, half, src, woven):
            for u in range(2):
                weave_scores(woven[u], src, u, on_vector)
            for u in range(2):
                quantise(name, 2 * half + u, 2 * half + u + 1, woven[u])

        def woven_pair(name, offsets):
            return [placed([P, 1, P, PACK], BF16, name + "_woven%d" % u, offsets[u])[:] for u in range(2)]

        y_woven = placed([P, 2, P, PACK], BF16, "y_woven", 3072)[:]
        weave_scores(y_woven[:, 0:1], w1_halves[0], 0, on_vector)
        weave_scores(y_woven[:, 1:2], w1_halves[0], 1, on_scalar)
        nc.vector.tensor_copy(out=x_bytes[:], in_=scale_table[:].indirect(offs_list[:]))
        quantise("y", 0, 2, y_woven)
        x_codes = placed([P, S], U32, "x_codes", 4608)
        point_halves = [slice(0, S // 2), slice(S // 2, S)]
        for cols in point_halves:
            nc.vector.tensor_copy(out=x_codes[:, cols], in_=word_table[:].bitcast(U32).indirect(
                offs_list[:, cols.start // LIST_ROWS : cols.stop // LIST_ROWS]))
        first_rows = tile([P, 2, S], F32, "y_rows0")
        rows["y", 0], rows["y", 1] = first_rows[:, 0, :], first_rows[:, 1, :]
        made = bank([P, 2, S // 2], "y_sums", 0)
        for t in range(2):
            product(made[:, t, :], "y", t, point_halves[0])
        nc.scalar.copy(out=first_rows[:, :, point_halves[0]], in_=made[:])
        for t, number in ((0, 1), (1, 7)):
            made = bank([P, S // 2], "y_sums", number)
            product(made[:], "y", t, point_halves[1])
            nc.scalar.copy(out=rows["y", t][:, point_halves[1]], in_=made[:])
        query[0] = tile([P, V], F32, "query0")[:]
        gather_query(0, scalar_gather)
        weave_and_quantise("e", 0, w2_halves[0], woven_pair("early_e", (2560, 3584)))
        for t in range(2):
            multiply("e", t, PACK + t)
            empty("e", t)
        weave_and_quantise("y", 1, w1_halves[1], woven_pair("late_y", (2560, 3584)))
        query[1] = placed([P, V], F32, "query1", 8192)[:]
        gather_query(1, vector_gather)
        for t in range(2, PACK):
            multiply("y", t, t)
        for t in range(2, PACK):
            empty("y", t)
        for t in range(2, PACK):
            query[t] = tile([P, V], F32, "query%d" % t)[:]
            gather_query(t, scalar_gather)
        weave_and_quantise("e", 1, w2_halves[1], woven_pair("late_e", (1536 + 256, 2560 + 256)))
        for t in range(2, PACK):
            multiply("e", t, PACK + t)

        prod = {(0, 0): placed([P, 2, V], F32, "prod00", 12288)}

        def keys(pair, side, place):
            t = 2 * place + pair
            nc.vector.tensor_tensor(prod[pair, place][:, side, :], rows["e", t].indirect(pos_lists[side][:]), query[t], ALU.mult)

        for side in range(2):
            keys(0, side, 0)
        h_woven = placed([P, PACK, P, PACK], BF16, "h_woven", 0)[:]
        weave(h_woven[:, 0:1], "h", 0, 1, on_vector)
        for t in range(1, PACK):
            weave(h_woven[:, t : t + 1], "h", t, t + 1, on_vector)
            quantise("h", t - 1, t, h_woven[:, t - 1 : t])
        quantise("h", PACK - 1, PACK, h_woven[:, PACK - 1 :])
        empty("e", 2)
        empty("e", 3)
        for t in range(PACK):
            multiply("h", t, t)
        prod[0, 1] = tile([P, 2, V], F32, "prod01", tag="w3_raw")
        for side in range(2):
            keys(0, side, 1)
        for place in range(2):
            prod[1, place] = placed([P, 2, V], F32, "prod1%d" % place, 2048 * place)
        for side in range(2):
            for place in range(2):
                keys(1, side, place)

        tanhs = [tile([P, 2, 2, 2, P], F32, "tanhs%d" % pair) for pair in range(2)]
        gates = [tile([P, 2, V], F32, "gates%d" % pair) for pair in range(2)]
        spreads = tile([P, PACK, V], F32, "spreads")
        weighted = tile([P, PACK, V], F32, "weighted")
        seconds = tile([P, PACK, V], F32, "seconds")

        def turn(pair, side, places, number):
            made = bank([P, len(places), V], "turned", number)
            for n, place in enumerate(places):
                for cols in halves:
                    nc.tensor.transpose(made[:, n, cols], prod[pair, place][:, side, cols], identity[:])
            return made

        def squash(pair, side, places, src):
            nc.scalar.activation(tanhs[pair][:, side].rearrange("p c a (h x) -> p h (c a) x", h=2),
                                 src[:].rearrange("p h (g x) -> p h g x", x=P // 2), ACT.Tanh, scale=signs[side])

        def turn_back(dst, pair, side, which):
            for half in which:
                for place in range(2):
                    nc.tensor.matmul(dst[:, place, slice(0, P) if len(which) == 1 else halves[half]],
                                     lhsT=tanhs[pair][:, side, half, place], rhs=identity[:], is_transpose=True,
                                     start=(side, half, place) == (0, which[0], 0), stop=(side, half, place) == (1, which[-1], 1))

        def second_values(t, gather, cols=slice(0, V)):
            gather(seconds[:, t, cols], rows["h", t], pos_lists[1][:, cols.start // LIST_ROWS : cols.stop // LIST_ROWS])

        def spread(t):
            nc.vector.tensor_tensor(spreads[:, t, :], rows["h", t].indirect(pos_lists[0][:]), seconds[:, t, :], ALU.subtract)

        def weigh(pair, cols):
            tiles = slice(2 * pair, 2 * pair + 2)
            nc.vector.tensor_tensor(weighted[:, tiles, cols], spreads[:, tiles, cols], gates[pair][:, :, cols], ALU.mult)

        both = (0, 1)
        turned = {(0, side): turn(0, side, both, PACK + side) for side in range(2)}
        empty("h", 0)
        empty("h", 1)
        second_values(0, scalar_gather)
        empty("h", 2)
        diffs = bank([P, 2, V], "diffs", 0)
        half_diffs = [bank([P, 2, P], "half_diffs", number) for number in (1, 2)]
        squash(0, 0, both, turned[0, 0])
        turn_back(diffs, 0, 0, both)
        turned[1, 0] = turn(1, 0, both, PACK)
        second_values(1, scalar_gather)
        empty("h", 3)
        turned[1, 1] = turn(1, 1, both, 3)
        squash(0, 1, both, turned[0, 1])
        turn_back(diffs, 0, 1, both)
        second_values(2, scalar_gather, halves[1])
        squash(1, 0, both, turned[1, 0])
        for half in range(2):
            turn_back(half_diffs[half], 1, 0, (half,))
        second_values(3, scalar_gather)
        for half, cols in enumerate(halves):
            nc.scalar.activation(tanhs[1][:, 1, half].rearrange("p a (h x) -> p h a x", h=2),
                                 turned[1, 1][:, :, cols].rearrange("p h (a x) -> p h a x", a=2), ACT.Tanh, scale=signs[1])
            turn_back(half_diffs[half], 1, 1, (half,))
        nc.scalar.activation(gates[0][:], diffs[:], ACT.Sigmoid)
        for half, cols in enumerate(halves):
            nc.scalar.activation(gates[1][:, :, cols], half_diffs[half][:], ACT.Sigmoid)
        spread(0)
        second_values(2, vector_gather, halves[0])
        for t in range(1, PACK):
            spread(t)
        weigh(0, slice(0, V))
        for cols in halves:
            weigh(1, cols)

        w4_woven = tile([P, N, PACK], BF16, "w4_woven", tag="tanhs1")
        w4_codes = tile([P, N], U32, "w4_codes", tag="gates1")
        w4_scales = tile([P, N], U8, "w4_scales")
        z_codes = tile([P, V], U32, "z_codes")
        z_scales = tile([P, V], U8, "z_scales")
        nc.scalar.copy(out=w4_woven[:].rearrange("p (c i) t -> p c t i", i=4), in_=w4_raw.rearrange("p t (c i) -> p c t i", i=4))
        z_woven = tile([P, V, PACK], BF16, "z_woven")
        for cols in halves:
            nc.vector.tensor_tensor(z_woven[:, cols, :].rearrange("p (c i) t -> p c t i", i=4),
                                    weighted[:, :, cols].rearrange("p t (c i) -> p c t i", i=4),
                                    seconds[:, :, cols].rearrange("p t (c i) -> p c t i", i=4), ALU.add)

        def quantise_z(cols):
            nc.vector.quantize_mx(out=z_codes[:, cols].bitcast(FP8X4), scales=z_scales[:, cols],
                                  in_=z_woven[:, cols, :].rearrange("p v t -> p (v t)"))

        quantise_z(halves[0])
        nc.vector.quantize_mx(out=w4_codes[:].bitcast(FP8X4), scales=w4_scales[:], in_=w4_woven[:].rearrange("p m t -> p (m t)"))
        quantise_z(halves[1])
        for half, cols in enumerate(halves):
            for block, out_rows in enumerate(halves):
                result = bank([P, P], "result", PACK + 2 * half + block)
                nc.tensor.matmul_mx(out=result[:], lhsT=w4_codes[:, out_rows].bitcast(FP8X4), lhsT_scale=w4_scales[:, out_rows],
                                    rhs=z_codes[:, cols].bitcast(FP8X4), rhs_scale=z_scales[:, cols], start=True, stop=True)
                staged = tile([P, P], F32, "staged%d%d" % (half, block))
                if block == 1:
                    nc.vector.tensor_copy(out=staged[:], in_=result[:])
                else:
                    nc.scalar.copy(out=staged[:], in_=result[:])
                queue = nc.scalar if (half, block) == (1, 0) else nc.sync
                queue.dma_start(out=out[out_rows, cols], in_=staged[:])
